import numpy as np
import ml_dtypes


def mxq(x, axis, fmt="e4m3"):
    dtype, down = {"e4m3": (ml_dtypes.float8_e4m3fn, 7), "e5m2": (ml_dtypes.float8_e5m2, 14)}[fmt]
    v = np.moveaxis(np.asarray(x, np.float32).astype(ml_dtypes.bfloat16).astype(np.float64), axis, -1)
    blocks = v.reshape(v.shape[:-1] + (-1, 32))
    amax = np.abs(blocks).max(-1, keepdims=True)
    byte = np.maximum(np.where(amax > 0, np.frexp(amax)[1] - 1 + 127, 0) - down, 1)
    scale = np.exp2(byte - 127.0)
    codes = (blocks / scale).astype(np.float32).astype(dtype).astype(np.float64)
    return np.moveaxis((codes * scale).reshape(v.shape), -1, axis)


WIDE = False


def mx_kscale(k):
    if not WIDE:
        return np.ones(k)
    levels = np.array([10, -10, 5, -5, 0])
    if k % 512:
        return np.exp2(np.random.permutation(np.resize(levels, k // 32))).repeat(32)
    a = np.empty((k // 512, 16))
    for p in range(k // 512):
        a[p, :8] = np.random.permutation(np.resize(levels, 8))
        for g in range(8):
            far = levels[np.abs(levels - a[p, g]) >= 10]
            a[p, g + 8] = far[np.random.randint(len(far))]
    return np.exp2(a.ravel()).repeat(32)


def f64(x):
    return np.asarray(x).astype(np.float64)


def striped(idx):
    return np.tile(idx.reshape(-1, 16).T, (8, 1)).astype(np.uint16)


def unstriped(offs):
    return offs[:16].T.reshape(-1).astype(np.int64)


E2M1 = np.array([0.0, 0.5, 1.0, 1.5, 2.0, 3.0, 4.0, 6.0, -0.0, -0.5, -1.0, -1.5, -2.0, -3.0, -4.0, -6.0])


def pack_weight(w, fmt):
    k, n = w.shape
    w = f64(np.asarray(w, np.float32).astype(ml_dtypes.bfloat16)).reshape(k // 32, 32, n)
    amax = np.abs(w).max(1)
    if fmt == "e4m3":
        byte = np.frexp(amax)[1] - 1 + 127 - 7
    else:
        mant, ex = np.frexp(amax / 6.0)
        byte = np.where(mant > 0.5, ex, ex - 1) + 127
    byte = np.clip(np.where(amax > 0, byte, 1), 1, 254)
    scaled = (w * np.exp2(127.0 - byte)[:, None, :]).reshape(k, n).astype(np.float32)
    by_word = np.ascontiguousarray(scaled.reshape(k // 512, 128, 4, n).transpose(0, 1, 3, 2))
    if fmt == "e4m3":
        words = by_word.astype(ml_dtypes.float8_e4m3fn).view(np.uint8)
    else:
        c = by_word.astype(ml_dtypes.float4_e2m1fn).view(np.uint8) & 0xF
        words = (c[..., 0::2] | (c[..., 1::2] << 4)).reshape(k // 512, 128, 2 * n)
    return np.ascontiguousarray(words), np.ascontiguousarray(byte.astype(np.uint8).reshape(k // 512, 16, n))


def unpack_weight(words, scales, fmt):
    g, _, n = scales.shape
    words = np.ascontiguousarray(words).reshape(g, 128, n, -1)
    if fmt == "e4m3":
        vals = words.view(ml_dtypes.float8_e4m3fn).astype(np.float64)
    else:
        nib = np.empty((g, 128, n, 4), np.uint8)
        nib[..., 0::2] = words & 0xF
        nib[..., 1::2] = words >> 4
        vals = E2M1[nib]
    vals = vals * np.repeat(np.exp2(scales.astype(np.float64) - 127.0), 8, axis=1)[..., None]
    return vals.transpose(0, 1, 3, 2).reshape(g * 512, n)


K, T, E, C, N, TOP = 1024, 512, 12, 128, 256, 3


def by_expert(wq, xq):
    return np.concatenate([wq[e].T @ xq[:, e * C:(e + 1) * C] for e in range(E)], axis=1)


def setup_inputs():
    n = np.random.standard_normal
    s = mx_kscale(K)
    deal = np.repeat(np.arange(E), C).reshape(TOP, T)[:, np.random.permutation(T)]
    deal = np.take_along_axis(deal, np.argsort(np.random.rand(TOP, T), axis=0), axis=0)
    for _ in range(8):
        s_, t_ = np.random.permutation(T).reshape(2, -1); r = np.random.randint(TOP, size=T // 2); x, y = deal[r, s_].copy(), deal[r, t_].copy()
        ok = ~((deal[:, s_] == y).any(0) | (deal[:, t_] == x).any(0)); deal[r[ok], s_[ok]] = y[ok]; deal[r[ok], t_[ok]] = x[ok]
    order = np.argsort(deal.reshape(-1) + 0.5 * np.random.rand(TOP * T))
    slot_token = order % T; pos = np.empty(TOP * T, np.int64); pos[order] = np.arange(TOP * T); pos = pos.reshape(TOP, T)
    g = np.random.uniform(0.5, 1.5, (TOP, T)); g = g / g.sum(0)
    x = pack_weight(n((K, T)) * s[:, None], "e4m3")
    wq = [pack_weight(m, "e2m1") for m in n((E, K, N)) / np.sqrt(K) / s[None, :, None]]
    wk = [pack_weight(m, "e4m3") for m in n((E, K, N)) / np.sqrt(K) / s[None, :, None]]
    return {
        "x_words": x[0],
        "x_scales": x[1],
        "wq_words": np.stack([m[0] for m in wq]),
        "wq_scales": np.stack([m[1] for m in wq]),
        "wk_words": np.stack([m[0] for m in wk]),
        "wk_scales": np.stack([m[1] for m in wk]),
        "wv": (n((E, K, N)) / np.sqrt(K) / s[None, :, None]).astype(np.float32),
        "bias": (0.3 * n((3 * N, E))).astype(np.float32),
        "gate": np.stack([np.tile(r, (128, 1)) for r in g]).astype(np.float32),
        "offs": striped(slot_token),
        "pos1": striped(pos[0]),
        "pos2": striped(pos[1]),
        "pos3": striped(pos[2]),
    }


def reference(x_words, x_scales, wq_words, wq_scales, wk_words, wk_scales, wv, bias, gate, offs, pos1, pos2, pos3):
    wq = np.stack([unpack_weight(wq_words[e], wq_scales[e], "e2m1") for e in range(E)])
    wk = np.stack([unpack_weight(wk_words[e], wk_scales[e], "e4m3") for e in range(E)])
    wvq = mxq(f64(wv), 1, "e4m3")
    idx = unstriped(offs)
    xq = unpack_weight(x_words, x_scales, "e4m3")[:, idx]
    y = np.concatenate([by_expert(w, xq) for w in (wq, wk, wvq)])
    y = y + np.repeat(f64(bias), C, axis=1)
    out = sum(f64(gate[r, :1]) * y[:, unstriped(p)] for r, p in enumerate((pos1, pos2, pos3)))
    return out

@@ -1,0 +1,195 @@
+from contextlib import ExitStack
+
+import concourse.mybir as mybir
+
+K, T, E, C, N, TOP = 1024, 512, 12, 128, 256, 3
+S = E * C
+FLOPS = 2 * K * 3 * N * S
+
+F32 = mybir.dt.float32
+BF16 = mybir.dt.bfloat16
+I32 = mybir.dt.int32
+U32 = mybir.dt.uint32
+U16 = mybir.dt.uint16
+U8 = mybir.dt.uint8
+FP8X4 = mybir.dt.float8_e4m3fn_x4
+FP4X4 = mybir.dt.float4_e2m1fn_x4
+MULT = mybir.AluOpType.mult
+ADD = mybir.AluOpType.add
+IDENT = mybir.ActivationFunctionType.Identity
+
+P = 128
+PASSES = 2
+CHUNK = 3
+WHOLE = 8
+
+
+def tile_moe_qkv_kernel(tc, x_words, x_scales, wq_words, wq_scales, wk_words, wk_scales, wv, bias, gate, offs, pos1, pos2, pos3, out):
+    nc = tc.nc
+    with ExitStack() as ctx:
+        keep = ctx.enter_context(tc.tile_pool(name="keep", bufs=1))
+        ring = ctx.enter_context(tc.tile_pool(name="ring", bufs=1))
+        psum = ctx.enter_context(tc.psum_pool(name="psum", bufs=1))
+
+        offs_sb = keep.tile([P, S // 16], U16, name="offs_sb")
+        pos_sb = [keep.tile([P, T // 16], U16, name=f"pos_sb{r}") for r in range(TOP)]
+        xw = [keep.tile([P, T], I32, name=f"xw{s}", align_bytes=64) for s in range(PASSES)]
+        xs = keep.tile([P, PASSES, T], U8, name="xs", align_bytes=64)
+        qs = keep.tile([P, E * PASSES, N], U8, name="qs", align_bytes=64)
+        ks = keep.tile([P, E * PASSES, N], U8, name="ks", align_bytes=64)
+        qw = [keep.tile([P, 3 * PASSES, 2 * N], U8, name=f"qw{i}", align_bytes=64) for i in range(4)]
+        kw = [keep.tile([P, 3 * PASSES, N], I32, name=f"kw{i}", align_bytes=64) for i in range(4)]
+        bias_sb = keep.tile([P, 6, 16], F32, name="bias_sb")
+        gate_sb = [keep.tile([P, T], F32, name=f"gate_sb{r}") for r in range(TOP)]
+        gw = [[keep.tile([P, CHUNK * C], U32, name=f"gw{s}_{c}", align_bytes=64) for c in range(E // CHUNK)] for s in range(PASSES)]
+        gs = [[keep.tile([P, CHUNK * C], U8, name=f"gs{s}_{c}", align_bytes=64) for c in range(E // CHUNK)] for s in range(PASSES)]
+        raw = {}
+
+        nc.vector.memset(xs[:].rearrange("p s t -> p (s t)").bitcast(I32), 0)
+        nc.vector.memset(qs[:].rearrange("p s t -> p (s t)").bitcast(I32), 0)
+        nc.gpsimd.memset(ks[:].rearrange("p s t -> p (s t)").bitcast(I32), 0)
+
+        def load_scales(dst, src):
+            for r in range(4):
+                nc.sync.dma_start(out=dst[r:P:32].bitcast(I32), in_=src[r].bitcast(I32))
+
+        def load_v(e):
+            raw[e] = ring.tile([P, PASSES, 4 * N], F32, name="raw", bufs=5)
+            nc.sync.dma_start(out=raw[e][:], in_=wv[e].rearrange("(s p j) n -> p s (j n)", s=PASSES, j=4))
+
+        def load_v_half(e, b):
+            for s in range(PASSES):
+                raw[e, b, s] = keep.tile([P, 4, P], F32, name=f"raw{e}_{b}_{s}")
+                nc.sync.dma_start(out=raw[e, b, s][:], in_=wv[e, 512 * s : 512 * (s + 1), b * P : (b + 1) * P].rearrange("(p j) n -> p j n", j=4))
+
+        def load_q(i):
+            nc.sync.dma_start(out=qw[i][:].bitcast(I32), in_=wq_words[3 * i : 3 * i + 3].rearrange("e s p w -> p (e s) w").bitcast(I32))
+
+        def load_k(i):
+            nc.sync.dma_start(out=kw[i][:], in_=wk_words[3 * i : 3 * i + 3].rearrange("e s p n d -> p (e s) (n d)").bitcast(I32))
+
+        nc.sync.dma_start(offs_sb[:], offs)
+        for s in range(PASSES):
+            nc.sync.dma_start(out=xw[s][:], in_=x_words[s].rearrange("p t d -> p (t d)").bitcast(I32))
+        load_scales(xs, x_scales.rearrange("s (q r) t -> r q s t", r=4))
+        load_v(0)
+        load_scales(qs, wq_scales.rearrange("e s (q r) n -> r q (e s) n", r=4))
+        load_q(0)
+        nc.sync.dma_start(out=bias_sb[:, :, 0:E], in_=bias.rearrange("(b p) e -> p b e", p=P))
+        load_v(1)
+        load_q(1)
+        load_v(2)
+        load_q(2)
+        for r, pos in enumerate((pos1, pos2, pos3)):
+            nc.sync.dma_start(pos_sb[r][:], pos)
+        for r in range(TOP):
+            nc.sync.dma_start(out=gate_sb[r][:], in_=gate[r])
+        load_v(3)
+        load_q(3)
+        load_scales(ks, wk_scales.rearrange("e s (q r) n -> r q (e s) n", r=4))
+        load_v(4)
+        load_k(0)
+        load_k(1)
+        load_v(5)
+        load_k(2)
+        load_k(3)
+        load_v(6)
+        load_v(7)
+        for b in range(2):
+            for e in range(WHOLE, E):
+                load_v_half(e, b)
+
+        y = {}
+
+        def slots_tile(blk):
+            y[blk] = ring.tile([P, S], F32, name="y", tag=f"y{blk % 4}")
+
+        def gather_tokens(c):
+            cols = offs_sb[:, c * CHUNK * C // 16 : (c + 1) * CHUNK * C // 16]
+            for s in range(PASSES):
+                nc.vector.tensor_copy(gw[s][c][:], xw[s][:].bitcast(U32).indirect(cols))
+                nc.vector.tensor_copy(gs[s][c][:], xs[:, s, :].indirect(cols))
+
+        def project(e, blks, lhs):
+            acc = psum.tile([P, 2, C], F32, name="acc", bufs=6)
+            c, u = divmod(e, CHUNK)
+            for i, blk in enumerate(blks):
+                for s in range(PASSES):
+                    words, scales = lhs(s, blk % 2)
+                    nc.tensor.matmul_mx(
+                        out=acc[:, i, :],
+                        lhsT=words,
+                        lhsT_scale=scales,
+                        rhs=gw[s][c][:, u * C : (u + 1) * C].bitcast(FP8X4),
+                        rhs_scale=gs[s][c][:, u * C : (u + 1) * C],
+                        start=(s == 0),
+                        stop=(s == PASSES - 1),
+                    )
+            for i, blk in enumerate(blks):
+                nc.scalar.activation(out=y[blk][:, e * C : (e + 1) * C], in_=acc[:, i, :], func=IDENT, bias=bias_sb[:, blk, e : e + 1])
+
+        def project_q(e):
+            project(e, (0, 1), lambda s, b: (qw[e // 3][:, (e % 3) * PASSES + s, b * 2 * P : (b + 1) * 2 * P].bitcast(FP4X4), qs[:, e * PASSES + s, b * P : (b + 1) * P]))
+
+        def project_k(e):
+            project(e, (2, 3), lambda s, b: (kw[e // 3][:, (e % 3) * PASSES + s, b * P : (b + 1) * P].bitcast(FP8X4), ks[:, e * PASSES + s, b * P : (b + 1) * P]))
+
+        def interleave(dst, src):
+            nc.scalar.copy(out=dst.rearrange("p (c i j) -> p c j i", i=4, j=4), in_=src.rearrange("p (j c i) -> p c j i", i=4, j=4))
+
+        vq = {}
+
+        def quantise(key, src, width):
+            staged = ring.tile([P, PASSES, 4 * width], BF16, name="staged", bufs=4, align_bytes=64)
+            for s in range(PASSES):
+                interleave(staged[:, s, :], src(s))
+            codes = keep.tile([P, PASSES * width], U32, name=f"codes{key}", align_bytes=64)
+            scales = keep.tile([P, PASSES * width], U8, name=f"scales{key}", align_bytes=64)
+            nc.vector.quantize_mx(out=codes[:].bitcast(FP8X4), scales=scales[:], in_=staged[:].rearrange("p s w -> p (s w)"))
+            vq[key] = (codes, scales)
+
+        def project_v(e):
+            codes, scales = vq[e]
+            project(e, (4, 5), lambda s, b: (codes[:, s * N + b * P : s * N + (b + 1) * P].bitcast(FP8X4), scales[:, s * N + b * P : s * N + (b + 1) * P]))
+
+        def project_v_half(e, half):
+            codes, scales = vq[e + 100 * (half + 1)]
+            project(e, (4 + half,), lambda s, b: (codes[:, s * P : (s + 1) * P].bitcast(FP8X4), scales[:, s * P : (s + 1) * P]))
+
+        def combine(blk):
+            parts = []
+            for r in range(TOP):
+                part = ring.tile([P, T], F32, name="part", tag=f"part{r}", bufs=2)
+                nc.vector.tensor_tensor(part[:], y[blk][:].indirect(pos_sb[r][:]), gate_sb[r][:], MULT)
+                parts.append(part)
+            nc.vector.tensor_tensor(parts[0][:], parts[0][:], parts[1][:], ADD)
+            res = ring.tile([P, T], F32, name="res", bufs=2)
+            nc.vector.tensor_tensor(res[:], parts[0][:], parts[2][:], ADD)
+            queue = nc.gpsimd if blk < 4 else nc.sync
+            queue.dma_start(out=out[blk * P : (blk + 1) * P, :], in_=res[:])
+
+        for blk in range(4):
+            slots_tile(blk)
+        for c in range(E // CHUNK):
+            gather_tokens(c)
+            for e in range(c * CHUNK, (c + 1) * CHUNK):
+                project_q(e)
+        for e in range(E):
+            project_k(e)
+        for e in range(WHOLE):
+            quantise(e, lambda s: raw[e][:, s, :], N)
+        for b in range(2):
+            for e in range(WHOLE, E):
+                quantise(e + 100 * (b + 1), lambda s: raw[e, b, s][:].rearrange("p j n -> p (j n)"), P)
+        combine(0)
+        combine(1)
+        slots_tile(4)
+        slots_tile(5)
+        for e in range(WHOLE):
+            project_v(e)
+        combine(2)
+        combine(3)
+        for b in range(2):
+            for e in range(WHOLE, E):
+                project_v_half(e, b)
+            combine(4 + b)

@@ -1,6 +1,7 @@
 from contextlib import ExitStack
 
 import concourse.mybir as mybir
+from concourse.masks import make_identity
 
 K, T, E, C, N, TOP = 1024, 512, 12, 128, 256, 3
 S = E * C
@@ -21,7 +22,8 @@ IDENT = mybir.ActivationFunctionType.Identity
 P = 128
 PASSES = 2
 CHUNK = 3
-WHOLE = 8
+WHOLE = 10
+ON_VECTOR = {(4, None, 1), (5, None, 1), (6, None, 1), (7, None, 1), (8, None, 1), (9, None, 1), (10, 0, 1), (11, 0, 1), (8, None, 0)}
 
 
 def tile_moe_qkv_kernel(tc, x_words, x_scales, wq_words, wq_scales, wk_words, wk_scales, wv, bias, gate, offs, pos1, pos2, pos3, out):
@@ -37,29 +39,32 @@ def tile_moe_qkv_kernel(tc, x_words, x_scales, wq_words, wq_scales, wk_words, wk
         xs = keep.tile([P, PASSES, T], U8, name="xs", align_bytes=64)
         qs = keep.tile([P, E * PASSES, N], U8, name="qs", align_bytes=64)
         ks = keep.tile([P, E * PASSES, N], U8, name="ks", align_bytes=64)
-        qw = [keep.tile([P, 3 * PASSES, 2 * N], U8, name=f"qw{i}", align_bytes=64) for i in range(4)]
-        kw = [keep.tile([P, 3 * PASSES, N], I32, name=f"kw{i}", align_bytes=64) for i in range(4)]
+        qw = [ring.tile([P, 3 * PASSES, 2 * N], U8, name=f"qw{i}", align_bytes=64) for i in range(4)]
+        kw = [ring.tile([P, 3 * PASSES, N], I32, name=f"kw{i}", align_bytes=64) for i in range(4)]
         bias_sb = keep.tile([P, 6, 16], F32, name="bias_sb")
+        gate_col = keep.tile([P, TOP, 8], F32, name="gate_col")
         gate_sb = [keep.tile([P, T], F32, name=f"gate_sb{r}") for r in range(TOP)]
+        ident = keep.tile([P, P], F32, name="ident")
         gw = [[keep.tile([P, CHUNK * C], U32, name=f"gw{s}_{c}", align_bytes=64) for c in range(E // CHUNK)] for s in range(PASSES)]
         gs = [[keep.tile([P, CHUNK * C], U8, name=f"gs{s}_{c}", align_bytes=64) for c in range(E // CHUNK)] for s in range(PASSES)]
         raw = {}
 
-        nc.vector.memset(xs[:].rearrange("p s t -> p (s t)").bitcast(I32), 0)
+        nc.gpsimd.memset(xs[:].rearrange("p s t -> p (s t)").bitcast(I32), 0)
         nc.vector.memset(qs[:].rearrange("p s t -> p (s t)").bitcast(I32), 0)
-        nc.gpsimd.memset(ks[:].rearrange("p s t -> p (s t)").bitcast(I32), 0)
+        make_identity(nc, ident[:])
+        nc.vector.memset(ks[:].rearrange("p s t -> p (s t)").bitcast(I32), 0)
 
-        def load_scales(dst, src):
+        def load_scales(dst, first, src, queue):
             for r in range(4):
-                nc.sync.dma_start(out=dst[r:P:32].bitcast(I32), in_=src[r].bitcast(I32))
+                queue.dma_start(out=dst[first + r : P : 32].bitcast(I32), in_=src[r].bitcast(I32))
 
         def load_v(e):
-            raw[e] = ring.tile([P, PASSES, 4 * N], F32, name="raw", bufs=5)
+            raw[e] = ring.tile([P, PASSES, 4 * N], F32, name="raw", tag=f"raw{e}", align_bytes=64)
             nc.sync.dma_start(out=raw[e][:], in_=wv[e].rearrange("(s p j) n -> p s (j n)", s=PASSES, j=4))
 
         def load_v_half(e, b):
             for s in range(PASSES):
-                raw[e, b, s] = keep.tile([P, 4, P], F32, name=f"raw{e}_{b}_{s}")
+                raw[e, b, s] = ring.tile([P, 4, P], F32, name="rawh", tag=f"raw{e}_{b}_{s}", align_bytes=64)
                 nc.sync.dma_start(out=raw[e, b, s][:], in_=wv[e, 512 * s : 512 * (s + 1), b * P : (b + 1) * P].rearrange("(p j) n -> p j n", j=4))
 
         def load_q(i):
@@ -71,38 +76,45 @@ def tile_moe_qkv_kernel(tc, x_words, x_scales, wq_words, wq_scales, wk_words, wk
         nc.sync.dma_start(offs_sb[:], offs)
         for s in range(PASSES):
             nc.sync.dma_start(out=xw[s][:], in_=x_words[s].rearrange("p t d -> p (t d)").bitcast(I32))
-        load_scales(xs, x_scales.rearrange("s (q r) t -> r q s t", r=4))
         load_v(0)
-        load_scales(qs, wq_scales.rearrange("e s (q r) n -> r q (e s) n", r=4))
-        load_q(0)
-        nc.sync.dma_start(out=bias_sb[:, :, 0:E], in_=bias.rearrange("(b p) e -> p b e", p=P))
-        load_v(1)
-        load_q(1)
-        load_v(2)
-        load_q(2)
+        nc.sync.dma_start(out=gate_col[:, :, 0:4], in_=gate[:, 0, :].rearrange("r (p j) -> p r j", j=4))
         for r, pos in enumerate((pos1, pos2, pos3)):
             nc.sync.dma_start(pos_sb[r][:], pos)
-        for r in range(TOP):
-            nc.sync.dma_start(out=gate_sb[r][:], in_=gate[r])
-        load_v(3)
+        load_scales(xs, 0, x_scales.rearrange("s (q r) t -> r q s t", r=4), nc.sync)
+        load_scales(qs, 0, wq_scales.rearrange("e s (q r) n -> r q (e s) n", r=4), nc.sync)
+        nc.sync.dma_start(out=bias_sb[:, :, 0:E], in_=bias.rearrange("(b p) e -> p b e", p=P))
+        load_q(0)
+        load_q(1)
+        load_q(2)
         load_q(3)
-        load_scales(ks, wk_scales.rearrange("e s (q r) n -> r q (e s) n", r=4))
-        load_v(4)
+        load_scales(ks, 4, wk_scales.rearrange("e s (q r) n -> r q (e s) n", r=4), nc.sync)
         load_k(0)
         load_k(1)
-        load_v(5)
         load_k(2)
         load_k(3)
+        load_v(1)
+        load_v(2)
+        load_v(3)
+        load_v(4)
+        load_v(5)
         load_v(6)
         load_v(7)
+        load_v(8)
+        load_v(9)
         for b in range(2):
             for e in range(WHOLE, E):
                 load_v_half(e, b)
 
-        y = {}
+        def bank():
+            return psum.tile([P, 4, P], F32, name="bank", bufs=4)
 
-        def slots_tile(blk):
-            y[blk] = ring.tile([P, S], F32, name="y", tag=f"y{blk % 4}")
+        def spread_gate(r):
+            acc = psum.tile([P, 4, P], F32, name="gate_bank", bufs=3)
+            for j in range(4):
+                nc.tensor.transpose(acc[:, j, :], gate_col[:, r, j : j + 1].to_broadcast([P, P]), ident[:])
+            nc.scalar.copy(out=gate_sb[r][:].rearrange("p (t j) -> p t j", j=4), in_=acc[:].rearrange("p j t -> p t j"))
+
+        y = {}
 
         def gather_tokens(c):
             cols = offs_sb[:, c * CHUNK * C // 16 : (c + 1) * CHUNK * C // 16]
@@ -111,7 +123,7 @@ def tile_moe_qkv_kernel(tc, x_words, x_scales, wq_words, wq_scales, wk_words, wk
                 nc.vector.tensor_copy(gs[s][c][:], xs[:, s, :].indirect(cols))
 
         def project(e, blks, lhs):
-            acc = psum.tile([P, 2, C], F32, name="acc", bufs=6)
+            acc = bank()
             c, u = divmod(e, CHUNK)
             for i, blk in enumerate(blks):
                 for s in range(PASSES):
@@ -132,64 +144,129 @@ def tile_moe_qkv_kernel(tc, x_words, x_scales, wq_words, wq_scales, wk_words, wk
             project(e, (0, 1), lambda s, b: (qw[e // 3][:, (e % 3) * PASSES + s, b * 2 * P : (b + 1) * 2 * P].bitcast(FP4X4), qs[:, e * PASSES + s, b * P : (b + 1) * P]))
 
         def project_k(e):
-            project(e, (2, 3), lambda s, b: (kw[e // 3][:, (e % 3) * PASSES + s, b * P : (b + 1) * P].bitcast(FP8X4), ks[:, e * PASSES + s, b * P : (b + 1) * P]))
-
-        def interleave(dst, src):
-            nc.scalar.copy(out=dst.rearrange("p (c i j) -> p c j i", i=4, j=4), in_=src.rearrange("p (j c i) -> p c j i", i=4, j=4))
+            project(e, (2, 3), lambda s, b: (kw[e // 3][:, (e % 3) * PASSES + s, b * P : (b + 1) * P].bitcast(FP8X4), ks[4:P, e * PASSES + s, b * P : (b + 1) * P]))
 
         vq = {}
 
-        def quantise(key, src, width):
-            staged = ring.tile([P, PASSES, 4 * width], BF16, name="staged", bufs=4, align_bytes=64)
+        def quantise(e, half):
+            width = N if half is None else P
+            kind = "whole" if half is None else "half"
+            staged = ring.tile([P, PASSES, 4 * width], BF16, name="staged", tag="staged" if half is None else f"kw{(e - WHOLE + half * (E - WHOLE)) % 4}", bufs=4 if half is None else 1, align_bytes=64)
             for s in range(PASSES):
-                interleave(staged[:, s, :], src(s))
-            codes = keep.tile([P, PASSES * width], U32, name=f"codes{key}", align_bytes=64)
-            scales = keep.tile([P, PASSES * width], U8, name=f"scales{key}", align_bytes=64)
+                src = raw[e][:, s, :] if half is None else raw[e, half, s][:].rearrange("p j n -> p (j n)")
+                dst = staged[:, s, :].rearrange("p (c i j) -> p c j i", i=4, j=4)
+                src = src.rearrange("p (j c i) -> p c j i", i=4, j=4)
+                if (e, half, s) in ON_VECTOR:
+                    nc.vector.tensor_copy(out=dst, in_=src)
+                else:
+                    nc.scalar.copy(out=dst, in_=src)
+            codes = ring.tile([P, PASSES * width], U32, name="codes", tag="codes" + kind, bufs=6 if half is None else 4, align_bytes=64)
+            scales = ring.tile([P, PASSES * width], U8, name="scales", tag="scales" + kind, bufs=6 if half is None else 4, align_bytes=64)
             nc.vector.quantize_mx(out=codes[:].bitcast(FP8X4), scales=scales[:], in_=staged[:].rearrange("p s w -> p (s w)"))
-            vq[key] = (codes, scales)
+            vq[e, half] = (codes, scales)
 
         def project_v(e):
-            codes, scales = vq[e]
+            codes, scales = vq[e, None]
             project(e, (4, 5), lambda s, b: (codes[:, s * N + b * P : s * N + (b + 1) * P].bitcast(FP8X4), scales[:, s * N + b * P : s * N + (b + 1) * P]))
 
         def project_v_half(e, half):
-            codes, scales = vq[e + 100 * (half + 1)]
+            codes, scales = vq[e, half]
             project(e, (4 + half,), lambda s, b: (codes[:, s * P : (s + 1) * P].bitcast(FP8X4), scales[:, s * P : (s + 1) * P]))
 
-        def combine(blk):
-            parts = []
+        parts = {}
+        turned = {}
+        spare = {0: "qw1", 1: "qw2", 2: "qw3", 3: "raw2", 4: "raw8", 5: "raw9"}
+        room = {0: "raw0", 1: "qw0", 2: "kw0", 3: "kw1", 4: ("raw0", "kw2", "kw3"), 5: "raw1"}
+
+        def fetch(blk):
+            if isinstance(room[blk], str):
+                whole = ring.tile([P, TOP, T], F32, name="parts", tag=room[blk], align_bytes=64)
+                parts[blk] = [whole[:, r, :] for r in range(TOP)]
+            else:
+                parts[blk] = [ring.tile([P, T], F32, name="part", tag=room[blk][r], align_bytes=64)[:] for r in range(TOP)]
             for r in range(TOP):
-                part = ring.tile([P, T], F32, name="part", tag=f"part{r}", bufs=2)
-                nc.vector.tensor_tensor(part[:], y[blk][:].indirect(pos_sb[r][:]), gate_sb[r][:], MULT)
-                parts.append(part)
-            nc.vector.tensor_tensor(parts[0][:], parts[0][:], parts[1][:], ADD)
-            res = ring.tile([P, T], F32, name="res", bufs=2)
-            nc.vector.tensor_tensor(res[:], parts[0][:], parts[2][:], ADD)
-            queue = nc.gpsimd if blk < 4 else nc.sync
-            queue.dma_start(out=out[blk * P : (blk + 1) * P, :], in_=res[:])
+                nc.vector.tensor_tensor(parts[blk][r], y[blk][:].indirect(pos_sb[r][:]), gate_sb[r][:], MULT)
+
+        def add_turned(blk):
+            acc = bank()
+            for c in range(4):
+                for r in range(TOP):
+                    nc.tensor.matmul(acc[:, c, :], parts[blk][r][:, c * P : (c + 1) * P], ident[:], start=(r == 0), stop=(r == TOP - 1), is_transpose=True)
+            turned[blk] = ring.tile([P, 4, P], F32, name="turned", tag="turned", bufs=1)
+            nc.scalar.copy(out=turned[blk][:], in_=acc[:])
+
+        def turn_back(blk):
+            acc = bank()
+            for c in range(4):
+                nc.tensor.transpose(acc[:, c, :], turned[blk][:, c, :], ident[:])
+            res = ring.tile([P, 4, P], F32, name="res", tag=spare[blk], align_bytes=64)
+            nc.scalar.copy(out=res[:], in_=acc[:])
+            queue = nc.scalar if blk == 4 else nc.sync
+            queue.dma_start(out=out[blk * P : (blk + 1) * P, :], in_=res[:].rearrange("p c t -> p (c t)"))
+
+        def add_plain(blk):
+            nc.vector.tensor_tensor(parts[blk][0], parts[blk][0], parts[blk][1], ADD)
+            res = ring.tile([P, T], F32, name="res", tag=spare[blk], align_bytes=64)
+            nc.vector.tensor_tensor(res[:], parts[blk][0], parts[blk][2], ADD)
+            nc.sync.dma_start(out=out[blk * P : (blk + 1) * P, :], in_=res[:])
 
         for blk in range(4):
-            slots_tile(blk)
-        for c in range(E // CHUNK):
-            gather_tokens(c)
-            for e in range(c * CHUNK, (c + 1) * CHUNK):
-                project_q(e)
-        for e in range(E):
+            y[blk] = keep.tile([P, S], F32, name=f"y{blk}")
+        gather_tokens(0)
+        for r in range(TOP):
+            spread_gate(r)
+        quantise(0, None)
+        for e in range(0, 3):
+            project_q(e)
+        gather_tokens(1)
+        for e in range(3, 6):
+            project_q(e)
+        gather_tokens(2)
+        for e in range(6, 9):
+            project_q(e)
+        gather_tokens(3)
+        for e in range(9, 12):
+            project_q(e)
+        for e in range(0, 12):
             project_k(e)
-        for e in range(WHOLE):
-            quantise(e, lambda s: raw[e][:, s, :], N)
-        for b in range(2):
-            for e in range(WHOLE, E):
-                quantise(e + 100 * (b + 1), lambda s: raw[e, b, s][:].rearrange("p j n -> p (j n)"), P)
-        combine(0)
-        combine(1)
-        slots_tile(4)
-        slots_tile(5)
-        for e in range(WHOLE):
+        fetch(0)
+        fetch(1)
+        quantise(1, None)
+        add_turned(0)
+        quantise(2, None)
+        turn_back(0)
+        add_turned(1)
+        quantise(3, None)
+        turn_back(1)
+        quantise(4, None)
+        quantise(5, None)
+        fetch(2)
+        add_plain(2)
+        fetch(3)
+        add_plain(3)
+        y[4] = ring.tile([P, S], F32, name="y4", tag="raw3", align_bytes=64)
+        y[5] = ring.tile([P, S], F32, name="y5", tag="raw4", align_bytes=64)
+        for e in range(0, 5):
             project_v(e)
-        combine(2)
-        combine(3)
-        for b in range(2):
-            for e in range(WHOLE, E):
-                project_v_half(e, b)
-            combine(4 + b)
+        quantise(6, None)
+        project_v(5)
+        quantise(7, None)
+        project_v(6)
+        quantise(8, None)
+        project_v(7)
+        quantise(9, None)
+        project_v(8)
+        for e in range(WHOLE, E):
+            quantise(e, 0)
+        project_v(9)
+        for e in range(WHOLE, E):
+            project_v_half(e, 0)
+        for e in range(WHOLE, E):
+            quantise(e, 1)
+        fetch(4)
+        for e in range(WHOLE, E):
+            project_v_half(e, 1)
+        fetch(5)
+        add_plain(5)
+        add_turned(4)
+        turn_back(4)

@@ -23,7 +23,7 @@ P = 128
 PASSES = 2
 CHUNK = 3
 WHOLE = 10
-ON_VECTOR = {(4, None, 1), (5, None, 1), (6, None, 1), (7, None, 1), (8, None, 1), (9, None, 1), (10, 0, 1), (11, 0, 1), (8, None, 0)}
+ON_VECTOR = {(8, None, 0), (8, None, 1), (9, None, 0), (9, None, 1), (10, 0, 1), (11, 0, 1)}
 
 
 def tile_moe_qkv_kernel(tc, x_words, x_scales, wq_words, wq_scales, wk_words, wk_scales, wv, bias, gate, offs, pos1, pos2, pos3, out):
@@ -76,26 +76,26 @@ def tile_moe_qkv_kernel(tc, x_words, x_scales, wq_words, wq_scales, wk_words, wk
         nc.sync.dma_start(offs_sb[:], offs)
         for s in range(PASSES):
             nc.sync.dma_start(out=xw[s][:], in_=x_words[s].rearrange("p t d -> p (t d)").bitcast(I32))
-        load_v(0)
         nc.sync.dma_start(out=gate_col[:, :, 0:4], in_=gate[:, 0, :].rearrange("r (p j) -> p r j", j=4))
+        load_v(0)
         for r, pos in enumerate((pos1, pos2, pos3)):
             nc.sync.dma_start(pos_sb[r][:], pos)
         load_scales(xs, 0, x_scales.rearrange("s (q r) t -> r q s t", r=4), nc.sync)
+        load_v(1)
+        load_v(2)
         load_scales(qs, 0, wq_scales.rearrange("e s (q r) n -> r q (e s) n", r=4), nc.sync)
         nc.sync.dma_start(out=bias_sb[:, :, 0:E], in_=bias.rearrange("(b p) e -> p b e", p=P))
         load_q(0)
         load_q(1)
+        load_v(3)
         load_q(2)
         load_q(3)
         load_scales(ks, 4, wk_scales.rearrange("e s (q r) n -> r q (e s) n", r=4), nc.sync)
+        load_v(4)
         load_k(0)
         load_k(1)
         load_k(2)
         load_k(3)
-        load_v(1)
-        load_v(2)
-        load_v(3)
-        load_v(4)
         load_v(5)
         load_v(6)
         load_v(7)
@@ -106,10 +106,10 @@ def tile_moe_qkv_kernel(tc, x_words, x_scales, wq_words, wq_scales, wk_words, wk
                 load_v_half(e, b)
 
         def bank():
-            return psum.tile([P, 4, P], F32, name="bank", bufs=4)
+            return psum.tile([P, 4, P], F32, name="bank", bufs=6)
 
         def spread_gate(r):
-            acc = psum.tile([P, 4, P], F32, name="gate_bank", bufs=3)
+            acc = bank()
             for j in range(4):
                 nc.tensor.transpose(acc[:, j, :], gate_col[:, r, j : j + 1].to_broadcast([P, P]), ident[:])
             nc.scalar.copy(out=gate_sb[r][:].rearrange("p (t j) -> p t j", j=4), in_=acc[:].rearrange("p j t -> p t j"))
@@ -147,11 +147,12 @@ def tile_moe_qkv_kernel(tc, x_words, x_scales, wq_words, wq_scales, wk_words, wk
             project(e, (2, 3), lambda s, b: (kw[e // 3][:, (e % 3) * PASSES + s, b * P : (b + 1) * P].bitcast(FP8X4), ks[4:P, e * PASSES + s, b * P : (b + 1) * P]))
 
         vq = {}
+        own = {8: "y2", 9: "y3"}
 
         def quantise(e, half):
             width = N if half is None else P
             kind = "whole" if half is None else "half"
-            staged = ring.tile([P, PASSES, 4 * width], BF16, name="staged", tag="staged" if half is None else f"kw{(e - WHOLE + half * (E - WHOLE)) % 4}", bufs=4 if half is None else 1, align_bytes=64)
+            staged = ring.tile([P, PASSES, 4 * width], BF16, name="staged", tag=own.get(e, "staged") if half is None else f"kw{(e - WHOLE + half * (E - WHOLE)) % 4}", bufs=3 if half is None and e not in own else 1, align_bytes=64)
             for s in range(PASSES):
                 src = raw[e][:, s, :] if half is None else raw[e, half, s][:].rearrange("p j n -> p (j n)")
                 dst = staged[:, s, :].rearrange("p (c i j) -> p c j i", i=4, j=4)
@@ -175,8 +176,8 @@ def tile_moe_qkv_kernel(tc, x_words, x_scales, wq_words, wq_scales, wk_words, wk
 
         parts = {}
         turned = {}
-        spare = {0: "qw1", 1: "qw2", 2: "qw3", 3: "raw2", 4: "raw8", 5: "raw9"}
-        room = {0: "raw0", 1: "qw0", 2: "kw0", 3: "kw1", 4: ("raw0", "kw2", "kw3"), 5: "raw1"}
+        spare = {0: "qw1", 1: "qw2", 2: "qw3", 3: "qw0", 4: "raw8", 5: "raw9"}
+        room = {0: "raw0", 1: "raw3", 2: "raw4", 3: "raw5", 4: ("raw0", "kw2", "kw3"), 5: "raw6"}
 
         def fetch(blk):
             if isinstance(room[blk], str):
@@ -192,7 +193,7 @@ def tile_moe_qkv_kernel(tc, x_words, x_scales, wq_words, wq_scales, wk_words, wk
             for c in range(4):
                 for r in range(TOP):
                     nc.tensor.matmul(acc[:, c, :], parts[blk][r][:, c * P : (c + 1) * P], ident[:], start=(r == 0), stop=(r == TOP - 1), is_transpose=True)
-            turned[blk] = ring.tile([P, 4, P], F32, name="turned", tag="turned", bufs=1)
+            turned[blk] = ring.tile([P, 4, P], F32, name="turned", tag="turned", bufs=2)
             nc.scalar.copy(out=turned[blk][:], in_=acc[:])
 
         def turn_back(blk):
@@ -211,11 +212,13 @@ def tile_moe_qkv_kernel(tc, x_words, x_scales, wq_words, wq_scales, wk_words, wk
             nc.sync.dma_start(out=out[blk * P : (blk + 1) * P, :], in_=res[:])
 
         for blk in range(4):
-            y[blk] = keep.tile([P, S], F32, name=f"y{blk}")
-        gather_tokens(0)
+            y[blk] = ring.tile([P, S], F32, name=f"y{blk}", align_bytes=64)
         for r in range(TOP):
             spread_gate(r)
+        gather_tokens(0)
         quantise(0, None)
+        quantise(1, None)
+        quantise(2, None)
         for e in range(0, 3):
             project_q(e)
         gather_tokens(1)
@@ -227,30 +230,28 @@ def tile_moe_qkv_kernel(tc, x_words, x_scales, wq_words, wq_scales, wk_words, wk
         gather_tokens(3)
         for e in range(9, 12):
             project_q(e)
-        for e in range(0, 12):
-            project_k(e)
-        fetch(0)
-        fetch(1)
-        quantise(1, None)
-        add_turned(0)
-        quantise(2, None)
-        turn_back(0)
-        add_turned(1)
         quantise(3, None)
-        turn_back(1)
+        y[4] = ring.tile([P, S], F32, name="y4", tag="raw1", align_bytes=64)
+        y[5] = ring.tile([P, S], F32, name="y5", tag="raw2", align_bytes=64)
         quantise(4, None)
-        quantise(5, None)
-        fetch(2)
-        add_plain(2)
-        fetch(3)
-        add_plain(3)
-        y[4] = ring.tile([P, S], F32, name="y4", tag="raw3", align_bytes=64)
-        y[5] = ring.tile([P, S], F32, name="y5", tag="raw4", align_bytes=64)
-        for e in range(0, 5):
+        for e in range(0, 3):
             project_v(e)
+        fetch(0)
+        add_plain(0)
+        for e in range(0, 6):
+            project_k(e)
+        project_v(3)
+        fetch(1)
+        add_plain(1)
+        for e in range(6, 12):
+            project_k(e)
+        quantise(5, None)
+        project_v(4)
         quantise(6, None)
+        fetch(2)
         project_v(5)
         quantise(7, None)
+        fetch(3)
         project_v(6)
         quantise(8, None)
         project_v(7)
@@ -268,5 +269,9 @@ def tile_moe_qkv_kernel(tc, x_words, x_scales, wq_words, wq_scales, wk_words, wk
             project_v_half(e, 1)
         fetch(5)
         add_plain(5)
+        add_turned(2)
+        add_turned(3)
+        turn_back(2)
+        turn_back(3)
         add_turned(4)
         turn_back(4)

@@ -82,20 +82,20 @@ def tile_moe_qkv_kernel(tc, x_words, x_scales, wq_words, wq_scales, wk_words, wk
             nc.sync.dma_start(pos_sb[r][:], pos)
         load_scales(xs, 0, x_scales.rearrange("s (q r) t -> r q s t", r=4), nc.sync)
         load_v(1)
-        load_v(2)
         load_scales(qs, 0, wq_scales.rearrange("e s (q r) n -> r q (e s) n", r=4), nc.sync)
         nc.sync.dma_start(out=bias_sb[:, :, 0:E], in_=bias.rearrange("(b p) e -> p b e", p=P))
         load_q(0)
         load_q(1)
-        load_v(3)
         load_q(2)
         load_q(3)
+        load_v(2)
         load_scales(ks, 4, wk_scales.rearrange("e s (q r) n -> r q (e s) n", r=4), nc.sync)
-        load_v(4)
         load_k(0)
+        load_v(3)
         load_k(1)
         load_k(2)
         load_k(3)
+        load_v(4)
         load_v(5)
         load_v(6)
         load_v(7)
@@ -155,8 +155,8 @@ def tile_moe_qkv_kernel(tc, x_words, x_scales, wq_words, wq_scales, wk_words, wk
             staged = ring.tile([P, PASSES, 4 * width], BF16, name="staged", tag=own.get(e, "staged") if half is None else f"kw{(e - WHOLE + half * (E - WHOLE)) % 4}", bufs=3 if half is None and e not in own else 1, align_bytes=64)
             for s in range(PASSES):
                 src = raw[e][:, s, :] if half is None else raw[e, half, s][:].rearrange("p j n -> p (j n)")
-                dst = staged[:, s, :].rearrange("p (c i j) -> p c j i", i=4, j=4)
-                src = src.rearrange("p (j c i) -> p c j i", i=4, j=4)
+                dst = staged[:, s, :].rearrange("p (c i j) -> p c j i", i=2, j=4)
+                src = src.rearrange("p (j c i) -> p c j i", i=2, j=4)
                 if (e, half, s) in ON_VECTOR:
                     nc.vector.tensor_copy(out=dst, in_=src)
                 else:
@@ -177,7 +177,7 @@ def tile_moe_qkv_kernel(tc, x_words, x_scales, wq_words, wq_scales, wk_words, wk
         parts = {}
         turned = {}
         spare = {0: "qw1", 1: "qw2", 2: "qw3", 3: "qw0", 4: "raw8", 5: "raw9"}
-        room = {0: "raw0", 1: "raw3", 2: "raw4", 3: "raw5", 4: ("raw0", "kw2", "kw3"), 5: "raw6"}
+        room = {0: "raw0", 1: "raw2", 2: "raw3", 3: "raw5", 4: ("raw4", "kw2", "kw3"), 5: "raw6"}
 
         def fetch(blk):
             if isinstance(room[blk], str):
@@ -218,7 +218,6 @@ def tile_moe_qkv_kernel(tc, x_words, x_scales, wq_words, wq_scales, wk_words, wk
         gather_tokens(0)
         quantise(0, None)
         quantise(1, None)
-        quantise(2, None)
         for e in range(0, 3):
             project_q(e)
         gather_tokens(1)
@@ -230,35 +229,37 @@ def tile_moe_qkv_kernel(tc, x_words, x_scales, wq_words, wq_scales, wk_words, wk
         gather_tokens(3)
         for e in range(9, 12):
             project_q(e)
-        quantise(3, None)
-        y[4] = ring.tile([P, S], F32, name="y4", tag="raw1", align_bytes=64)
-        y[5] = ring.tile([P, S], F32, name="y5", tag="raw2", align_bytes=64)
-        quantise(4, None)
-        for e in range(0, 3):
-            project_v(e)
+        quantise(2, None)
         fetch(0)
         add_plain(0)
+        quantise(3, None)
         for e in range(0, 6):
             project_k(e)
-        project_v(3)
         fetch(1)
         add_plain(1)
         for e in range(6, 12):
             project_k(e)
+        y[4] = ring.tile([P, S], F32, name="y4", tag="raw1", align_bytes=64)
+        y[5] = ring.tile([P, S], F32, name="y5", tag="y0", align_bytes=64)
+        quantise(4, None)
+        for e in range(0, 4):
+            project_v(e)
         quantise(5, None)
-        project_v(4)
-        quantise(6, None)
         fetch(2)
-        project_v(5)
+        add_plain(2)
+        quantise(6, None)
+        project_v(4)
         quantise(7, None)
         fetch(3)
-        project_v(6)
+        add_plain(3)
+        project_v(5)
         quantise(8, None)
-        project_v(7)
+        project_v(6)
         quantise(9, None)
-        project_v(8)
+        project_v(7)
         for e in range(WHOLE, E):
             quantise(e, 0)
+        project_v(8)
         project_v(9)
         for e in range(WHOLE, E):
             project_v_half(e, 0)
@@ -269,9 +270,5 @@ def tile_moe_qkv_kernel(tc, x_words, x_scales, wq_words, wq_scales, wk_words, wk
             project_v_half(e, 1)
         fetch(5)
         add_plain(5)
-        add_turned(2)
-        add_turned(3)
-        turn_back(2)
-        turn_back(3)
         add_turned(4)
         turn_back(4)

@@ -41,8 +41,9 @@ def tile_moe_qkv_kernel(tc, x_words, x_scales, wq_words, wq_scales, wk_words, wk
         ks = keep.tile([P, E * PASSES, N], U8, name="ks", align_bytes=64)
         qw = [ring.tile([P, 3 * PASSES, 2 * N], U8, name=f"qw{i}", align_bytes=64) for i in range(4)]
         kw = [ring.tile([P, 3 * PASSES, N], I32, name=f"kw{i}", align_bytes=64) for i in range(4)]
-        bias_sb = keep.tile([P, 6, 16], F32, name="bias_sb")
-        gate_col = keep.tile([P, TOP, 8], F32, name="gate_col")
+        bias_sb = keep.tile([P, E, 8], F32, name="bias_sb")
+        bias_rows = ring.tile([P, P, E], F32, name="bias_rows", tag="y2", align_bytes=64)
+        gate_col = keep.tile([P, 4, 4], F32, name="gate_col")
         gate_sb = [keep.tile([P, T], F32, name=f"gate_sb{r}") for r in range(TOP)]
         ident = keep.tile([P, P], F32, name="ident")
         gw = [[keep.tile([P, CHUNK * C], U32, name=f"gw{s}_{c}", align_bytes=64) for c in range(E // CHUNK)] for s in range(PASSES)]
@@ -50,8 +51,8 @@ def tile_moe_qkv_kernel(tc, x_words, x_scales, wq_words, wq_scales, wk_words, wk
         raw = {}
 
         nc.gpsimd.memset(xs[:].rearrange("p s t -> p (s t)").bitcast(I32), 0)
+        nc.vector.memset(bias_rows[:].rearrange("p n e -> p (n e)"), 0.0)
         nc.vector.memset(qs[:].rearrange("p s t -> p (s t)").bitcast(I32), 0)
-        make_identity(nc, ident[:])
         nc.vector.memset(ks[:].rearrange("p s t -> p (s t)").bitcast(I32), 0)
 
         def load_scales(dst, first, src, queue):
@@ -76,14 +77,14 @@ def tile_moe_qkv_kernel(tc, x_words, x_scales, wq_words, wq_scales, wk_words, wk
         nc.sync.dma_start(offs_sb[:], offs)
         for s in range(PASSES):
             nc.sync.dma_start(out=xw[s][:], in_=x_words[s].rearrange("p t d -> p (t d)").bitcast(I32))
-        nc.sync.dma_start(out=gate_col[:, :, 0:4], in_=gate[:, 0, :].rearrange("r (p j) -> p r j", j=4))
         load_v(0)
         for r, pos in enumerate((pos1, pos2, pos3)):
             nc.sync.dma_start(pos_sb[r][:], pos)
-        load_scales(xs, 0, x_scales.rearrange("s (q r) t -> r q s t", r=4), nc.sync)
         load_v(1)
+        nc.scalar.dma_start(out=bias_rows[0:6].rearrange("b n e -> b (n e)"), in_=bias.rearrange("(b n) e -> b (n e)", n=P))
+        nc.scalar.dma_start(out=bias_rows[6 : 6 + TOP].rearrange("b n e -> b (n e)")[:, 0:T], in_=gate[:, 0, :])
+        load_scales(xs, 0, x_scales.rearrange("s (q r) t -> r q s t", r=4), nc.sync)
         load_scales(qs, 0, wq_scales.rearrange("e s (q r) n -> r q (e s) n", r=4), nc.sync)
-        nc.sync.dma_start(out=bias_sb[:, :, 0:E], in_=bias.rearrange("(b p) e -> p b e", p=P))
         load_q(0)
         load_q(1)
         load_q(2)
@@ -105,14 +106,10 @@ def tile_moe_qkv_kernel(tc, x_words, x_scales, wq_words, wq_scales, wk_words, wk
             for e in range(WHOLE, E):
                 load_v_half(e, b)
 
+        make_identity(nc, ident[:])
+
         def bank():
             return psum.tile([P, 4, P], F32, name="bank", bufs=6)
-
-        def spread_gate(r):
-            acc = bank()
-            for j in range(4):
-                nc.tensor.transpose(acc[:, j, :], gate_col[:, r, j : j + 1].to_broadcast([P, P]), ident[:])
-            nc.scalar.copy(out=gate_sb[r][:].rearrange("p (t j) -> p t j", j=4), in_=acc[:].rearrange("p j t -> p t j"))
 
         y = {}
 
@@ -138,7 +135,7 @@ def tile_moe_qkv_kernel(tc, x_words, x_scales, wq_words, wq_scales, wk_words, wk
                         stop=(s == PASSES - 1),
                     )
             for i, blk in enumerate(blks):
-                nc.scalar.activation(out=y[blk][:, e * C : (e + 1) * C], in_=acc[:, i, :], func=IDENT, bias=bias_sb[:, blk, e : e + 1])
+                nc.scalar.activation(out=y[blk][:, e * C : (e + 1) * C], in_=acc[:, i, :], func=IDENT, bias=bias_sb[:, e, blk : blk + 1])
 
         def project_q(e):
             project(e, (0, 1), lambda s, b: (qw[e // 3][:, (e % 3) * PASSES + s, b * 2 * P : (b + 1) * 2 * P].bitcast(FP4X4), qs[:, e * PASSES + s, b * P : (b + 1) * P]))
@@ -193,7 +190,7 @@ def tile_moe_qkv_kernel(tc, x_words, x_scales, wq_words, wq_scales, wk_words, wk
             for c in range(4):
                 for r in range(TOP):
                     nc.tensor.matmul(acc[:, c, :], parts[blk][r][:, c * P : (c + 1) * P], ident[:], start=(r == 0), stop=(r == TOP - 1), is_transpose=True)
-            turned[blk] = ring.tile([P, 4, P], F32, name="turned", tag="turned", bufs=2)
+            turned[blk] = ring.tile([P, 4, P], F32, name="turned", tag="turned", bufs=1)
             nc.scalar.copy(out=turned[blk][:], in_=acc[:])
 
         def turn_back(blk):
@@ -213,10 +210,22 @@ def tile_moe_qkv_kernel(tc, x_words, x_scales, wq_words, wq_scales, wk_words, wk
 
         for blk in range(4):
             y[blk] = ring.tile([P, S], F32, name=f"y{blk}", align_bytes=64)
-        for r in range(TOP):
-            spread_gate(r)
         gather_tokens(0)
         quantise(0, None)
+        for first in range(0, E, 4):
+            acc = bank()
+            for i in range(4):
+                nc.tensor.transpose(acc[:, i, :], bias_rows[:, :, first + i], ident[:])
+            nc.scalar.copy(out=bias_sb[:, first : first + 4, 0:6], in_=acc[:, :, 0:6])
+        acc = bank()
+        for j in range(4):
+            nc.tensor.transpose(acc[:, j, :], bias_rows[:].rearrange("b n e -> b (n e)")[:, j * P : (j + 1) * P], ident[:])
+        nc.scalar.copy(out=gate_col[:, :, 0:TOP], in_=acc[:, :, 6 : 6 + TOP])
+        for r in range(TOP):
+            acc = bank()
+            for j in range(4):
+                nc.tensor.transpose(acc[:, j, :], gate_col[:, j, r : r + 1].to_broadcast([P, P]), ident[:])
+            nc.scalar.copy(out=gate_sb[r][:], in_=acc[:].rearrange("p j t -> p (j t)"))
         quantise(1, None)
         for e in range(0, 3):
             project_q(e)

@@ -18,12 +18,14 @@ FP4X4 = mybir.dt.float4_e2m1fn_x4
 MULT = mybir.AluOpType.mult
 ADD = mybir.AluOpType.add
 IDENT = mybir.ActivationFunctionType.Identity
+COPY = mybir.ActivationFunctionType.Copy
 
 P = 128
 PASSES = 2
 CHUNK = 3
-WHOLE = 10
-ON_VECTOR = {(8, None, 0), (8, None, 1), (9, None, 0), (9, None, 1), (10, 0, 1), (11, 0, 1)}
+CHUNKS = E // CHUNK
+LAST_BANKS = (6, 7)
+WHOLE = 8
 
 
 def tile_moe_qkv_kernel(tc, x_words, x_scales, wq_words, wq_scales, wk_words, wk_scales, wv, bias, gate, offs, pos1, pos2, pos3, out):
@@ -36,91 +38,106 @@ def tile_moe_qkv_kernel(tc, x_words, x_scales, wq_words, wq_scales, wk_words, wk
         offs_sb = keep.tile([P, S // 16], U16, name="offs_sb")
         pos_sb = [keep.tile([P, T // 16], U16, name=f"pos_sb{r}") for r in range(TOP)]
         xw = [keep.tile([P, T], I32, name=f"xw{s}", align_bytes=64) for s in range(PASSES)]
-        xs = keep.tile([P, PASSES, T], U8, name="xs", align_bytes=64)
+        xs = keep.tile([P, T], U8, name="xs", align_bytes=64)
         qs = keep.tile([P, E * PASSES, N], U8, name="qs", align_bytes=64)
-        ks = keep.tile([P, E * PASSES, N], U8, name="ks", align_bytes=64)
-        qw = [ring.tile([P, 3 * PASSES, 2 * N], U8, name=f"qw{i}", align_bytes=64) for i in range(4)]
+        qw = [ring.tile([P, 6 * PASSES, 2 * N], U8, name=f"qw{i}", align_bytes=64) for i in range(2)]
         kw = [ring.tile([P, 3 * PASSES, N], I32, name=f"kw{i}", align_bytes=64) for i in range(4)]
-        bias_sb = keep.tile([P, E, 8], F32, name="bias_sb")
-        bias_rows = ring.tile([P, P, E], F32, name="bias_rows", tag="y2", align_bytes=64)
-        gate_col = keep.tile([P, 4, 4], F32, name="gate_col")
+        ks = keep.tile([P, E * PASSES, N], U8, name="ks", align_bytes=64)
+        bias_sb = keep.tile([P, 6, E], F32, name="bias_sb")
+        gate_rows = keep.tile([P, P], F32, name="gate_rows")
+        gate_col = keep.tile([P, TOP * 4], F32, name="gate_col")
         gate_sb = [keep.tile([P, T], F32, name=f"gate_sb{r}") for r in range(TOP)]
         ident = keep.tile([P, P], F32, name="ident")
-        gw = [[keep.tile([P, CHUNK * C], U32, name=f"gw{s}_{c}", align_bytes=64) for c in range(E // CHUNK)] for s in range(PASSES)]
-        gs = [[keep.tile([P, CHUNK * C], U8, name=f"gs{s}_{c}", align_bytes=64) for c in range(E // CHUNK)] for s in range(PASSES)]
+        gw = [[keep.tile([P, CHUNK * C], U32, name=f"gw{s}_{c}", align_bytes=64) for c in range(CHUNKS)] for s in range(PASSES)]
+        gs_both = keep.tile([P, S], U8, name="gs_both", align_bytes=64)
+        gs_moved = keep.tile([P, S], U8, name="gs_moved", align_bytes=64)
+        gs = [gs_both, gs_moved]
         raw = {}
 
-        nc.gpsimd.memset(xs[:].rearrange("p s t -> p (s t)").bitcast(I32), 0)
-        nc.vector.memset(bias_rows[:].rearrange("p n e -> p (n e)"), 0.0)
+        nc.gpsimd.memset(xs[:].bitcast(I32), 0)
+        nc.gpsimd.memset(gate_rows[:], 0.0)
         nc.vector.memset(qs[:].rearrange("p s t -> p (s t)").bitcast(I32), 0)
+        nc.vector.memset(gs_moved[:].bitcast(I32), 0)
         nc.vector.memset(ks[:].rearrange("p s t -> p (s t)").bitcast(I32), 0)
 
-        def load_scales(dst, first, src, queue):
+        def chunk_offsets(c):
+            return offs_sb[:, c * CHUNK * C // 16 : (c + 1) * CHUNK * C // 16]
+
+        def load_scales(dst, first, src):
             for r in range(4):
-                queue.dma_start(out=dst[first + r : P : 32].bitcast(I32), in_=src[r].bitcast(I32))
+                nc.sync.dma_start(out=dst[first + r : P : 32].bitcast(I32), in_=src[r].bitcast(I32))
 
         def load_v(e):
             raw[e] = ring.tile([P, PASSES, 4 * N], F32, name="raw", tag=f"raw{e}", align_bytes=64)
             nc.sync.dma_start(out=raw[e][:], in_=wv[e].rearrange("(s p j) n -> p s (j n)", s=PASSES, j=4))
 
-        def load_v_half(e, b):
-            for s in range(PASSES):
-                raw[e, b, s] = ring.tile([P, 4, P], F32, name="rawh", tag=f"raw{e}_{b}_{s}", align_bytes=64)
-                nc.sync.dma_start(out=raw[e, b, s][:], in_=wv[e, 512 * s : 512 * (s + 1), b * P : (b + 1) * P].rearrange("(p j) n -> p j n", j=4))
+        def load_v_half(e, b, s):
+            raw[e, b, s] = ring.tile([P, 4, P], F32, name="rawh", tag=f"raw{e}_{b}_{s}", align_bytes=64)
+            nc.sync.dma_start(out=raw[e, b, s][:], in_=wv[e, 512 * s : 512 * (s + 1), b * P : (b + 1) * P].rearrange("(p j) n -> p j n", j=4))
 
         def load_q(i):
-            nc.sync.dma_start(out=qw[i][:].bitcast(I32), in_=wq_words[3 * i : 3 * i + 3].rearrange("e s p w -> p (e s) w").bitcast(I32))
+            nc.sync.dma_start(out=qw[i][:].bitcast(I32), in_=wq_words[6 * i : 6 * i + 6].rearrange("e s p w -> p (e s) w").bitcast(I32))
 
         def load_k(i):
             nc.sync.dma_start(out=kw[i][:], in_=wk_words[3 * i : 3 * i + 3].rearrange("e s p n d -> p (e s) (n d)").bitcast(I32))
 
         nc.sync.dma_start(offs_sb[:], offs)
+        for q in range(4):
+            nc.sync.dma_start(out=xs[32 * q : 32 * q + 8].bitcast(I32), in_=x_scales[:, 4 * q : 4 * q + 4, :].bitcast(I32))
         for s in range(PASSES):
             nc.sync.dma_start(out=xw[s][:], in_=x_words[s].rearrange("p t d -> p (t d)").bitcast(I32))
         load_v(0)
+        nc.sync.dma_start(out=gate_rows[0 : TOP * 4], in_=gate[:, 0, :].rearrange("r (c t) -> r c t", t=P))
+        nc.sync.dma_start(out=bias_sb[:], in_=bias.rearrange("(b n) e -> n b e", n=P))
+        load_scales(qs, 0, wq_scales.rearrange("e s (q r) n -> r q (e s) n", r=4))
+        load_q(0)
+        for c in range(CHUNKS):
+            nc.vector.tensor_copy(gs_both[:, c * CHUNK * C : (c + 1) * CHUNK * C], xs[:].indirect(chunk_offsets(c)))
+        for r in range(4):
+            nc.sync.dma_start(out=gs_moved[r:P:32].bitcast(I32), in_=gs_both[4 + r : P : 32].bitcast(I32))
+        load_q(1)
         for r, pos in enumerate((pos1, pos2, pos3)):
             nc.sync.dma_start(pos_sb[r][:], pos)
-        load_v(1)
-        nc.scalar.dma_start(out=bias_rows[0:6].rearrange("b n e -> b (n e)"), in_=bias.rearrange("(b n) e -> b (n e)", n=P))
-        nc.scalar.dma_start(out=bias_rows[6 : 6 + TOP].rearrange("b n e -> b (n e)")[:, 0:T], in_=gate[:, 0, :])
-        load_scales(xs, 0, x_scales.rearrange("s (q r) t -> r q s t", r=4), nc.sync)
-        load_scales(qs, 0, wq_scales.rearrange("e s (q r) n -> r q (e s) n", r=4), nc.sync)
-        load_q(0)
-        load_q(1)
-        load_q(2)
-        load_q(3)
-        load_v(2)
-        load_scales(ks, 4, wk_scales.rearrange("e s (q r) n -> r q (e s) n", r=4), nc.sync)
-        load_k(0)
-        load_v(3)
-        load_k(1)
-        load_k(2)
-        load_k(3)
-        load_v(4)
-        load_v(5)
-        load_v(6)
-        load_v(7)
-        load_v(8)
-        load_v(9)
-        for b in range(2):
-            for e in range(WHOLE, E):
-                load_v_half(e, b)
 
         make_identity(nc, ident[:])
 
-        def bank():
-            return psum.tile([P, 4, P], F32, name="bank", bufs=6)
+        turns = {"sum": list(range(4)) * 12, "turn": list(range(4, 8)) * 4}
+
+        def bank(kind="sum", which=None):
+            return psum.tile([P, 4, P], F32, name="bank", tag=f"bank{turns[kind].pop(0) if which is None else which}")
+
+
+        acc = bank()
+        nc.tensor.transpose(acc[:, 0, :], gate_rows[:], ident[:])
+        nc.scalar.copy(out=gate_col[:], in_=acc[:, 0, 0 : TOP * 4])
+        for r in range(TOP):
+            acc = bank()
+            for c in range(4):
+                nc.tensor.transpose(acc[:, c, :], gate_col[:, 4 * r + c : 4 * r + c + 1].to_broadcast([P, P]), ident[:])
+            nc.scalar.copy(out=gate_sb[r][:], in_=acc[:].rearrange("p c t -> p (c t)"))
+
+        load_scales(ks, 4, wk_scales.rearrange("e s (q r) n -> r q (e s) n", r=4))
+        load_k(0)
+        load_k(1)
+        load_v(1)
+        load_k(2)
+        load_k(3)
+        for e in range(2, WHOLE):
+            load_v(e)
+        for b in range(2):
+            for pair in range(WHOLE, E, 2):
+                for s in range(PASSES):
+                    for e in (pair, pair + 1):
+                        load_v_half(e, b, s)
 
         y = {}
 
-        def gather_tokens(c):
-            cols = offs_sb[:, c * CHUNK * C // 16 : (c + 1) * CHUNK * C // 16]
+        def gather_words(c):
             for s in range(PASSES):
-                nc.vector.tensor_copy(gw[s][c][:], xw[s][:].bitcast(U32).indirect(cols))
-                nc.vector.tensor_copy(gs[s][c][:], xs[:, s, :].indirect(cols))
+                nc.vector.tensor_copy(gw[s][c][:], xw[s][:].bitcast(U32).indirect(chunk_offsets(c)))
 
-        def project(e, blks, lhs):
-            acc = bank()
+        def project(e, blks, lhs, engine="S", which=None):
+            acc = bank("sum", which)
             c, u = divmod(e, CHUNK)
             for i, blk in enumerate(blks):
                 for s in range(PASSES):
@@ -130,154 +147,133 @@ def tile_moe_qkv_kernel(tc, x_words, x_scales, wq_words, wq_scales, wk_words, wk
                         lhsT=words,
                         lhsT_scale=scales,
                         rhs=gw[s][c][:, u * C : (u + 1) * C].bitcast(FP8X4),
-                        rhs_scale=gs[s][c][:, u * C : (u + 1) * C],
+                        rhs_scale=gs[s][:, e * C : (e + 1) * C],
                         start=(s == 0),
                         stop=(s == PASSES - 1),
                     )
             for i, blk in enumerate(blks):
-                nc.scalar.activation(out=y[blk][:, e * C : (e + 1) * C], in_=acc[:, i, :], func=IDENT, bias=bias_sb[:, e, blk : blk + 1])
+                if engine == "V":
+                    nc.vector.tensor_scalar_add(out=y[blk][:, e * C : (e + 1) * C], in0=acc[:, i, :], scalar1=bias_sb[:, blk, e : e + 1])
+                else:
+                    nc.scalar.activation(out=y[blk][:, e * C : (e + 1) * C], in_=acc[:, i, :], func=IDENT, bias=bias_sb[:, blk, e : e + 1])
 
         def project_q(e):
-            project(e, (0, 1), lambda s, b: (qw[e // 3][:, (e % 3) * PASSES + s, b * 2 * P : (b + 1) * 2 * P].bitcast(FP4X4), qs[:, e * PASSES + s, b * P : (b + 1) * P]))
+            project(e, (0, 1), lambda s, b: (qw[e // 6][:, (e % 6) * PASSES + s, b * 2 * P : (b + 1) * 2 * P].bitcast(FP4X4), qs[:, e * PASSES + s, b * P : (b + 1) * P]), "V" if e >= 10 else "S")
 
         def project_k(e):
             project(e, (2, 3), lambda s, b: (kw[e // 3][:, (e % 3) * PASSES + s, b * P : (b + 1) * P].bitcast(FP8X4), ks[4:P, e * PASSES + s, b * P : (b + 1) * P]))
 
         vq = {}
-        own = {8: "y2", 9: "y3"}
+        staged = {}
 
-        def quantise(e, half):
-            width = N if half is None else P
-            kind = "whole" if half is None else "half"
-            staged = ring.tile([P, PASSES, 4 * width], BF16, name="staged", tag=own.get(e, "staged") if half is None else f"kw{(e - WHOLE + half * (E - WHOLE)) % 4}", bufs=3 if half is None and e not in own else 1, align_bytes=64)
+        def round_copy(dst, src, engine):
+            dst = dst.rearrange("p (c i j) -> p c j i", i=2, j=4)
+            src = src.rearrange("p (j c i) -> p c j i", i=2, j=4)
+            if engine == "V":
+                nc.vector.tensor_copy(out=dst, in_=src)
+            else:
+                nc.scalar.copy(out=dst, in_=src)
+
+        def cast(e, engines):
+            staged[e] = ring.tile([P, PASSES, 4 * N], BF16, name="staged", tag="staged", bufs=3, align_bytes=64)
             for s in range(PASSES):
-                src = raw[e][:, s, :] if half is None else raw[e, half, s][:].rearrange("p j n -> p (j n)")
-                dst = staged[:, s, :].rearrange("p (c i j) -> p c j i", i=2, j=4)
-                src = src.rearrange("p (j c i) -> p c j i", i=2, j=4)
-                if (e, half, s) in ON_VECTOR:
-                    nc.vector.tensor_copy(out=dst, in_=src)
-                else:
-                    nc.scalar.copy(out=dst, in_=src)
-            codes = ring.tile([P, PASSES * width], U32, name="codes", tag="codes" + kind, bufs=6 if half is None else 4, align_bytes=64)
-            scales = ring.tile([P, PASSES * width], U8, name="scales", tag="scales" + kind, bufs=6 if half is None else 4, align_bytes=64)
-            nc.vector.quantize_mx(out=codes[:].bitcast(FP8X4), scales=scales[:], in_=staged[:].rearrange("p s w -> p (s w)"))
-            vq[e, half] = (codes, scales)
+                round_copy(staged[e][:, s, :], raw[e][:, s, :], engines[s])
+
+        def quantise(key, width):
+            codes = ring.tile([P, width], U32, name="codes", tag="codes", bufs=4, align_bytes=64)
+            scales = ring.tile([P, width], U8, name="scales", tag="scales", bufs=4, align_bytes=64)
+            nc.vector.quantize_mx(out=codes[:].bitcast(FP8X4), scales=scales[:], in_=staged[key][:].rearrange("p s w -> p (s w)"))
+            vq[key] = (codes, scales)
 
         def project_v(e):
-            codes, scales = vq[e, None]
+            codes, scales = vq[e]
             project(e, (4, 5), lambda s, b: (codes[:, s * N + b * P : s * N + (b + 1) * P].bitcast(FP8X4), scales[:, s * N + b * P : s * N + (b + 1) * P]))
 
-        def project_v_half(e, half):
-            codes, scales = vq[e, half]
-            project(e, (4 + half,), lambda s, b: (codes[:, s * P : (s + 1) * P].bitcast(FP8X4), scales[:, s * P : (s + 1) * P]))
+        def cast_pair(pair, b, s):
+            staged[pair, b, s] = ring.tile([P, 2, 4 * P], BF16, name="staged", tag="staged", bufs=3, align_bytes=64)
+            for i in range(2):
+                round_copy(staged[pair, b, s][:, i, :], raw[pair + i, b, s][:].rearrange("p j n -> p (j n)"), "V")
+
+        def project_pair(pair, b, engine, banks=(None, None)):
+            for i in range(2):
+                project(pair + i, (4 + b,), lambda s, unused: (vq[pair, b, s][0][:, i * P : (i + 1) * P].bitcast(FP8X4), vq[pair, b, s][1][:, i * P : (i + 1) * P]), engine, banks[i])
 
         parts = {}
-        turned = {}
-        spare = {0: "qw1", 1: "qw2", 2: "qw3", 3: "qw0", 4: "raw8", 5: "raw9"}
-        room = {0: "raw0", 1: "raw2", 2: "raw3", 3: "raw5", 4: ("raw4", "kw2", "kw3"), 5: "raw6"}
+        room = {0: "raw0", 1: "qw0", 2: "qw1", 3: "kw2", 4: "kw1", 5: "kw0"}
 
         def fetch(blk):
-            if isinstance(room[blk], str):
-                whole = ring.tile([P, TOP, T], F32, name="parts", tag=room[blk], align_bytes=64)
-                parts[blk] = [whole[:, r, :] for r in range(TOP)]
-            else:
-                parts[blk] = [ring.tile([P, T], F32, name="part", tag=room[blk][r], align_bytes=64)[:] for r in range(TOP)]
+            whole = ring.tile([P, TOP, T], F32, name="parts", tag=room[blk], align_bytes=64)
+            parts[blk] = [whole[:, r, :] for r in range(TOP)]
             for r in range(TOP):
                 nc.vector.tensor_tensor(parts[blk][r], y[blk][:].indirect(pos_sb[r][:]), gate_sb[r][:], MULT)
 
-        def add_turned(blk):
-            acc = bank()
+        def fetch_plain(blk):
+            whole = ring.tile([P, TOP, T], F32, name="parts", tag=room[blk], align_bytes=64)
+            parts[blk] = [whole[:, r, :] for r in range(TOP)]
+            for r in range(TOP):
+                nc.scalar.activation(out=parts[blk][r], in_=y[blk][:].indirect(pos_sb[r][:]), func=COPY)
+
+        def weigh_turned(blk):
+            scaled = ring.tile([P, 4, TOP, P], F32, name="scaled", tag="scaled", bufs=1)
+            for c in range(4):
+                acc = bank("turn", LAST_BANKS[c % 2] if blk == 4 else None)
+                for r in range(TOP):
+                    nc.tensor.transpose(acc[:, r, :], parts[blk][r][:, c * P : (c + 1) * P], ident[:])
+                for r in range(TOP):
+                    nc.scalar.activation(out=scaled[:, c, r, :], in_=acc[:, r, :], func=COPY, scale=gate_col[:, 4 * r + c : 4 * r + c + 1])
+            acc = bank("turn")
             for c in range(4):
                 for r in range(TOP):
-                    nc.tensor.matmul(acc[:, c, :], parts[blk][r][:, c * P : (c + 1) * P], ident[:], start=(r == 0), stop=(r == TOP - 1), is_transpose=True)
-            turned[blk] = ring.tile([P, 4, P], F32, name="turned", tag="turned", bufs=1)
-            nc.scalar.copy(out=turned[blk][:], in_=acc[:])
-
-        def turn_back(blk):
-            acc = bank()
-            for c in range(4):
-                nc.tensor.transpose(acc[:, c, :], turned[blk][:, c, :], ident[:])
-            res = ring.tile([P, 4, P], F32, name="res", tag=spare[blk], align_bytes=64)
-            nc.scalar.copy(out=res[:], in_=acc[:])
-            queue = nc.scalar if blk == 4 else nc.sync
-            queue.dma_start(out=out[blk * P : (blk + 1) * P, :], in_=res[:].rearrange("p c t -> p (c t)"))
+                    nc.tensor.matmul(acc[:, c, :], scaled[:, c, r, :], ident[:], start=(r == 0), stop=(r == TOP - 1), is_transpose=True)
+            nc.scalar.copy(out=parts[blk][0], in_=acc[:].rearrange("p c t -> p (c t)"))
+            nc.sync.dma_start(out=out[blk * P : (blk + 1) * P, :], in_=parts[blk][0])
 
         def add_plain(blk):
             nc.vector.tensor_tensor(parts[blk][0], parts[blk][0], parts[blk][1], ADD)
-            res = ring.tile([P, T], F32, name="res", tag=spare[blk], align_bytes=64)
-            nc.vector.tensor_tensor(res[:], parts[blk][0], parts[blk][2], ADD)
-            nc.sync.dma_start(out=out[blk * P : (blk + 1) * P, :], in_=res[:])
+            nc.vector.tensor_tensor(parts[blk][1], parts[blk][0], parts[blk][2], ADD)
+            nc.sync.dma_start(out=out[blk * P : (blk + 1) * P, :], in_=parts[blk][1])
 
         for blk in range(4):
             y[blk] = ring.tile([P, S], F32, name=f"y{blk}", align_bytes=64)
-        gather_tokens(0)
-        quantise(0, None)
-        for first in range(0, E, 4):
-            acc = bank()
-            for i in range(4):
-                nc.tensor.transpose(acc[:, i, :], bias_rows[:, :, first + i], ident[:])
-            nc.scalar.copy(out=bias_sb[:, first : first + 4, 0:6], in_=acc[:, :, 0:6])
-        acc = bank()
-        for j in range(4):
-            nc.tensor.transpose(acc[:, j, :], bias_rows[:].rearrange("b n e -> b (n e)")[:, j * P : (j + 1) * P], ident[:])
-        nc.scalar.copy(out=gate_col[:, :, 0:TOP], in_=acc[:, :, 6 : 6 + TOP])
-        for r in range(TOP):
-            acc = bank()
-            for j in range(4):
-                nc.tensor.transpose(acc[:, j, :], gate_col[:, j, r : r + 1].to_broadcast([P, P]), ident[:])
-            nc.scalar.copy(out=gate_sb[r][:], in_=acc[:].rearrange("p j t -> p (j t)"))
-        quantise(1, None)
-        for e in range(0, 3):
-            project_q(e)
-        gather_tokens(1)
-        for e in range(3, 6):
-            project_q(e)
-        gather_tokens(2)
-        for e in range(6, 9):
-            project_q(e)
-        gather_tokens(3)
-        for e in range(9, 12):
-            project_q(e)
-        quantise(2, None)
+        cast(0, "SS")
+        for c in range(CHUNKS):
+            gather_words(c)
+            for e in range(c * CHUNK, (c + 1) * CHUNK):
+                project_q(e)
+        quantise(0, PASSES * N)
         fetch(0)
+        fetch(1)
         add_plain(0)
-        quantise(3, None)
+        add_plain(1)
         for e in range(0, 6):
             project_k(e)
-        fetch(1)
-        add_plain(1)
+        cast(1, "SS")
         for e in range(6, 12):
             project_k(e)
+        quantise(1, PASSES * N)
         y[4] = ring.tile([P, S], F32, name="y4", tag="raw1", align_bytes=64)
-        y[5] = ring.tile([P, S], F32, name="y5", tag="y0", align_bytes=64)
-        quantise(4, None)
-        for e in range(0, 4):
-            project_v(e)
-        quantise(5, None)
-        fetch(2)
-        add_plain(2)
-        quantise(6, None)
-        project_v(4)
-        quantise(7, None)
-        fetch(3)
-        add_plain(3)
-        project_v(5)
-        quantise(8, None)
-        project_v(6)
-        quantise(9, None)
-        project_v(7)
-        for e in range(WHOLE, E):
-            quantise(e, 0)
-        project_v(8)
-        project_v(9)
-        for e in range(WHOLE, E):
-            project_v_half(e, 0)
-        for e in range(WHOLE, E):
-            quantise(e, 1)
-        fetch(4)
-        for e in range(WHOLE, E):
-            project_v_half(e, 1)
+        y[5] = ring.tile([P, S], F32, name="y5", tag="raw2", align_bytes=64)
+        fetch_plain(2)
+        fetch_plain(3)
+        weigh_turned(2)
+        weigh_turned(3)
+        for e in range(2, WHOLE):
+            cast(e, "VV")
+            quantise(e, PASSES * N)
+            project_v(e - 2)
+        project_v(WHOLE - 2)
+        project_v(WHOLE - 1)
+        for b in range(2):
+            for pair in range(WHOLE, E, 2):
+                for s in range(PASSES):
+                    cast_pair(pair, b, s)
+                    quantise((pair, b, s), 2 * P)
+                if (b, pair) == (1, E - 2):
+                    project_pair(pair, b, "V", LAST_BANKS)
+                else:
+                    project_pair(pair, b, "S")
+            if b == 0:
+                fetch_plain(4)
         fetch(5)
         add_plain(5)
-        add_turned(4)
-        turn_back(4)
+        weigh_turned(4)

@@ -38,7 +38,7 @@ def tile_moe_qkv_kernel(tc, x_words, x_scales, wq_words, wq_scales, wk_words, wk
         offs_sb = keep.tile([P, S // 16], U16, name="offs_sb")
         pos_sb = [keep.tile([P, T // 16], U16, name=f"pos_sb{r}") for r in range(TOP)]
         xw = [keep.tile([P, T], I32, name=f"xw{s}", align_bytes=64) for s in range(PASSES)]
-        xs = keep.tile([P, T], U8, name="xs", align_bytes=64)
+        xs = keep.tile([P, PASSES, T], U8, name="xs", align_bytes=64)
         qs = keep.tile([P, E * PASSES, N], U8, name="qs", align_bytes=64)
         qw = [ring.tile([P, 6 * PASSES, 2 * N], U8, name=f"qw{i}", align_bytes=64) for i in range(2)]
         kw = [ring.tile([P, 3 * PASSES, N], I32, name=f"kw{i}", align_bytes=64) for i in range(4)]
@@ -49,15 +49,12 @@ def tile_moe_qkv_kernel(tc, x_words, x_scales, wq_words, wq_scales, wk_words, wk
         gate_sb = [keep.tile([P, T], F32, name=f"gate_sb{r}") for r in range(TOP)]
         ident = keep.tile([P, P], F32, name="ident")
         gw = [[keep.tile([P, CHUNK * C], U32, name=f"gw{s}_{c}", align_bytes=64) for c in range(CHUNKS)] for s in range(PASSES)]
-        gs_both = keep.tile([P, S], U8, name="gs_both", align_bytes=64)
-        gs_moved = keep.tile([P, S], U8, name="gs_moved", align_bytes=64)
-        gs = [gs_both, gs_moved]
+        gs = [keep.tile([P, S], U8, name=f"gs{s}", align_bytes=64) for s in range(PASSES)]
         raw = {}
 
-        nc.gpsimd.memset(xs[:].bitcast(I32), 0)
+        nc.gpsimd.memset(xs[:].rearrange("p s t -> p (s t)").bitcast(I32), 0)
         nc.gpsimd.memset(gate_rows[:], 0.0)
         nc.vector.memset(qs[:].rearrange("p s t -> p (s t)").bitcast(I32), 0)
-        nc.vector.memset(gs_moved[:].bitcast(I32), 0)
         nc.vector.memset(ks[:].rearrange("p s t -> p (s t)").bitcast(I32), 0)
 
         def chunk_offsets(c):
@@ -82,19 +79,15 @@ def tile_moe_qkv_kernel(tc, x_words, x_scales, wq_words, wq_scales, wk_words, wk
             nc.sync.dma_start(out=kw[i][:], in_=wk_words[3 * i : 3 * i + 3].rearrange("e s p n d -> p (e s) (n d)").bitcast(I32))
 
         nc.sync.dma_start(offs_sb[:], offs)
-        for q in range(4):
-            nc.sync.dma_start(out=xs[32 * q : 32 * q + 8].bitcast(I32), in_=x_scales[:, 4 * q : 4 * q + 4, :].bitcast(I32))
         for s in range(PASSES):
             nc.sync.dma_start(out=xw[s][:], in_=x_words[s].rearrange("p t d -> p (t d)").bitcast(I32))
-        load_v(0)
+        load_scales(xs, 0, x_scales.rearrange("s (q r) t -> r q s t", r=4))
         nc.sync.dma_start(out=gate_rows[0 : TOP * 4], in_=gate[:, 0, :].rearrange("r (c t) -> r c t", t=P))
-        nc.sync.dma_start(out=bias_sb[:], in_=bias.rearrange("(b n) e -> n b e", n=P))
         load_scales(qs, 0, wq_scales.rearrange("e s (q r) n -> r q (e s) n", r=4))
+        load_scales(ks, 4, wk_scales.rearrange("e s (q r) n -> r q (e s) n", r=4))
+        load_v(0)
         load_q(0)
-        for c in range(CHUNKS):
-            nc.vector.tensor_copy(gs_both[:, c * CHUNK * C : (c + 1) * CHUNK * C], xs[:].indirect(chunk_offsets(c)))
-        for r in range(4):
-            nc.sync.dma_start(out=gs_moved[r:P:32].bitcast(I32), in_=gs_both[4 + r : P : 32].bitcast(I32))
+        nc.sync.dma_start(out=bias_sb[:], in_=bias.rearrange("(b n) e -> n b e", n=P))
         load_q(1)
         for r, pos in enumerate((pos1, pos2, pos3)):
             nc.sync.dma_start(pos_sb[r][:], pos)
@@ -116,7 +109,6 @@ def tile_moe_qkv_kernel(tc, x_words, x_scales, wq_words, wq_scales, wk_words, wk
                 nc.tensor.transpose(acc[:, c, :], gate_col[:, 4 * r + c : 4 * r + c + 1].to_broadcast([P, P]), ident[:])
             nc.scalar.copy(out=gate_sb[r][:], in_=acc[:].rearrange("p c t -> p (c t)"))
 
-        load_scales(ks, 4, wk_scales.rearrange("e s (q r) n -> r q (e s) n", r=4))
         load_k(0)
         load_k(1)
         load_v(1)
@@ -135,6 +127,7 @@ def tile_moe_qkv_kernel(tc, x_words, x_scales, wq_words, wq_scales, wk_words, wk
         def gather_words(c):
             for s in range(PASSES):
                 nc.vector.tensor_copy(gw[s][c][:], xw[s][:].bitcast(U32).indirect(chunk_offsets(c)))
+                nc.vector.tensor_copy(gs[s][:, c * CHUNK * C : (c + 1) * CHUNK * C], xs[:, s, :].indirect(chunk_offsets(c)))
 
         def project(e, blks, lhs, engine="S", which=None):
             acc = bank("sum", which)
@@ -271,7 +264,7 @@ def tile_moe_qkv_kernel(tc, x_words, x_scales, wq_words, wq_scales, wk_words, wk
                 if (b, pair) == (1, E - 2):
                     project_pair(pair, b, "V", LAST_BANKS)
                 else:
-                    project_pair(pair, b, "S")
+                    project_pair(pair, b, "V" if b else "S")
             if b == 0:
                 fetch_plain(4)
         fetch(5)

@@ -44,7 +44,7 @@ def tile_moe_qkv_kernel(tc, x_words, x_scales, wq_words, wq_scales, wk_words, wk
         kw = [ring.tile([P, 3 * PASSES, N], I32, name=f"kw{i}", align_bytes=64) for i in range(4)]
         ks = keep.tile([P, E * PASSES, N], U8, name="ks", align_bytes=64)
         bias_sb = keep.tile([P, 6, E], F32, name="bias_sb")
-        gate_rows = keep.tile([P, P], F32, name="gate_rows")
+        gate_rows = keep.tile([P, TOP, P], F32, name="gate_rows")
         gate_col = keep.tile([P, TOP * 4], F32, name="gate_col")
         gate_sb = [keep.tile([P, T], F32, name=f"gate_sb{r}") for r in range(TOP)]
         ident = keep.tile([P, P], F32, name="ident")
@@ -53,16 +53,12 @@ def tile_moe_qkv_kernel(tc, x_words, x_scales, wq_words, wq_scales, wk_words, wk
         raw = {}
 
         nc.gpsimd.memset(xs[:].rearrange("p s t -> p (s t)").bitcast(I32), 0)
-        nc.gpsimd.memset(gate_rows[:], 0.0)
+        nc.gpsimd.memset(gate_rows[:].rearrange("c r t -> c (r t)"), 0.0)
         nc.vector.memset(qs[:].rearrange("p s t -> p (s t)").bitcast(I32), 0)
         nc.vector.memset(ks[:].rearrange("p s t -> p (s t)").bitcast(I32), 0)
 
         def chunk_offsets(c):
             return offs_sb[:, c * CHUNK * C // 16 : (c + 1) * CHUNK * C // 16]
-
-        def load_scales(dst, first, src):
-            for r in range(4):
-                nc.sync.dma_start(out=dst[first + r : P : 32].bitcast(I32), in_=src[r].bitcast(I32))
 
         def load_v(e):
             raw[e] = ring.tile([P, PASSES, 4 * N], F32, name="raw", tag=f"raw{e}", align_bytes=64)
@@ -79,36 +75,22 @@ def tile_moe_qkv_kernel(tc, x_words, x_scales, wq_words, wq_scales, wk_words, wk
             nc.sync.dma_start(out=kw[i][:], in_=wk_words[3 * i : 3 * i + 3].rearrange("e s p n d -> p (e s) (n d)").bitcast(I32))
 
         nc.sync.dma_start(offs_sb[:], offs)
+        for q in range(4):
+            nc.sync.dma_start(out=xs[32 * q : 32 * q + 4].bitcast(I32), in_=x_scales[:, 4 * q : 4 * q + 4, :].rearrange("s r t -> r s t").bitcast(I32))
+        nc.sync.dma_start(out=gate_rows[0:4], in_=gate[:, 0, :].rearrange("r (c t) -> c r t", t=P))
         for s in range(PASSES):
             nc.sync.dma_start(out=xw[s][:], in_=x_words[s].rearrange("p t d -> p (t d)").bitcast(I32))
-        load_scales(xs, 0, x_scales.rearrange("s (q r) t -> r q s t", r=4))
-        nc.sync.dma_start(out=gate_rows[0 : TOP * 4], in_=gate[:, 0, :].rearrange("r (c t) -> r c t", t=P))
-        load_scales(qs, 0, wq_scales.rearrange("e s (q r) n -> r q (e s) n", r=4))
-        load_scales(ks, 4, wk_scales.rearrange("e s (q r) n -> r q (e s) n", r=4))
+        q_rows = wq_scales.rearrange("e s (q r) n -> r q (e s) n", r=4)
+        k_rows = wk_scales.rearrange("e s (q r) n -> r q (e s) n", r=4)
+        for r in range(4):
+            nc.sync.dma_start(out=qs[r:P:32].bitcast(I32), in_=q_rows[r].bitcast(I32))
+            nc.sync.dma_start(out=ks[4 + r : P : 32].bitcast(I32), in_=k_rows[r].bitcast(I32))
         load_v(0)
         load_q(0)
         nc.sync.dma_start(out=bias_sb[:], in_=bias.rearrange("(b n) e -> n b e", n=P))
         load_q(1)
         for r, pos in enumerate((pos1, pos2, pos3)):
             nc.sync.dma_start(pos_sb[r][:], pos)
-
-        make_identity(nc, ident[:])
-
-        turns = {"sum": list(range(4)) * 12, "turn": list(range(4, 8)) * 4}
-
-        def bank(kind="sum", which=None):
-            return psum.tile([P, 4, P], F32, name="bank", tag=f"bank{turns[kind].pop(0) if which is None else which}")
-
-
-        acc = bank()
-        nc.tensor.transpose(acc[:, 0, :], gate_rows[:], ident[:])
-        nc.scalar.copy(out=gate_col[:], in_=acc[:, 0, 0 : TOP * 4])
-        for r in range(TOP):
-            acc = bank()
-            for c in range(4):
-                nc.tensor.transpose(acc[:, c, :], gate_col[:, 4 * r + c : 4 * r + c + 1].to_broadcast([P, P]), ident[:])
-            nc.scalar.copy(out=gate_sb[r][:], in_=acc[:].rearrange("p c t -> p (c t)"))
-
         load_k(0)
         load_k(1)
         load_v(1)
@@ -121,6 +103,24 @@ def tile_moe_qkv_kernel(tc, x_words, x_scales, wq_words, wq_scales, wk_words, wk
                 for s in range(PASSES):
                     for e in (pair, pair + 1):
                         load_v_half(e, b, s)
+
+        make_identity(nc, ident[:])
+
+        turns = {"sum": list(range(4)) * 12, "turn": list(range(4, 8)) * 4}
+
+        def bank(kind="sum", which=None):
+            return psum.tile([P, 4, P], F32, name="bank", tag=f"bank{turns[kind].pop(0) if which is None else which}")
+
+
+        acc = bank()
+        for r in range(TOP):
+            nc.tensor.transpose(acc[:, r, :], gate_rows[:, r, :], ident[:])
+        nc.scalar.copy(out=gate_col[:].rearrange("p (r c) -> p r c", c=4), in_=acc[:, 0:TOP, 0:4])
+        for r in range(TOP):
+            acc = bank()
+            for c in range(4):
+                nc.tensor.transpose(acc[:, c, :], gate_col[:, 4 * r + c : 4 * r + c + 1].to_broadcast([P, P]), ident[:])
+            nc.scalar.copy(out=gate_sb[r][:], in_=acc[:].rearrange("p c t -> p (c t)"))
 
         y = {}
 
@@ -173,8 +173,8 @@ def tile_moe_qkv_kernel(tc, x_words, x_scales, wq_words, wq_scales, wk_words, wk
                 round_copy(staged[e][:, s, :], raw[e][:, s, :], engines[s])
 
         def quantise(key, width):
-            codes = ring.tile([P, width], U32, name="codes", tag="codes", bufs=4, align_bytes=64)
-            scales = ring.tile([P, width], U8, name="scales", tag="scales", bufs=4, align_bytes=64)
+            codes = ring.tile([P, width], U32, name="codes", tag="codes", bufs=8, align_bytes=64)
+            scales = ring.tile([P, width], U8, name="scales", tag="scales", bufs=8, align_bytes=64)
             nc.vector.quantize_mx(out=codes[:].bitcast(FP8X4), scales=scales[:], in_=staged[key][:].rearrange("p s w -> p (s w)"))
             vq[key] = (codes, scales)
 
@@ -221,6 +221,16 @@ def tile_moe_qkv_kernel(tc, x_words, x_scales, wq_words, wq_scales, wk_words, wk
             nc.scalar.copy(out=parts[blk][0], in_=acc[:].rearrange("p c t -> p (c t)"))
             nc.sync.dma_start(out=out[blk * P : (blk + 1) * P, :], in_=parts[blk][0])
 
+        def combine_halves(blk):
+            whole = ring.tile([P, TOP, T], F32, name="parts", tag=room[blk], align_bytes=64)
+            for h in range(2):
+                cols, entries = slice(h * T // 2, (h + 1) * T // 2), slice(h * T // 32, (h + 1) * T // 32)
+                for r in range(TOP):
+                    nc.vector.tensor_tensor(whole[:, r, cols], y[blk][:].indirect(pos_sb[r][:, entries]), gate_sb[r][:, cols], MULT)
+                nc.vector.tensor_tensor(whole[:, 0, cols], whole[:, 0, cols], whole[:, 1, cols], ADD)
+                nc.vector.tensor_tensor(whole[:, 1, cols], whole[:, 0, cols], whole[:, 2, cols], ADD)
+                nc.sync.dma_start(out=out[blk * P : (blk + 1) * P, cols], in_=whole[:, 1, cols])
+
         def add_plain(blk):
             nc.vector.tensor_tensor(parts[blk][0], parts[blk][0], parts[blk][1], ADD)
             nc.vector.tensor_tensor(parts[blk][1], parts[blk][0], parts[blk][2], ADD)
@@ -246,16 +256,18 @@ def tile_moe_qkv_kernel(tc, x_words, x_scales, wq_words, wq_scales, wk_words, wk
         quantise(1, PASSES * N)
         y[4] = ring.tile([P, S], F32, name="y4", tag="raw1", align_bytes=64)
         y[5] = ring.tile([P, S], F32, name="y5", tag="raw2", align_bytes=64)
+        for e in range(2, 3):
+            cast(e, "SS")
+            quantise(e, PASSES * N)
         fetch_plain(2)
         fetch_plain(3)
         weigh_turned(2)
         weigh_turned(3)
-        for e in range(2, WHOLE):
+        for e in range(3, WHOLE):
             cast(e, "VV")
             quantise(e, PASSES * N)
-            project_v(e - 2)
-        project_v(WHOLE - 2)
-        project_v(WHOLE - 1)
+        for e in range(WHOLE):
+            project_v(e)
         for b in range(2):
             for pair in range(WHOLE, E, 2):
                 for s in range(PASSES):
@@ -267,6 +279,5 @@ def tile_moe_qkv_kernel(tc, x_words, x_scales, wq_words, wq_scales, wk_words, wk
                     project_pair(pair, b, "V" if b else "S")
             if b == 0:
                 fetch_plain(4)
-        fetch(5)
-        add_plain(5)
+        combine_halves(5)
         weigh_turned(4)

@@ -25,7 +25,7 @@ PASSES = 2
 CHUNK = 3
 CHUNKS = E // CHUNK
 LAST_BANKS = (6, 7)
-WHOLE = 8
+WHOLE = 10
 
 
 def tile_moe_qkv_kernel(tc, x_words, x_scales, wq_words, wq_scales, wk_words, wk_scales, wv, bias, gate, offs, pos1, pos2, pos3, out):
@@ -85,10 +85,10 @@ def tile_moe_qkv_kernel(tc, x_words, x_scales, wq_words, wq_scales, wk_words, wk
         for r in range(4):
             nc.sync.dma_start(out=qs[r:P:32].bitcast(I32), in_=q_rows[r].bitcast(I32))
             nc.sync.dma_start(out=ks[4 + r : P : 32].bitcast(I32), in_=k_rows[r].bitcast(I32))
-        load_v(0)
         load_q(0)
         nc.sync.dma_start(out=bias_sb[:], in_=bias.rearrange("(b n) e -> n b e", n=P))
         load_q(1)
+        load_v(0)
         for r, pos in enumerate((pos1, pos2, pos3)):
             nc.sync.dma_start(pos_sb[r][:], pos)
         load_k(0)
@@ -106,7 +106,7 @@ def tile_moe_qkv_kernel(tc, x_words, x_scales, wq_words, wq_scales, wk_words, wk
 
         make_identity(nc, ident[:])
 
-        turns = {"sum": list(range(4)) * 12, "turn": list(range(4, 8)) * 4}
+        turns = {"sum": list(range(4)) * 12, "turn": [4, 5, 6, 7, 4, 5, 6, 7, 4]}
 
         def bank(kind="sum", which=None):
             return psum.tile([P, 4, P], F32, name="bank", tag=f"bank{turns[kind].pop(0) if which is None else which}")
@@ -151,7 +151,7 @@ def tile_moe_qkv_kernel(tc, x_words, x_scales, wq_words, wq_scales, wk_words, wk
                     nc.scalar.activation(out=y[blk][:, e * C : (e + 1) * C], in_=acc[:, i, :], func=IDENT, bias=bias_sb[:, blk, e : e + 1])
 
         def project_q(e):
-            project(e, (0, 1), lambda s, b: (qw[e // 6][:, (e % 6) * PASSES + s, b * 2 * P : (b + 1) * 2 * P].bitcast(FP4X4), qs[:, e * PASSES + s, b * P : (b + 1) * P]), "V" if e >= 10 else "S")
+            project(e, (0, 1), lambda s, b: (qw[e // 6][:, (e % 6) * PASSES + s, b * 2 * P : (b + 1) * 2 * P].bitcast(FP4X4), qs[:, e * PASSES + s, b * P : (b + 1) * P]), "V" if e >= 9 else "S")
 
         def project_k(e):
             project(e, (2, 3), lambda s, b: (kw[e // 3][:, (e % 3) * PASSES + s, b * P : (b + 1) * P].bitcast(FP8X4), ks[4:P, e * PASSES + s, b * P : (b + 1) * P]))
@@ -172,8 +172,11 @@ def tile_moe_qkv_kernel(tc, x_words, x_scales, wq_words, wq_scales, wk_words, wk
             for s in range(PASSES):
                 round_copy(staged[e][:, s, :], raw[e][:, s, :], engines[s])
 
-        def quantise(key, width):
-            codes = ring.tile([P, width], U32, name="codes", tag="codes", bufs=8, align_bytes=64)
+        def quantise(key, width, over=None):
+            if over is None:
+                codes = ring.tile([P, width], U32, name="codes", tag="codes", bufs=4, align_bytes=64)
+            else:
+                codes = ring.tile([P, width], U32, name="codes", tag=over, align_bytes=64)
             scales = ring.tile([P, width], U8, name="scales", tag="scales", bufs=8, align_bytes=64)
             nc.vector.quantize_mx(out=codes[:].bitcast(FP8X4), scales=scales[:], in_=staged[key][:].rearrange("p s w -> p (s w)"))
             vq[key] = (codes, scales)
@@ -208,12 +211,13 @@ def tile_moe_qkv_kernel(tc, x_words, x_scales, wq_words, wq_scales, wk_words, wk
 
         def weigh_turned(blk):
             scaled = ring.tile([P, 4, TOP, P], F32, name="scaled", tag="scaled", bufs=1)
-            for c in range(4):
-                acc = bank("turn", LAST_BANKS[c % 2] if blk == 4 else None)
-                for r in range(TOP):
-                    nc.tensor.transpose(acc[:, r, :], parts[blk][r][:, c * P : (c + 1) * P], ident[:])
-                for r in range(TOP):
-                    nc.scalar.activation(out=scaled[:, c, r, :], in_=acc[:, r, :], func=COPY, scale=gate_col[:, 4 * r + c : 4 * r + c + 1])
+            for first in range(0, 4 * TOP, 4):
+                acc = bank("turn", LAST_BANKS[first // 4 % 2] if blk == 4 else None)
+                pieces = [divmod(first + i, TOP) for i in range(4)]
+                for i, (c, r) in enumerate(pieces):
+                    nc.tensor.transpose(acc[:, i, :], parts[blk][r][:, c * P : (c + 1) * P], ident[:])
+                for i, (c, r) in enumerate(pieces):
+                    nc.scalar.activation(out=scaled[:, c, r, :], in_=acc[:, i, :], func=COPY, scale=gate_col[:, 4 * r + c : 4 * r + c + 1])
             acc = bank("turn")
             for c in range(4):
                 for r in range(TOP):
@@ -238,13 +242,13 @@ def tile_moe_qkv_kernel(tc, x_words, x_scales, wq_words, wq_scales, wk_words, wk
 
         for blk in range(4):
             y[blk] = ring.tile([P, S], F32, name=f"y{blk}", align_bytes=64)
-        cast(0, "SS")
         for c in range(CHUNKS):
             gather_words(c)
             for e in range(c * CHUNK, (c + 1) * CHUNK):
                 project_q(e)
-        quantise(0, PASSES * N)
+        cast(0, "SS")
         fetch(0)
+        quantise(0, PASSES * N)
         fetch(1)
         add_plain(0)
         add_plain(1)
@@ -263,21 +267,26 @@ def tile_moe_qkv_kernel(tc, x_words, x_scales, wq_words, wq_scales, wk_words, wk
         fetch_plain(3)
         weigh_turned(2)
         weigh_turned(3)
-        for e in range(3, WHOLE):
-            cast(e, "VV")
-            quantise(e, PASSES * N)
+        groups = [(pair, b, s) for b in range(2) for pair in range(WHOLE, E, 2) for s in range(PASSES)]
+        cast(3, "VV")
+        for e in range(3, WHOLE - 1):
+            cast(e + 1, "VV")
+            quantise(e, PASSES * N, f"raw{e + 1}")
+        cast_pair(*groups[0])
+        quantise(WHOLE - 1, PASSES * N, f"raw{WHOLE}_0_0")
         for e in range(WHOLE):
             project_v(e)
-        for b in range(2):
-            for pair in range(WHOLE, E, 2):
-                for s in range(PASSES):
-                    cast_pair(pair, b, s)
-                    quantise((pair, b, s), 2 * P)
-                if (b, pair) == (1, E - 2):
-                    project_pair(pair, b, "V", LAST_BANKS)
-                else:
-                    project_pair(pair, b, "V" if b else "S")
-            if b == 0:
-                fetch_plain(4)
+        for i, (pair, b, s) in enumerate(groups):
+            ahead = groups[i + 1] if i + 1 < len(groups) else None
+            hold = ahead is not None and (pair, s) != (E - 2, 1)
+            if hold:
+                cast_pair(*ahead)
+            quantise((pair, b, s), 2 * P, f"raw{ahead[0]}_{ahead[1]}_{ahead[2]}" if hold else None)
+            if ahead is not None and not hold:
+                cast_pair(*ahead)
+            if s == 1:
+                project_pair(pair, b, "V" if b else "S", LAST_BANKS if ahead is None else (None, None))
+                if (pair, b) == (E - 2, 0):
+                    fetch_plain(4)
         combine_halves(5)
         weigh_turned(4)

@@ -21,11 +21,25 @@ IDENT = mybir.ActivationFunctionType.Identity
 COPY = mybir.ActivationFunctionType.Copy
 
 P = 128
-PASSES = 2
+PACK = 4
+QUADRANT = 32
+PASS_ROWS = P * PACK
+PASSES = K // PASS_ROWS
+BLOCKS = 3 * N // P
+TOKEN_PIECES = T // P
+OFFSETS_A_COLUMN = 16
+ALIGN = 64
+K_PLANE = 4
 CHUNK = 3
-CHUNKS = E // CHUNK
+Q_LOAD = 6
+WALK = 2
+WHOLE = E - 2
+Q_ON_VECTOR = E - CHUNK
+ROUND_ON_SCALAR = 3
+SUM_BANKS = (0, 1, 2, 3)
+TURN_BANKS = (4, 5, 6, 7)
 LAST_BANKS = (6, 7)
-WHOLE = 10
+STAGED_BUFS, CODE_BUFS, SCALE_BUFS = 3, 4, 10
 
 
 def tile_moe_qkv_kernel(tc, x_words, x_scales, wq_words, wq_scales, wk_words, wk_scales, wv, bias, gate, offs, pos1, pos2, pos3, out):
@@ -35,60 +49,61 @@ def tile_moe_qkv_kernel(tc, x_words, x_scales, wq_words, wq_scales, wk_words, wk
         ring = ctx.enter_context(tc.tile_pool(name="ring", bufs=1))
         psum = ctx.enter_context(tc.psum_pool(name="psum", bufs=1))
 
-        offs_sb = keep.tile([P, S // 16], U16, name="offs_sb")
-        pos_sb = [keep.tile([P, T // 16], U16, name=f"pos_sb{r}") for r in range(TOP)]
-        xw = [keep.tile([P, T], I32, name=f"xw{s}", align_bytes=64) for s in range(PASSES)]
-        xs = keep.tile([P, PASSES, T], U8, name="xs", align_bytes=64)
-        qs = keep.tile([P, E * PASSES, N], U8, name="qs", align_bytes=64)
-        qw = [ring.tile([P, 6 * PASSES, 2 * N], U8, name=f"qw{i}", align_bytes=64) for i in range(2)]
-        kw = [ring.tile([P, 3 * PASSES, N], I32, name=f"kw{i}", align_bytes=64) for i in range(4)]
-        ks = keep.tile([P, E * PASSES, N], U8, name="ks", align_bytes=64)
-        bias_sb = keep.tile([P, 6, E], F32, name="bias_sb")
+        offs_sb = keep.tile([P, S // OFFSETS_A_COLUMN], U16, name="offs_sb")
+        pos_sb = [keep.tile([P, T // OFFSETS_A_COLUMN], U16, name=f"pos_sb{r}") for r in range(TOP)]
+        xw = [keep.tile([P, T], I32, name=f"xw{s}", align_bytes=ALIGN) for s in range(PASSES)]
+        xs = keep.tile([P, PASSES, T], U8, name="xs", align_bytes=ALIGN)
+        qs = keep.tile([P, E * PASSES, N], U8, name="qs", align_bytes=ALIGN)
+        qw = [ring.tile([P, Q_LOAD * PASSES, 2 * N], U8, name=f"qw{i}", align_bytes=ALIGN) for i in range(E // Q_LOAD)]
+        kw = [ring.tile([P, CHUNK * PASSES, N], I32, name=f"kw{i}", align_bytes=ALIGN) for i in range(E // CHUNK)]
+        ks = keep.tile([P, E * PASSES, N], U8, name="ks", align_bytes=ALIGN)
+        bias_sb = keep.tile([P, BLOCKS, E], F32, name="bias_sb")
         gate_rows = keep.tile([P, TOP, P], F32, name="gate_rows")
-        gate_col = keep.tile([P, TOP * 4], F32, name="gate_col")
+        gate_col = keep.tile([P, TOP * TOKEN_PIECES], F32, name="gate_col")
         gate_sb = [keep.tile([P, T], F32, name=f"gate_sb{r}") for r in range(TOP)]
         ident = keep.tile([P, P], F32, name="ident")
-        gw = [[keep.tile([P, CHUNK * C], U32, name=f"gw{s}_{c}", align_bytes=64) for c in range(CHUNKS)] for s in range(PASSES)]
-        gs = [keep.tile([P, S], U8, name=f"gs{s}", align_bytes=64) for s in range(PASSES)]
-        raw = {}
+        gw = [[keep.tile([P, CHUNK * C], U32, name=f"gw{s}_{c}", align_bytes=ALIGN) for c in range(E // CHUNK)] for s in range(PASSES)]
+        gs = [keep.tile([P, S], U8, name=f"gs{s}", align_bytes=ALIGN) for s in range(PASSES)]
+        raw, staged, quantised, y, parts = {}, {}, {}, {}, {}
 
         nc.gpsimd.memset(xs[:].rearrange("p s t -> p (s t)").bitcast(I32), 0)
         nc.gpsimd.memset(gate_rows[:].rearrange("c r t -> c (r t)"), 0.0)
         nc.vector.memset(qs[:].rearrange("p s t -> p (s t)").bitcast(I32), 0)
         nc.vector.memset(ks[:].rearrange("p s t -> p (s t)").bitcast(I32), 0)
 
-        def chunk_offsets(c):
-            return offs_sb[:, c * CHUNK * C // 16 : (c + 1) * CHUNK * C // 16]
-
         def load_v(e):
-            raw[e] = ring.tile([P, PASSES, 4 * N], F32, name="raw", tag=f"raw{e}", align_bytes=64)
-            nc.sync.dma_start(out=raw[e][:], in_=wv[e].rearrange("(s p j) n -> p s (j n)", s=PASSES, j=4))
+            raw[e] = ring.tile([P, PASSES, PACK * N], F32, name="raw", tag=f"raw{e}", align_bytes=ALIGN)
+            nc.sync.dma_start(out=raw[e][:], in_=wv[e].rearrange("(s p j) n -> p s (j n)", s=PASSES, j=PACK))
 
         def load_v_half(e, b, s):
-            raw[e, b, s] = ring.tile([P, 4, P], F32, name="rawh", tag=f"raw{e}_{b}_{s}", align_bytes=64)
-            nc.sync.dma_start(out=raw[e, b, s][:], in_=wv[e, 512 * s : 512 * (s + 1), b * P : (b + 1) * P].rearrange("(p j) n -> p j n", j=4))
+            raw[e, b, s] = ring.tile([P, PACK, P], F32, name="rawh", tag=f"raw{e}_{b}_{s}", align_bytes=ALIGN)
+            rows = wv[e, PASS_ROWS * s : PASS_ROWS * (s + 1), b * P : (b + 1) * P]
+            nc.sync.dma_start(out=raw[e, b, s][:], in_=rows.rearrange("(p j) n -> p j n", j=PACK))
 
         def load_q(i):
-            nc.sync.dma_start(out=qw[i][:].bitcast(I32), in_=wq_words[6 * i : 6 * i + 6].rearrange("e s p w -> p (e s) w").bitcast(I32))
+            words = wq_words[Q_LOAD * i : Q_LOAD * (i + 1)].rearrange("e s p w -> p (e s) w")
+            nc.sync.dma_start(out=qw[i][:].bitcast(I32), in_=words.bitcast(I32))
 
         def load_k(i):
-            nc.sync.dma_start(out=kw[i][:], in_=wk_words[3 * i : 3 * i + 3].rearrange("e s p n d -> p (e s) (n d)").bitcast(I32))
+            words = wk_words[CHUNK * i : CHUNK * (i + 1)].rearrange("e s p n d -> p (e s) (n d)")
+            nc.sync.dma_start(out=kw[i][:], in_=words.bitcast(I32))
 
         nc.sync.dma_start(offs_sb[:], offs)
-        for q in range(4):
-            nc.sync.dma_start(out=xs[32 * q : 32 * q + 4].bitcast(I32), in_=x_scales[:, 4 * q : 4 * q + 4, :].rearrange("s r t -> r s t").bitcast(I32))
-        nc.sync.dma_start(out=gate_rows[0:4], in_=gate[:, 0, :].rearrange("r (c t) -> c r t", t=P))
+        for q in range(P // QUADRANT):
+            rows = x_scales[:, PACK * q : PACK * (q + 1), :].rearrange("s r t -> r s t")
+            nc.sync.dma_start(out=xs[QUADRANT * q : QUADRANT * q + PACK].bitcast(I32), in_=rows.bitcast(I32))
+        nc.sync.dma_start(out=gate_rows[0:TOKEN_PIECES], in_=gate[:, 0, :].rearrange("r (c t) -> c r t", t=P))
         for s in range(PASSES):
             nc.sync.dma_start(out=xw[s][:], in_=x_words[s].rearrange("p t d -> p (t d)").bitcast(I32))
-        q_rows = wq_scales.rearrange("e s (q r) n -> r q (e s) n", r=4)
-        k_rows = wk_scales.rearrange("e s (q r) n -> r q (e s) n", r=4)
-        for r in range(4):
-            nc.sync.dma_start(out=qs[r:P:32].bitcast(I32), in_=q_rows[r].bitcast(I32))
-            nc.sync.dma_start(out=ks[4 + r : P : 32].bitcast(I32), in_=k_rows[r].bitcast(I32))
+        q_rows = wq_scales.rearrange("e s (q r) n -> r q (e s) n", r=PACK)
+        k_rows = wk_scales.rearrange("e s (q r) n -> r q (e s) n", r=PACK)
+        for r in range(PACK):
+            nc.sync.dma_start(out=qs[r:P:QUADRANT].bitcast(I32), in_=q_rows[r].bitcast(I32))
+            nc.sync.dma_start(out=ks[K_PLANE + r : P : QUADRANT].bitcast(I32), in_=k_rows[r].bitcast(I32))
+        load_v(0)
         load_q(0)
         nc.sync.dma_start(out=bias_sb[:], in_=bias.rearrange("(b n) e -> n b e", n=P))
         load_q(1)
-        load_v(0)
         for r, pos in enumerate((pos1, pos2, pos3)):
             nc.sync.dma_start(pos_sb[r][:], pos)
         load_k(0)
@@ -98,195 +113,216 @@ def tile_moe_qkv_kernel(tc, x_words, x_scales, wq_words, wq_scales, wk_words, wk
         load_k(3)
         for e in range(2, WHOLE):
             load_v(e)
-        for b in range(2):
-            for pair in range(WHOLE, E, 2):
-                for s in range(PASSES):
-                    for e in (pair, pair + 1):
-                        load_v_half(e, b, s)
+        halves = [(b, s) for b in range(2) for s in range(PASSES)]
+        for b, s in halves:
+            for e in range(WHOLE, E):
+                load_v_half(e, b, s)
 
         make_identity(nc, ident[:])
 
-        turns = {"sum": list(range(4)) * 12, "turn": [4, 5, 6, 7, 4, 5, 6, 7, 4]}
+        taken = {SUM_BANKS: 0, TURN_BANKS: 0}
 
-        def bank(kind="sum", which=None):
-            return psum.tile([P, 4, P], F32, name="bank", tag=f"bank{turns[kind].pop(0) if which is None else which}")
-
+        def bank(group=SUM_BANKS, which=None):
+            if which is None:
+                which = group[taken[group] % len(group)]
+                taken[group] = taken[group] + 1
+            return psum.tile([P, PACK, P], F32, name="bank", tag=f"bank{which}")
 
         acc = bank()
         for r in range(TOP):
             nc.tensor.transpose(acc[:, r, :], gate_rows[:, r, :], ident[:])
-        nc.scalar.copy(out=gate_col[:].rearrange("p (r c) -> p r c", c=4), in_=acc[:, 0:TOP, 0:4])
+        nc.scalar.copy(out=gate_col[:].rearrange("p (r c) -> p r c", c=TOKEN_PIECES), in_=acc[:, 0:TOP, 0:TOKEN_PIECES])
+
+        def gate_column(r, c):
+            return gate_col[:, TOKEN_PIECES * r + c : TOKEN_PIECES * r + c + 1]
+
         for r in range(TOP):
             acc = bank()
-            for c in range(4):
-                nc.tensor.transpose(acc[:, c, :], gate_col[:, 4 * r + c : 4 * r + c + 1].to_broadcast([P, P]), ident[:])
+            for c in range(TOKEN_PIECES):
+                nc.tensor.transpose(acc[:, c, :], gate_column(r, c).to_broadcast([P, P]), ident[:])
             nc.scalar.copy(out=gate_sb[r][:], in_=acc[:].rearrange("p c t -> p (c t)"))
 
-        y = {}
-
-        def gather_words(c):
+        def gather_tokens(c):
+            width = CHUNK * C
+            entries = offs_sb[:, c * width // OFFSETS_A_COLUMN : (c + 1) * width // OFFSETS_A_COLUMN]
             for s in range(PASSES):
-                nc.vector.tensor_copy(gw[s][c][:], xw[s][:].bitcast(U32).indirect(chunk_offsets(c)))
-                nc.vector.tensor_copy(gs[s][:, c * CHUNK * C : (c + 1) * CHUNK * C], xs[:, s, :].indirect(chunk_offsets(c)))
+                nc.vector.tensor_copy(gw[s][c][:], xw[s][:].bitcast(U32).indirect(entries))
+                nc.vector.tensor_copy(gs[s][:, c * width : (c + 1) * width], xs[:, s, :].indirect(entries))
 
-        def project(e, blks, lhs, engine="S", which=None):
-            acc = bank("sum", which)
+        def project(e, blks, weights, on_vector=False, which=None):
+            acc = bank(SUM_BANKS, which)
             c, u = divmod(e, CHUNK)
+            slots = slice(e * C, (e + 1) * C)
             for i, blk in enumerate(blks):
                 for s in range(PASSES):
-                    words, scales = lhs(s, blk % 2)
+                    words, scales = weights(s, blk % 2)
                     nc.tensor.matmul_mx(
                         out=acc[:, i, :],
                         lhsT=words,
                         lhsT_scale=scales,
                         rhs=gw[s][c][:, u * C : (u + 1) * C].bitcast(FP8X4),
-                        rhs_scale=gs[s][:, e * C : (e + 1) * C],
+                        rhs_scale=gs[s][:, slots],
                         start=(s == 0),
                         stop=(s == PASSES - 1),
                     )
             for i, blk in enumerate(blks):
-                if engine == "V":
-                    nc.vector.tensor_scalar_add(out=y[blk][:, e * C : (e + 1) * C], in0=acc[:, i, :], scalar1=bias_sb[:, blk, e : e + 1])
+                if on_vector:
+                    nc.vector.tensor_scalar_add(out=y[blk][:, slots], in0=acc[:, i, :], scalar1=bias_sb[:, blk, e : e + 1])
                 else:
-                    nc.scalar.activation(out=y[blk][:, e * C : (e + 1) * C], in_=acc[:, i, :], func=IDENT, bias=bias_sb[:, blk, e : e + 1])
+                    nc.scalar.activation(out=y[blk][:, slots], in_=acc[:, i, :], func=IDENT, bias=bias_sb[:, blk, e : e + 1])
 
         def project_q(e):
-            project(e, (0, 1), lambda s, b: (qw[e // 6][:, (e % 6) * PASSES + s, b * 2 * P : (b + 1) * 2 * P].bitcast(FP4X4), qs[:, e * PASSES + s, b * P : (b + 1) * P]), "V" if e >= 9 else "S")
+            def weights(s, b):
+                words = qw[e // Q_LOAD][:, (e % Q_LOAD) * PASSES + s, b * 2 * P : (b + 1) * 2 * P]
+                return words.bitcast(FP4X4), qs[:, e * PASSES + s, b * P : (b + 1) * P]
+
+            project(e, (0, 1), weights, e >= Q_ON_VECTOR)
 
         def project_k(e):
-            project(e, (2, 3), lambda s, b: (kw[e // 3][:, (e % 3) * PASSES + s, b * P : (b + 1) * P].bitcast(FP8X4), ks[4:P, e * PASSES + s, b * P : (b + 1) * P]))
+            def weights(s, b):
+                words = kw[e // CHUNK][:, (e % CHUNK) * PASSES + s, b * P : (b + 1) * P]
+                return words.bitcast(FP8X4), ks[K_PLANE:P, e * PASSES + s, b * P : (b + 1) * P]
 
-        vq = {}
-        staged = {}
+            project(e, (2, 3), weights)
 
-        def round_copy(dst, src, engine):
-            dst = dst.rearrange("p (c i j) -> p c j i", i=2, j=4)
-            src = src.rearrange("p (j c i) -> p c j i", i=2, j=4)
-            if engine == "V":
+        def project_v(e):
+            def weights(s, b):
+                codes, scales = quantised[e]
+                cols = slice(s * N + b * P, s * N + (b + 1) * P)
+                return codes[:, cols].bitcast(FP8X4), scales[:, cols]
+
+            project(e, (4, 5), weights, which=SUM_BANKS[-1 - e % len(SUM_BANKS)])
+
+        def project_v_half(e, b):
+            def weights(s, half):
+                codes, scales = quantised[half, s]
+                cols = slice((e - WHOLE) * P, (e - WHOLE + 1) * P)
+                return codes[:, cols].bitcast(FP8X4), scales[:, cols]
+
+            project(e, (4 + b,), weights, b == 1, LAST_BANKS[e - WHOLE] if b == 1 else None)
+
+        def round_copy(dst, src, on_vector):
+            dst = dst.rearrange("p (c i j) -> p c j i", i=WALK, j=PACK)
+            src = src.rearrange("p (j c i) -> p c j i", i=WALK, j=PACK)
+            if on_vector:
                 nc.vector.tensor_copy(out=dst, in_=src)
             else:
                 nc.scalar.copy(out=dst, in_=src)
 
-        def cast(e, engines):
-            staged[e] = ring.tile([P, PASSES, 4 * N], BF16, name="staged", tag="staged", bufs=3, align_bytes=64)
+        def round_expert(e):
+            staged[e] = ring.tile([P, PASSES, PACK * N], BF16, name="staged", tag="staged", bufs=STAGED_BUFS, align_bytes=ALIGN)
             for s in range(PASSES):
-                round_copy(staged[e][:, s, :], raw[e][:, s, :], engines[s])
+                round_copy(staged[e][:, s, :], raw[e][:, s, :], e >= ROUND_ON_SCALAR)
+
+        def round_half(b, s):
+            staged[b, s] = ring.tile([P, E - WHOLE, PACK * P], BF16, name="staged", tag="staged", bufs=STAGED_BUFS, align_bytes=ALIGN)
+            for e in range(WHOLE, E):
+                round_copy(staged[b, s][:, e - WHOLE, :], raw[e, b, s][:].rearrange("p j n -> p (j n)"), True)
 
         def quantise(key, width, over=None):
             if over is None:
-                codes = ring.tile([P, width], U32, name="codes", tag="codes", bufs=4, align_bytes=64)
+                codes = ring.tile([P, width], U32, name="codes", tag="codes", bufs=CODE_BUFS, align_bytes=ALIGN)
             else:
-                codes = ring.tile([P, width], U32, name="codes", tag=over, align_bytes=64)
-            scales = ring.tile([P, width], U8, name="scales", tag="scales", bufs=8, align_bytes=64)
+                codes = ring.tile([P, width], U32, name="codes", tag=over, align_bytes=ALIGN)
+            scales = ring.tile([P, width], U8, name="scales", tag="scales", bufs=SCALE_BUFS, align_bytes=ALIGN)
             nc.vector.quantize_mx(out=codes[:].bitcast(FP8X4), scales=scales[:], in_=staged[key][:].rearrange("p s w -> p (s w)"))
-            vq[key] = (codes, scales)
+            quantised[key] = (codes, scales)
 
-        def project_v(e):
-            codes, scales = vq[e]
-            project(e, (4, 5), lambda s, b: (codes[:, s * N + b * P : s * N + (b + 1) * P].bitcast(FP8X4), scales[:, s * N + b * P : s * N + (b + 1) * P]))
+        room = ("raw0", "qw0", "qw1", "kw2", "kw1", "kw0")
 
-        def cast_pair(pair, b, s):
-            staged[pair, b, s] = ring.tile([P, 2, 4 * P], BF16, name="staged", tag="staged", bufs=3, align_bytes=64)
-            for i in range(2):
-                round_copy(staged[pair, b, s][:, i, :], raw[pair + i, b, s][:].rearrange("p j n -> p (j n)"), "V")
+        def new_parts(blk):
+            parts[blk] = ring.tile([P, TOP, T], F32, name="parts", tag=room[blk], align_bytes=ALIGN)
 
-        def project_pair(pair, b, engine, banks=(None, None)):
-            for i in range(2):
-                project(pair + i, (4 + b,), lambda s, unused: (vq[pair, b, s][0][:, i * P : (i + 1) * P].bitcast(FP8X4), vq[pair, b, s][1][:, i * P : (i + 1) * P]), engine, banks[i])
+        def token_cut(h, cuts):
+            width = T // cuts
+            return slice(h * width, (h + 1) * width), slice(h * width // OFFSETS_A_COLUMN, (h + 1) * width // OFFSETS_A_COLUMN)
 
-        parts = {}
-        room = {0: "raw0", 1: "qw0", 2: "qw1", 3: "kw2", 4: "kw1", 5: "kw0"}
-
-        def fetch(blk):
-            whole = ring.tile([P, TOP, T], F32, name="parts", tag=room[blk], align_bytes=64)
-            parts[blk] = [whole[:, r, :] for r in range(TOP)]
+        def fetch_weighed(blk, cols, entries):
             for r in range(TOP):
-                nc.vector.tensor_tensor(parts[blk][r], y[blk][:].indirect(pos_sb[r][:]), gate_sb[r][:], MULT)
+                nc.vector.tensor_tensor(parts[blk][:, r, cols], y[blk][:].indirect(pos_sb[r][:, entries]), gate_sb[r][:, cols], MULT)
 
-        def fetch_plain(blk):
-            whole = ring.tile([P, TOP, T], F32, name="parts", tag=room[blk], align_bytes=64)
-            parts[blk] = [whole[:, r, :] for r in range(TOP)]
-            for r in range(TOP):
-                nc.scalar.activation(out=parts[blk][r], in_=y[blk][:].indirect(pos_sb[r][:]), func=COPY)
+        def add_and_store(blk, cols):
+            nc.vector.tensor_tensor(parts[blk][:, 0, cols], parts[blk][:, 0, cols], parts[blk][:, 1, cols], ADD)
+            nc.vector.tensor_tensor(parts[blk][:, 1, cols], parts[blk][:, 0, cols], parts[blk][:, 2, cols], ADD)
+            nc.sync.dma_start(out=out[blk * P : (blk + 1) * P, cols], in_=parts[blk][:, 1, cols])
 
-        def weigh_turned(blk):
-            scaled = ring.tile([P, 4, TOP, P], F32, name="scaled", tag="scaled", bufs=1)
-            for first in range(0, 4 * TOP, 4):
-                acc = bank("turn", LAST_BANKS[first // 4 % 2] if blk == 4 else None)
-                pieces = [divmod(first + i, TOP) for i in range(4)]
+        def fetch_plain(blk, cuts):
+            new_parts(blk)
+            for h in range(cuts):
+                cols, entries = token_cut(h, cuts)
+                for r in range(TOP):
+                    nc.scalar.activation(out=parts[blk][:, r, cols], in_=y[blk][:].indirect(pos_sb[r][:, entries]), func=COPY)
+
+        def weigh_turned(blk, banks=None):
+            scaled = ring.tile([P, TOKEN_PIECES, TOP, P], F32, name="scaled", tag="scaled", bufs=1)
+            for group in range(TOP):
+                acc = bank(TURN_BANKS, banks[group % 2] if banks else None)
+                pieces = [divmod(PACK * group + i, TOP) for i in range(PACK)]
                 for i, (c, r) in enumerate(pieces):
-                    nc.tensor.transpose(acc[:, i, :], parts[blk][r][:, c * P : (c + 1) * P], ident[:])
+                    nc.tensor.transpose(acc[:, i, :], parts[blk][:, r, c * P : (c + 1) * P], ident[:])
                 for i, (c, r) in enumerate(pieces):
-                    nc.scalar.activation(out=scaled[:, c, r, :], in_=acc[:, i, :], func=COPY, scale=gate_col[:, 4 * r + c : 4 * r + c + 1])
-            acc = bank("turn")
-            for c in range(4):
+                    nc.scalar.activation(out=scaled[:, c, r, :], in_=acc[:, i, :], func=COPY, scale=gate_column(r, c))
+            acc = bank(TURN_BANKS)
+            for c in range(TOKEN_PIECES):
                 for r in range(TOP):
                     nc.tensor.matmul(acc[:, c, :], scaled[:, c, r, :], ident[:], start=(r == 0), stop=(r == TOP - 1), is_transpose=True)
-            nc.scalar.copy(out=parts[blk][0], in_=acc[:].rearrange("p c t -> p (c t)"))
-            nc.sync.dma_start(out=out[blk * P : (blk + 1) * P, :], in_=parts[blk][0])
+            nc.scalar.copy(out=parts[blk][:, 0, :], in_=acc[:].rearrange("p c t -> p (c t)"))
+            nc.sync.dma_start(out=out[blk * P : (blk + 1) * P, :], in_=parts[blk][:, 0, :])
 
-        def combine_halves(blk):
-            whole = ring.tile([P, TOP, T], F32, name="parts", tag=room[blk], align_bytes=64)
-            for h in range(2):
-                cols, entries = slice(h * T // 2, (h + 1) * T // 2), slice(h * T // 32, (h + 1) * T // 32)
-                for r in range(TOP):
-                    nc.vector.tensor_tensor(whole[:, r, cols], y[blk][:].indirect(pos_sb[r][:, entries]), gate_sb[r][:, cols], MULT)
-                nc.vector.tensor_tensor(whole[:, 0, cols], whole[:, 0, cols], whole[:, 1, cols], ADD)
-                nc.vector.tensor_tensor(whole[:, 1, cols], whole[:, 0, cols], whole[:, 2, cols], ADD)
-                nc.sync.dma_start(out=out[blk * P : (blk + 1) * P, cols], in_=whole[:, 1, cols])
-
-        def add_plain(blk):
-            nc.vector.tensor_tensor(parts[blk][0], parts[blk][0], parts[blk][1], ADD)
-            nc.vector.tensor_tensor(parts[blk][1], parts[blk][0], parts[blk][2], ADD)
-            nc.sync.dma_start(out=out[blk * P : (blk + 1) * P, :], in_=parts[blk][1])
-
+        all_cols, all_entries = token_cut(0, 1)
+        whole_width, half_width = PASSES * N, (E - WHOLE) * P
         for blk in range(4):
-            y[blk] = ring.tile([P, S], F32, name=f"y{blk}", align_bytes=64)
-        for c in range(CHUNKS):
-            gather_words(c)
+            y[blk] = ring.tile([P, S], F32, name=f"y{blk}", align_bytes=ALIGN)
+        for c in range(E // CHUNK):
+            gather_tokens(c)
             for e in range(c * CHUNK, (c + 1) * CHUNK):
                 project_q(e)
-        cast(0, "SS")
-        fetch(0)
-        quantise(0, PASSES * N)
-        fetch(1)
-        add_plain(0)
-        add_plain(1)
-        for e in range(0, 6):
+        round_expert(0)
+        new_parts(0)
+        fetch_weighed(0, all_cols, all_entries)
+        quantise(0, whole_width)
+        new_parts(1)
+        fetch_weighed(1, all_cols, all_entries)
+        add_and_store(0, all_cols)
+        add_and_store(1, all_cols)
+
+        for e in range(E // 2):
             project_k(e)
-        cast(1, "SS")
-        for e in range(6, 12):
+        round_expert(1)
+        for e in range(E // 2, E):
             project_k(e)
-        quantise(1, PASSES * N)
-        y[4] = ring.tile([P, S], F32, name="y4", tag="raw1", align_bytes=64)
-        y[5] = ring.tile([P, S], F32, name="y5", tag="raw2", align_bytes=64)
-        for e in range(2, 3):
-            cast(e, "SS")
-            quantise(e, PASSES * N)
-        fetch_plain(2)
-        fetch_plain(3)
+        quantise(1, whole_width)
+        y[4] = ring.tile([P, S], F32, name="y4", tag="raw1", align_bytes=ALIGN)
+        y[5] = ring.tile([P, S], F32, name="y5", tag="raw2", align_bytes=ALIGN)
+        round_expert(2)
+        quantise(2, whole_width)
+        fetch_plain(2, 1)
+        fetch_plain(3, 1)
         weigh_turned(2)
         weigh_turned(3)
-        groups = [(pair, b, s) for b in range(2) for pair in range(WHOLE, E, 2) for s in range(PASSES)]
-        cast(3, "VV")
-        for e in range(3, WHOLE - 1):
-            cast(e + 1, "VV")
-            quantise(e, PASSES * N, f"raw{e + 1}")
-        cast_pair(*groups[0])
-        quantise(WHOLE - 1, PASSES * N, f"raw{WHOLE}_0_0")
+
+        round_expert(ROUND_ON_SCALAR)
+        for e in range(ROUND_ON_SCALAR, WHOLE - 1):
+            round_expert(e + 1)
+            quantise(e, whole_width, f"raw{e + 1}")
+        round_half(0, 0)
+        quantise(WHOLE - 1, whole_width, f"raw{WHOLE}_0_0")
         for e in range(WHOLE):
             project_v(e)
-        for i, (pair, b, s) in enumerate(groups):
-            ahead = groups[i + 1] if i + 1 < len(groups) else None
-            hold = ahead is not None and (pair, s) != (E - 2, 1)
-            if hold:
-                cast_pair(*ahead)
-            quantise((pair, b, s), 2 * P, f"raw{ahead[0]}_{ahead[1]}_{ahead[2]}" if hold else None)
-            if ahead is not None and not hold:
-                cast_pair(*ahead)
-            if s == 1:
-                project_pair(pair, b, "V" if b else "S", LAST_BANKS if ahead is None else (None, None))
-                if (pair, b) == (E - 2, 0):
-                    fetch_plain(4)
-        combine_halves(5)
-        weigh_turned(4)
+        for b in range(2):
+            round_half(b, 1)
+            quantise((b, 0), half_width, f"raw{WHOLE}_{b}_1")
+            quantise((b, 1), half_width)
+            if b == 0:
+                round_half(1, 0)
+            for e in range(WHOLE, E):
+                project_v_half(e, b)
+            if b == 0:
+                fetch_plain(4, 2)
+
+        new_parts(5)
+        for h in range(2):
+            cols, entries = token_cut(h, 2)
+            fetch_weighed(5, cols, entries)
+            add_and_store(5, cols)
+        weigh_turned(4, LAST_BANKS)

@@ -32,14 +32,9 @@ ALIGN = 64
 K_PLANE = 4
 CHUNK = 3
 Q_LOAD = 6
-WALK = 2
-WHOLE = E - 2
-Q_ON_VECTOR = E - CHUNK
-ROUND_ON_SCALAR = 3
-SUM_BANKS = (0, 1, 2, 3)
-TURN_BANKS = (4, 5, 6, 7)
-LAST_BANKS = (6, 7)
-STAGED_BUFS, CODE_BUFS, SCALE_BUFS = 3, 4, 10
+WALK = 4
+WHOLE = E - 1
+CODE_BUFS = 16
 
 
 def tile_moe_qkv_kernel(tc, x_words, x_scales, wq_words, wq_scales, wk_words, wk_scales, wv, bias, gate, offs, pos1, pos2, pos3, out):
@@ -53,10 +48,9 @@ def tile_moe_qkv_kernel(tc, x_words, x_scales, wq_words, wq_scales, wk_words, wk
         pos_sb = [keep.tile([P, T // OFFSETS_A_COLUMN], U16, name=f"pos_sb{r}") for r in range(TOP)]
         xw = [keep.tile([P, T], I32, name=f"xw{s}", align_bytes=ALIGN) for s in range(PASSES)]
         xs = keep.tile([P, PASSES, T], U8, name="xs", align_bytes=ALIGN)
-        qs = keep.tile([P, E * PASSES, N], U8, name="qs", align_bytes=ALIGN)
+        ws = keep.tile([P, E * PASSES, N], U8, name="ws", align_bytes=ALIGN)
         qw = [ring.tile([P, Q_LOAD * PASSES, 2 * N], U8, name=f"qw{i}", align_bytes=ALIGN) for i in range(E // Q_LOAD)]
         kw = [ring.tile([P, CHUNK * PASSES, N], I32, name=f"kw{i}", align_bytes=ALIGN) for i in range(E // CHUNK)]
-        ks = keep.tile([P, E * PASSES, N], U8, name="ks", align_bytes=ALIGN)
         bias_sb = keep.tile([P, BLOCKS, E], F32, name="bias_sb")
         gate_rows = keep.tile([P, TOP, P], F32, name="gate_rows")
         gate_col = keep.tile([P, TOP * TOKEN_PIECES], F32, name="gate_col")
@@ -64,21 +58,21 @@ def tile_moe_qkv_kernel(tc, x_words, x_scales, wq_words, wq_scales, wk_words, wk
         ident = keep.tile([P, P], F32, name="ident")
         gw = [[keep.tile([P, CHUNK * C], U32, name=f"gw{s}_{c}", align_bytes=ALIGN) for c in range(E // CHUNK)] for s in range(PASSES)]
         gs = [keep.tile([P, S], U8, name=f"gs{s}", align_bytes=ALIGN) for s in range(PASSES)]
-        raw, staged, quantised, y, parts = {}, {}, {}, {}, {}
+        raw, staged, quantised, y = {}, {}, {}, {}
 
+        nc.vector.memset(ws[:].rearrange("p s t -> p (s t)").bitcast(I32), 0)
         nc.gpsimd.memset(xs[:].rearrange("p s t -> p (s t)").bitcast(I32), 0)
         nc.gpsimd.memset(gate_rows[:].rearrange("c r t -> c (r t)"), 0.0)
-        nc.vector.memset(qs[:].rearrange("p s t -> p (s t)").bitcast(I32), 0)
-        nc.vector.memset(ks[:].rearrange("p s t -> p (s t)").bitcast(I32), 0)
+        make_identity(nc, ident[:])
 
         def load_v(e):
             raw[e] = ring.tile([P, PASSES, PACK * N], F32, name="raw", tag=f"raw{e}", align_bytes=ALIGN)
             nc.sync.dma_start(out=raw[e][:], in_=wv[e].rearrange("(s p j) n -> p s (j n)", s=PASSES, j=PACK))
 
-        def load_v_half(e, b, s):
-            raw[e, b, s] = ring.tile([P, PACK, P], F32, name="rawh", tag=f"raw{e}_{b}_{s}", align_bytes=ALIGN)
-            rows = wv[e, PASS_ROWS * s : PASS_ROWS * (s + 1), b * P : (b + 1) * P]
-            nc.sync.dma_start(out=raw[e, b, s][:], in_=rows.rearrange("(p j) n -> p j n", j=PACK))
+        def load_v_pass(e, s):
+            raw[e, s] = ring.tile([P, PACK * N], F32, name="rawp", tag=f"raw{e}_{s}", align_bytes=ALIGN)
+            rows = wv[e, PASS_ROWS * s : PASS_ROWS * (s + 1), :]
+            nc.sync.dma_start(out=raw[e, s][:], in_=rows.rearrange("(p j) n -> p (j n)", j=PACK))
 
         def load_q(i):
             words = wq_words[Q_LOAD * i : Q_LOAD * (i + 1)].rearrange("e s p w -> p (e s) w")
@@ -88,241 +82,235 @@ def tile_moe_qkv_kernel(tc, x_words, x_scales, wq_words, wq_scales, wk_words, wk
             words = wk_words[CHUNK * i : CHUNK * (i + 1)].rearrange("e s p n d -> p (e s) (n d)")
             nc.sync.dma_start(out=kw[i][:], in_=words.bitcast(I32))
 
-        nc.sync.dma_start(offs_sb[:], offs)
-        for q in range(P // QUADRANT):
-            rows = x_scales[:, PACK * q : PACK * (q + 1), :].rearrange("s r t -> r s t")
-            nc.sync.dma_start(out=xs[QUADRANT * q : QUADRANT * q + PACK].bitcast(I32), in_=rows.bitcast(I32))
-        nc.sync.dma_start(out=gate_rows[0:TOKEN_PIECES], in_=gate[:, 0, :].rearrange("r (c t) -> c r t", t=P))
-        for s in range(PASSES):
-            nc.sync.dma_start(out=xw[s][:], in_=x_words[s].rearrange("p t d -> p (t d)").bitcast(I32))
         q_rows = wq_scales.rearrange("e s (q r) n -> r q (e s) n", r=PACK)
         k_rows = wk_scales.rearrange("e s (q r) n -> r q (e s) n", r=PACK)
+
+        def load_q_scales(r, queue):
+            queue.dma_start(out=ws[r:P:QUADRANT].bitcast(I32), in_=q_rows[r].bitcast(I32))
+
+        def load_k_scales(r, queue):
+            queue.dma_start(out=ws[K_PLANE + r : P : QUADRANT].bitcast(I32), in_=k_rows[r].bitcast(I32))
+
+        def load_x_scales(q):
+            rows = x_scales[:, PACK * q : PACK * (q + 1), :].rearrange("s r t -> r s t")
+            nc.sync.dma_start(out=xs[QUADRANT * q : QUADRANT * q + PACK].bitcast(I32), in_=rows.bitcast(I32))
+
+        def load_x_words(s):
+            nc.sync.dma_start(out=xw[s][:], in_=x_words[s].rearrange("p t d -> p (t d)").bitcast(I32))
+
+        def load_bias(queue):
+            queue.dma_start(out=bias_sb[:], in_=bias.rearrange("(b n) e -> n b e", n=P))
+
+        def load_gate(queue):
+            queue.dma_start(out=gate_rows[0:TOKEN_PIECES], in_=gate[:, 0, :].rearrange("r (c t) -> c r t", t=P))
+
+        nc.sync.dma_start(offs_sb[:], offs)
+        for q in range(P // QUADRANT):
+            load_x_scales(q)
+        load_gate(nc.sync)
+        load_x_words(0)
+        load_x_words(1)
         for r in range(PACK):
-            nc.sync.dma_start(out=qs[r:P:QUADRANT].bitcast(I32), in_=q_rows[r].bitcast(I32))
-            nc.sync.dma_start(out=ks[K_PLANE + r : P : QUADRANT].bitcast(I32), in_=k_rows[r].bitcast(I32))
-        load_v(0)
+            load_q_scales(r, nc.sync)
+            load_k_scales(r, nc.sync)
         load_q(0)
-        nc.sync.dma_start(out=bias_sb[:], in_=bias.rearrange("(b n) e -> n b e", n=P))
+        load_v(0)
+        load_bias(nc.sync)
         load_q(1)
         for r, pos in enumerate((pos1, pos2, pos3)):
             nc.sync.dma_start(pos_sb[r][:], pos)
-        load_k(0)
-        load_k(1)
         load_v(1)
-        load_k(2)
-        load_k(3)
+        for i in range(E // CHUNK):
+            load_k(i)
         for e in range(2, WHOLE):
             load_v(e)
-        halves = [(b, s) for b in range(2) for s in range(PASSES)]
-        for b, s in halves:
-            for e in range(WHOLE, E):
-                load_v_half(e, b, s)
+        for e in range(WHOLE, E):
+            for s in range(PASSES):
+                load_v_pass(e, s)
 
-        make_identity(nc, ident[:])
-
-        taken = {SUM_BANKS: 0, TURN_BANKS: 0}
-
-        def bank(group=SUM_BANKS, which=None):
-            if which is None:
-                which = group[taken[group] % len(group)]
-                taken[group] = taken[group] + 1
+        def bank(which):
             return psum.tile([P, PACK, P], F32, name="bank", tag=f"bank{which}")
 
-        acc = bank()
-        for r in range(TOP):
-            nc.tensor.transpose(acc[:, r, :], gate_rows[:, r, :], ident[:])
-        nc.scalar.copy(out=gate_col[:].rearrange("p (r c) -> p r c", c=TOKEN_PIECES), in_=acc[:, 0:TOP, 0:TOKEN_PIECES])
+        def columns(first, count):
+            return slice(first, first + count), slice(first // OFFSETS_A_COLUMN, (first + count) // OFFSETS_A_COLUMN)
 
         def gate_column(r, c):
             return gate_col[:, TOKEN_PIECES * r + c : TOKEN_PIECES * r + c + 1]
 
-        for r in range(TOP):
-            acc = bank()
-            for c in range(TOKEN_PIECES):
-                nc.tensor.transpose(acc[:, c, :], gate_column(r, c).to_broadcast([P, P]), ident[:])
-            nc.scalar.copy(out=gate_sb[r][:], in_=acc[:].rearrange("p c t -> p (c t)"))
+        def spread_gate():
+            acc = bank(4)
+            for r in range(TOP):
+                nc.tensor.transpose(acc[:, r, :], gate_rows[:, r, :], ident[:])
+            nc.scalar.copy(out=gate_col[:].rearrange("p (r c) -> p r c", c=TOKEN_PIECES), in_=acc[:, 0:TOP, 0:TOKEN_PIECES])
+            for r in range(TOP):
+                acc = bank(5 + r)
+                for c in range(TOKEN_PIECES):
+                    nc.tensor.transpose(acc[:, c, :], gate_column(r, c).to_broadcast([P, P]), ident[:])
+                nc.scalar.copy(out=gate_sb[r][:], in_=acc[:].rearrange("p c t -> p (c t)"))
 
-        def gather_tokens(c):
-            width = CHUNK * C
-            entries = offs_sb[:, c * width // OFFSETS_A_COLUMN : (c + 1) * width // OFFSETS_A_COLUMN]
+        def gather_scales(c):
+            cols, entries = columns(c * CHUNK * C, CHUNK * C)
             for s in range(PASSES):
-                nc.vector.tensor_copy(gw[s][c][:], xw[s][:].bitcast(U32).indirect(entries))
-                nc.vector.tensor_copy(gs[s][:, c * width : (c + 1) * width], xs[:, s, :].indirect(entries))
+                nc.vector.tensor_copy(gs[s][:, cols], xs[:, s, :].indirect(offs_sb[:, entries]))
 
-        def project(e, blks, weights, on_vector=False, which=None):
-            acc = bank(SUM_BANKS, which)
-            c, u = divmod(e, CHUNK)
-            slots = slice(e * C, (e + 1) * C)
-            for i, blk in enumerate(blks):
+        def gather_words(c):
+            cols, entries = columns(c * CHUNK * C, CHUNK * C)
+            for s in range(PASSES):
+                nc.vector.tensor_copy(gw[s][c][:], xw[s][:].bitcast(U32).indirect(offs_sb[:, entries]))
+
+        def project(sums, weights, which, on_vector=False):
+            acc = bank(which)
+            for i, (e, blk) in enumerate(sums):
+                c, u = divmod(e, CHUNK)
                 for s in range(PASSES):
-                    words, scales = weights(s, blk % 2)
+                    words, scales = weights(e, s, blk % 2)
                     nc.tensor.matmul_mx(
                         out=acc[:, i, :],
                         lhsT=words,
                         lhsT_scale=scales,
                         rhs=gw[s][c][:, u * C : (u + 1) * C].bitcast(FP8X4),
-                        rhs_scale=gs[s][:, slots],
+                        rhs_scale=gs[s][:, e * C : (e + 1) * C],
                         start=(s == 0),
                         stop=(s == PASSES - 1),
                     )
-            for i, blk in enumerate(blks):
+            for i, (e, blk) in enumerate(sums):
+                slots = slice(e * C, (e + 1) * C)
                 if on_vector:
                     nc.vector.tensor_scalar_add(out=y[blk][:, slots], in0=acc[:, i, :], scalar1=bias_sb[:, blk, e : e + 1])
                 else:
                     nc.scalar.activation(out=y[blk][:, slots], in_=acc[:, i, :], func=IDENT, bias=bias_sb[:, blk, e : e + 1])
 
-        def project_q(e):
-            def weights(s, b):
-                words = qw[e // Q_LOAD][:, (e % Q_LOAD) * PASSES + s, b * 2 * P : (b + 1) * 2 * P]
-                return words.bitcast(FP4X4), qs[:, e * PASSES + s, b * P : (b + 1) * P]
+        def q_weights(e, s, b):
+            words = qw[e // Q_LOAD][:, (e % Q_LOAD) * PASSES + s, b * 2 * P : (b + 1) * 2 * P]
+            return words.bitcast(FP4X4), ws[:, e * PASSES + s, b * P : (b + 1) * P]
 
-            project(e, (0, 1), weights, e >= Q_ON_VECTOR)
+        def k_weights(e, s, b):
+            words = kw[e // CHUNK][:, (e % CHUNK) * PASSES + s, b * P : (b + 1) * P]
+            return words.bitcast(FP8X4), ws[K_PLANE:P, e * PASSES + s, b * P : (b + 1) * P]
 
-        def project_k(e):
-            def weights(s, b):
-                words = kw[e // CHUNK][:, (e % CHUNK) * PASSES + s, b * P : (b + 1) * P]
-                return words.bitcast(FP8X4), ks[K_PLANE:P, e * PASSES + s, b * P : (b + 1) * P]
+        def v_weights(e, s, b):
+            if (e, s, b) in quantised:
+                codes, scales = quantised[e, s, b]
+                return codes[:].bitcast(FP8X4), scales[:]
+            codes, scales = quantised[e, s]
+            return codes[:, b * P : (b + 1) * P].bitcast(FP8X4), scales[:, b * P : (b + 1) * P]
 
-            project(e, (2, 3), weights)
+        def pair(first, blks):
+            return [(e, blk) for blk in blks for e in (first, first + 1)]
 
-        def project_v(e):
-            def weights(s, b):
-                codes, scales = quantised[e]
-                cols = slice(s * N + b * P, s * N + (b + 1) * P)
-                return codes[:, cols].bitcast(FP8X4), scales[:, cols]
+        def chunk(c, blk):
+            return [(e, blk) for e in range(c * CHUNK, (c + 1) * CHUNK)]
 
-            project(e, (4, 5), weights, which=SUM_BANKS[-1 - e % len(SUM_BANKS)])
-
-        def project_v_half(e, b):
-            def weights(s, half):
-                codes, scales = quantised[half, s]
-                cols = slice((e - WHOLE) * P, (e - WHOLE + 1) * P)
-                return codes[:, cols].bitcast(FP8X4), scales[:, cols]
-
-            project(e, (4 + b,), weights, b == 1, LAST_BANKS[e - WHOLE] if b == 1 else None)
-
-        def round_copy(dst, src, on_vector):
+        def round_rows(key, dst, src, on_vector):
+            staged[key] = dst
             dst = dst.rearrange("p (c i j) -> p c j i", i=WALK, j=PACK)
-            src = src.rearrange("p (j c i) -> p c j i", i=WALK, j=PACK)
+            src = src.rearrange("p j (c i) -> p c j i", i=WALK)
             if on_vector:
                 nc.vector.tensor_copy(out=dst, in_=src)
             else:
                 nc.scalar.copy(out=dst, in_=src)
 
-        def round_expert(e):
-            staged[e] = ring.tile([P, PASSES, PACK * N], BF16, name="staged", tag="staged", bufs=STAGED_BUFS, align_bytes=ALIGN)
+        def new_stage(width, room):
+            return ring.tile([P, PACK * width], BF16, name="staged", tag=room, align_bytes=ALIGN)
+
+        def round_piece(e, room, on_vector=True):
+            both = new_stage(PASSES * N, room)
             for s in range(PASSES):
-                round_copy(staged[e][:, s, :], raw[e][:, s, :], e >= ROUND_ON_SCALAR)
+                round_rows((e, s), both[:, s * PACK * N : (s + 1) * PACK * N], raw[e][:, s, :].rearrange("p (j n) -> p j n", j=PACK), on_vector)
 
-        def round_half(b, s):
-            staged[b, s] = ring.tile([P, E - WHOLE, PACK * P], BF16, name="staged", tag="staged", bufs=STAGED_BUFS, align_bytes=ALIGN)
-            for e in range(WHOLE, E):
-                round_copy(staged[b, s][:, e - WHOLE, :], raw[e, b, s][:].rearrange("p j n -> p (j n)"), True)
-
-        def quantise(key, width, over=None):
-            if over is None:
-                codes = ring.tile([P, width], U32, name="codes", tag="codes", bufs=CODE_BUFS, align_bytes=ALIGN)
-            else:
-                codes = ring.tile([P, width], U32, name="codes", tag=over, align_bytes=ALIGN)
-            scales = ring.tile([P, width], U8, name="scales", tag="scales", bufs=SCALE_BUFS, align_bytes=ALIGN)
-            nc.vector.quantize_mx(out=codes[:].bitcast(FP8X4), scales=scales[:], in_=staged[key][:].rearrange("p s w -> p (s w)"))
+        def quantise_rows(key):
+            width = staged[key].shape[1] // PACK
+            codes = ring.tile([P, width], U32, name="codes", tag="codes", bufs=CODE_BUFS, align_bytes=ALIGN)
+            scales = ring.tile([P, width], U8, name="scales", tag="scales", bufs=CODE_BUFS, align_bytes=ALIGN)
+            nc.vector.quantize_mx(out=codes[:].bitcast(FP8X4), scales=scales[:], in_=staged[key])
             quantised[key] = (codes, scales)
 
-        room = ("raw0", "qw0", "qw1", "kw2", "kw1", "kw0")
+        def quantise(e):
+            for s in range(PASSES):
+                quantise_rows((e, s))
 
-        def new_parts(blk):
-            parts[blk] = ring.tile([P, TOP, T], F32, name="parts", tag=room[blk], align_bytes=ALIGN)
-
-        def token_cut(h, cuts):
-            width = T // cuts
-            return slice(h * width, (h + 1) * width), slice(h * width // OFFSETS_A_COLUMN, (h + 1) * width // OFFSETS_A_COLUMN)
-
-        def fetch_weighed(blk, cols, entries):
+        def combine_on_vector(blk, first, count, room, stages=("stage0", "stage1")):
+            cols, entries = columns(first, count)
+            two = ring.tile([P, 2, count], F32, name="two", tag=stages[0], align_bytes=ALIGN)
+            third = ring.tile([P, count], F32, name="third", tag=stages[1], align_bytes=ALIGN)
+            parts = (two[:, 0, :], two[:, 1, :], third[:])
+            total = ring.tile([P, count], F32, name="total", tag=room, align_bytes=ALIGN)
             for r in range(TOP):
-                nc.vector.tensor_tensor(parts[blk][:, r, cols], y[blk][:].indirect(pos_sb[r][:, entries]), gate_sb[r][:, cols], MULT)
+                nc.vector.tensor_tensor(parts[r], y[blk][:].indirect(pos_sb[r][:, entries]), gate_sb[r][:, cols], MULT)
+            nc.vector.tensor_tensor(parts[0], parts[0], parts[1], ADD)
+            nc.vector.tensor_tensor(total[:], parts[0], parts[2], ADD)
+            nc.sync.dma_start(out=out[blk * P : (blk + 1) * P, cols], in_=total[:])
 
-        def add_and_store(blk, cols):
-            nc.vector.tensor_tensor(parts[blk][:, 0, cols], parts[blk][:, 0, cols], parts[blk][:, 1, cols], ADD)
-            nc.vector.tensor_tensor(parts[blk][:, 1, cols], parts[blk][:, 0, cols], parts[blk][:, 2, cols], ADD)
-            nc.sync.dma_start(out=out[blk * P : (blk + 1) * P, cols], in_=parts[blk][:, 1, cols])
-
-        def fetch_plain(blk, cuts):
-            new_parts(blk)
-            for h in range(cuts):
-                cols, entries = token_cut(h, cuts)
+        def fetch_on_scalar(blk, first_piece, pieces, room):
+            count = pieces * P
+            parts = ring.tile([P, TOP, count], F32, name="parts", tag=room, align_bytes=ALIGN)
+            for first in range(0, count, 2 * P):
+                width = min(2 * P, count - first)
+                cols, entries = columns(first_piece * P + first, width)
                 for r in range(TOP):
-                    nc.scalar.activation(out=parts[blk][:, r, cols], in_=y[blk][:].indirect(pos_sb[r][:, entries]), func=COPY)
+                    nc.scalar.activation(out=parts[:, r, first : first + width], in_=y[blk][:].indirect(pos_sb[r][:, entries]), func=COPY)
+            return parts
 
-        def weigh_turned(blk, banks=None):
-            scaled = ring.tile([P, TOKEN_PIECES, TOP, P], F32, name="scaled", tag="scaled", bufs=1)
-            for group in range(TOP):
-                acc = bank(TURN_BANKS, banks[group % 2] if banks else None)
-                pieces = [divmod(PACK * group + i, TOP) for i in range(PACK)]
-                for i, (c, r) in enumerate(pieces):
-                    nc.tensor.transpose(acc[:, i, :], parts[blk][:, r, c * P : (c + 1) * P], ident[:])
-                for i, (c, r) in enumerate(pieces):
-                    nc.scalar.activation(out=scaled[:, c, r, :], in_=acc[:, i, :], func=COPY, scale=gate_column(r, c))
-            acc = bank(TURN_BANKS)
-            for c in range(TOKEN_PIECES):
+        def weigh_turned(blk, first_piece, pieces, parts, turn_banks, sum_bank=7, queue=nc.sync):
+            count = pieces * P
+            scaled = ring.tile([P, pieces, TOP, P], F32, name="scaled", tag="scaled", bufs=1)
+            for c in range(pieces):
+                acc = bank(turn_banks[c])
+                for r in range(TOP):
+                    nc.tensor.transpose(acc[:, r, :], parts[:, r, c * P : (c + 1) * P], ident[:])
+                for r in range(TOP):
+                    nc.scalar.activation(out=scaled[:, c, r, :], in_=acc[:, r, :], func=COPY, scale=gate_column(r, first_piece + c))
+            acc = bank(sum_bank)
+            for c in range(pieces):
                 for r in range(TOP):
                     nc.tensor.matmul(acc[:, c, :], scaled[:, c, r, :], ident[:], start=(r == 0), stop=(r == TOP - 1), is_transpose=True)
-            nc.scalar.copy(out=parts[blk][:, 0, :], in_=acc[:].rearrange("p c t -> p (c t)"))
-            nc.sync.dma_start(out=out[blk * P : (blk + 1) * P, :], in_=parts[blk][:, 0, :])
+            nc.scalar.copy(out=parts[:, 0, :], in_=acc[:, 0:pieces, :].rearrange("p c t -> p (c t)"))
+            queue.dma_start(out=out[blk * P : (blk + 1) * P, first_piece * P : first_piece * P + count], in_=parts[:, 0, :])
 
-        all_cols, all_entries = token_cut(0, 1)
-        whole_width, half_width = PASSES * N, (E - WHOLE) * P
+        def combine_on_scalar(blk, first_piece, pieces, room, turn_banks, sum_bank=7, queue=nc.sync):
+            weigh_turned(blk, first_piece, pieces, fetch_on_scalar(blk, first_piece, pieces, room), turn_banks, sum_bank, queue)
+
         for blk in range(4):
             y[blk] = ring.tile([P, S], F32, name=f"y{blk}", align_bytes=ALIGN)
         for c in range(E // CHUNK):
-            gather_tokens(c)
-            for e in range(c * CHUNK, (c + 1) * CHUNK):
-                project_q(e)
-        round_expert(0)
-        new_parts(0)
-        fetch_weighed(0, all_cols, all_entries)
-        quantise(0, whole_width)
-        new_parts(1)
-        fetch_weighed(1, all_cols, all_entries)
-        add_and_store(0, all_cols)
-        add_and_store(1, all_cols)
-
-        for e in range(E // 2):
-            project_k(e)
-        round_expert(1)
-        for e in range(E // 2, E):
-            project_k(e)
-        quantise(1, whole_width)
-        y[4] = ring.tile([P, S], F32, name="y4", tag="raw1", align_bytes=ALIGN)
-        y[5] = ring.tile([P, S], F32, name="y5", tag="raw2", align_bytes=ALIGN)
-        round_expert(2)
-        quantise(2, whole_width)
-        fetch_plain(2, 1)
-        fetch_plain(3, 1)
-        weigh_turned(2)
-        weigh_turned(3)
-
-        round_expert(ROUND_ON_SCALAR)
-        for e in range(ROUND_ON_SCALAR, WHOLE - 1):
-            round_expert(e + 1)
-            quantise(e, whole_width, f"raw{e + 1}")
-        round_half(0, 0)
-        quantise(WHOLE - 1, whole_width, f"raw{WHOLE}_0_0")
-        for e in range(WHOLE):
-            project_v(e)
-        for b in range(2):
-            round_half(b, 1)
-            quantise((b, 0), half_width, f"raw{WHOLE}_{b}_1")
-            quantise((b, 1), half_width)
-            if b == 0:
-                round_half(1, 0)
-            for e in range(WHOLE, E):
-                project_v_half(e, b)
-            if b == 0:
-                fetch_plain(4, 2)
-
-        new_parts(5)
+            gather_words(c)
+            gather_scales(c)
+        spread_gate()
+        round_piece(0, "stage0", on_vector=False)
+        for c in range(E // CHUNK):
+            for b in range(2):
+                project(chunk(c, b), q_weights, (5, 6, 7, 4, 0, 1, 2, 3)[2 * c + b])
+        round_piece(1, "qw0", on_vector=False)
+        quantise(0)
+        combine_on_vector(0, 0, T, "total0", ("pair0", "third0"))
+        quantise(1)
+        combine_on_vector(1, 0, T, "total1", ("qw1", "stage0"))
+        for c in range(E // CHUNK):
+            for b in range(2):
+                project(chunk(c, 2 + b), k_weights, (2, 3, 0, 1)[(2 * c + b) % 4])
+        combine_on_scalar(2, 0, TOKEN_PIECES, "kw0", (4, 5, 6, 2))
+        y[4] = ring.tile([P, S], F32, name="y4", tag="raw0", align_bytes=ALIGN)
+        y[5] = ring.tile([P, S], F32, name="y5", tag="raw1", align_bytes=ALIGN)
+        project(pair(0, (4, 5)), v_weights, 4)
+        for e in range(2, WHOLE):
+            round_piece(e, ("qw1", "stage0")[e % 2])
+            quantise(e)
+            if e == E - 2:
+                project([(e, 4), (e, 5)], v_weights, 5)
+            elif e % 2:
+                project(pair(e - 1, (4, 5)), v_weights, (4, 7, 5, 1, 3)[e // 2])
+            if e == 3:
+                combine_on_scalar(3, 0, TOKEN_PIECES, "kw1", (5, 6, 0, 1), 3)
+        last = E - 1
+        rows = [raw[last, s][:].rearrange("p (j n) -> p j n", j=PACK) for s in range(PASSES)]
+        round_rows((last, 0), new_stage(N, "raw8")[:], rows[0], False)
+        round_rows((last, 1, 1), new_stage(P, "stage0")[:], rows[1][:, :, P:N], True)
+        round_rows((last, 1, 0), new_stage(P, "raw9")[:], rows[1][:, :, 0:P], False)
+        for key in ((last, 0), (last, 1, 1), (last, 1, 0)):
+            quantise_rows(key)
+        project([(last, 5)], v_weights, 6, on_vector=True)
+        project([(last, 4)], v_weights, 7)
+        combine_on_scalar(4, 0, TOKEN_PIECES - 1, "kw2", (4, 5, 6), 0, nc.scalar)
         for h in range(2):
-            cols, entries = token_cut(h, 2)
-            fetch_weighed(5, cols, entries)
-            add_and_store(5, cols)
-        weigh_turned(4, LAST_BANKS)
+            combine_on_vector(5, h * T // 2, T // 2, ("kw3", "raw2")[h], (("raw4", "raw3"), ("pair0", "third0"))[h])
+        combine_on_vector(4, T - P, P, "raw5", ("raw6", "raw7"))

@@ -46,7 +46,7 @@ def tile_moe_qkv_kernel(tc, x_words, x_scales, wq_words, wq_scales, wk_words, wk
 
         offs_sb = keep.tile([P, S // OFFSETS_A_COLUMN], U16, name="offs_sb")
         pos_sb = [keep.tile([P, T // OFFSETS_A_COLUMN], U16, name=f"pos_sb{r}") for r in range(TOP)]
-        xw = [keep.tile([P, T], I32, name=f"xw{s}", align_bytes=ALIGN) for s in range(PASSES)]
+        xw = keep.tile([P, PASSES, T], I32, name="xw", align_bytes=ALIGN)
         xs = keep.tile([P, PASSES, T], U8, name="xs", align_bytes=ALIGN)
         ws = keep.tile([P, E * PASSES, N], U8, name="ws", align_bytes=ALIGN)
         qw = [ring.tile([P, Q_LOAD * PASSES, 2 * N], U8, name=f"qw{i}", align_bytes=ALIGN) for i in range(E // Q_LOAD)]
@@ -95,8 +95,8 @@ def tile_moe_qkv_kernel(tc, x_words, x_scales, wq_words, wq_scales, wk_words, wk
             rows = x_scales[:, PACK * q : PACK * (q + 1), :].rearrange("s r t -> r s t")
             nc.sync.dma_start(out=xs[QUADRANT * q : QUADRANT * q + PACK].bitcast(I32), in_=rows.bitcast(I32))
 
-        def load_x_words(s):
-            nc.sync.dma_start(out=xw[s][:], in_=x_words[s].rearrange("p t d -> p (t d)").bitcast(I32))
+        def load_x_words():
+            nc.sync.dma_start(out=xw[:], in_=x_words.rearrange("s p t d -> p s (t d)").bitcast(I32))
 
         def load_bias(queue):
             queue.dma_start(out=bias_sb[:], in_=bias.rearrange("(b n) e -> n b e", n=P))
@@ -105,11 +105,10 @@ def tile_moe_qkv_kernel(tc, x_words, x_scales, wq_words, wq_scales, wk_words, wk
             queue.dma_start(out=gate_rows[0:TOKEN_PIECES], in_=gate[:, 0, :].rearrange("r (c t) -> c r t", t=P))
 
         nc.sync.dma_start(offs_sb[:], offs)
+        load_x_words()
         for q in range(P // QUADRANT):
             load_x_scales(q)
         load_gate(nc.sync)
-        load_x_words(0)
-        load_x_words(1)
         for r in range(PACK):
             load_q_scales(r, nc.sync)
             load_k_scales(r, nc.sync)
@@ -156,7 +155,7 @@ def tile_moe_qkv_kernel(tc, x_words, x_scales, wq_words, wq_scales, wk_words, wk
         def gather_words(c):
             cols, entries = columns(c * CHUNK * C, CHUNK * C)
             for s in range(PASSES):
-                nc.vector.tensor_copy(gw[s][c][:], xw[s][:].bitcast(U32).indirect(offs_sb[:, entries]))
+                nc.vector.tensor_copy(gw[s][c][:], xw[:, s, :].bitcast(U32).indirect(offs_sb[:, entries]))
 
         def project(sums, weights, which, on_vector=False):
             acc = bank(which)
@@ -251,8 +250,7 @@ def tile_moe_qkv_kernel(tc, x_words, x_scales, wq_words, wq_scales, wk_words, wk
                     nc.scalar.activation(out=parts[:, r, first : first + width], in_=y[blk][:].indirect(pos_sb[r][:, entries]), func=COPY)
             return parts
 
-        def weigh_turned(blk, first_piece, pieces, parts, turn_banks, sum_bank=7, queue=nc.sync):
-            count = pieces * P
+        def weigh_turned(blk, first_piece, pieces, parts, turn_banks, sum_banks, queue):
             scaled = ring.tile([P, pieces, TOP, P], F32, name="scaled", tag="scaled", bufs=1)
             for c in range(pieces):
                 acc = bank(turn_banks[c])
@@ -260,15 +258,20 @@ def tile_moe_qkv_kernel(tc, x_words, x_scales, wq_words, wq_scales, wk_words, wk
                     nc.tensor.transpose(acc[:, r, :], parts[:, r, c * P : (c + 1) * P], ident[:])
                 for r in range(TOP):
                     nc.scalar.activation(out=scaled[:, c, r, :], in_=acc[:, r, :], func=COPY, scale=gate_column(r, first_piece + c))
-            acc = bank(sum_bank)
-            for c in range(pieces):
-                for r in range(TOP):
-                    nc.tensor.matmul(acc[:, c, :], scaled[:, c, r, :], ident[:], start=(r == 0), stop=(r == TOP - 1), is_transpose=True)
-            nc.scalar.copy(out=parts[:, 0, :], in_=acc[:, 0:pieces, :].rearrange("p c t -> p (c t)"))
-            queue.dma_start(out=out[blk * P : (blk + 1) * P, first_piece * P : first_piece * P + count], in_=parts[:, 0, :])
+            done = 0
+            for which, group in sum_banks:
+                acc = bank(which)
+                for c in range(group):
+                    for r in range(TOP):
+                        nc.tensor.matmul(acc[:, c, :], scaled[:, done + c, r, :], ident[:], start=(r == 0), stop=(r == TOP - 1), is_transpose=True)
+                cols = slice(done * P, (done + group) * P)
+                nc.scalar.copy(out=parts[:, 0, cols], in_=acc[:, 0:group, :].rearrange("p c t -> p (c t)"))
+                first = (first_piece + done) * P
+                queue.dma_start(out=out[blk * P : (blk + 1) * P, first : first + group * P], in_=parts[:, 0, cols])
+                done += group
 
-        def combine_on_scalar(blk, first_piece, pieces, room, turn_banks, sum_bank=7, queue=nc.sync):
-            weigh_turned(blk, first_piece, pieces, fetch_on_scalar(blk, first_piece, pieces, room), turn_banks, sum_bank, queue)
+        def combine_on_scalar(blk, first_piece, pieces, room, turn_banks, sum_banks, queue=nc.sync):
+            weigh_turned(blk, first_piece, pieces, fetch_on_scalar(blk, first_piece, pieces, room), turn_banks, sum_banks, queue)
 
         for blk in range(4):
             y[blk] = ring.tile([P, S], F32, name=f"y{blk}", align_bytes=ALIGN)
@@ -288,7 +291,7 @@ def tile_moe_qkv_kernel(tc, x_words, x_scales, wq_words, wq_scales, wk_words, wk
         for c in range(E // CHUNK):
             for b in range(2):
                 project(chunk(c, 2 + b), k_weights, (2, 3, 0, 1)[(2 * c + b) % 4])
-        combine_on_scalar(2, 0, TOKEN_PIECES, "kw0", (4, 5, 6, 2))
+        combine_on_scalar(2, 0, TOKEN_PIECES, "kw0", (4, 5, 6, 2), [(7, TOKEN_PIECES)])
         y[4] = ring.tile([P, S], F32, name="y4", tag="raw0", align_bytes=ALIGN)
         y[5] = ring.tile([P, S], F32, name="y5", tag="raw1", align_bytes=ALIGN)
         project(pair(0, (4, 5)), v_weights, 4)
@@ -300,7 +303,7 @@ def tile_moe_qkv_kernel(tc, x_words, x_scales, wq_words, wq_scales, wk_words, wk
             elif e % 2:
                 project(pair(e - 1, (4, 5)), v_weights, (4, 7, 5, 1, 3)[e // 2])
             if e == 3:
-                combine_on_scalar(3, 0, TOKEN_PIECES, "kw1", (5, 6, 0, 1), 3)
+                combine_on_scalar(3, 0, TOKEN_PIECES, "kw1", (5, 6, 0, 1), [(3, TOKEN_PIECES)])
         last = E - 1
         rows = [raw[last, s][:].rearrange("p (j n) -> p j n", j=PACK) for s in range(PASSES)]
         round_rows((last, 0), new_stage(N, "raw8")[:], rows[0], False)
@@ -310,7 +313,6 @@ def tile_moe_qkv_kernel(tc, x_words, x_scales, wq_words, wq_scales, wk_words, wk
             quantise_rows(key)
         project([(last, 5)], v_weights, 6, on_vector=True)
         project([(last, 4)], v_weights, 7)
-        combine_on_scalar(4, 0, TOKEN_PIECES - 1, "kw2", (4, 5, 6), 0, nc.scalar)
-        for h in range(2):
-            combine_on_vector(5, h * T // 2, T // 2, ("kw3", "raw2")[h], (("raw4", "raw3"), ("pair0", "third0"))[h])
+        combine_on_scalar(4, 0, TOKEN_PIECES - 1, "kw2", (4, 5, 6), [(0, 2), (1, 1)], nc.scalar)
+        combine_on_vector(5, 0, T, "kw3", ("raw4", "raw3"))
         combine_on_vector(4, T - P, P, "raw5", ("raw6", "raw7"))

@@ -35,6 +35,7 @@ Q_LOAD = 6
 WALK = 4
 WHOLE = E - 1
 CODE_BUFS = 16
+PORT = 4
 
 
 def tile_moe_qkv_kernel(tc, x_words, x_scales, wq_words, wq_scales, wk_words, wk_scales, wv, bias, gate, offs, pos1, pos2, pos3, out):
@@ -60,8 +61,8 @@ def tile_moe_qkv_kernel(tc, x_words, x_scales, wq_words, wq_scales, wk_words, wk
         gs = [keep.tile([P, S], U8, name=f"gs{s}", align_bytes=ALIGN) for s in range(PASSES)]
         raw, staged, quantised, y = {}, {}, {}, {}
 
+        nc.vector.memset(xs[:].rearrange("p s t -> p (s t)").bitcast(I32), 0)
         nc.vector.memset(ws[:].rearrange("p s t -> p (s t)").bitcast(I32), 0)
-        nc.gpsimd.memset(xs[:].rearrange("p s t -> p (s t)").bitcast(I32), 0)
         nc.gpsimd.memset(gate_rows[:].rearrange("c r t -> c (r t)"), 0.0)
         make_identity(nc, ident[:])
 
@@ -91,9 +92,9 @@ def tile_moe_qkv_kernel(tc, x_words, x_scales, wq_words, wq_scales, wk_words, wk
         def load_k_scales(r, queue):
             queue.dma_start(out=ws[K_PLANE + r : P : QUADRANT].bitcast(I32), in_=k_rows[r].bitcast(I32))
 
-        def load_x_scales(q):
-            rows = x_scales[:, PACK * q : PACK * (q + 1), :].rearrange("s r t -> r s t")
-            nc.sync.dma_start(out=xs[QUADRANT * q : QUADRANT * q + PACK].bitcast(I32), in_=rows.bitcast(I32))
+        def load_x_scales(r):
+            rows = x_scales.rearrange("s (q r) t -> r q s t", r=PACK)[r]
+            nc.sync.dma_start(out=xs[r:P:QUADRANT].bitcast(I32), in_=rows.bitcast(I32))
 
         def load_x_words():
             nc.sync.dma_start(out=xw[:], in_=x_words.rearrange("s p t d -> p s (t d)").bitcast(I32))
@@ -102,19 +103,19 @@ def tile_moe_qkv_kernel(tc, x_words, x_scales, wq_words, wq_scales, wk_words, wk
             queue.dma_start(out=bias_sb[:], in_=bias.rearrange("(b n) e -> n b e", n=P))
 
         def load_gate(queue):
-            queue.dma_start(out=gate_rows[0:TOKEN_PIECES], in_=gate[:, 0, :].rearrange("r (c t) -> c r t", t=P))
+            queue.dma_start(out=gate_rows[0 : TOKEN_PIECES * PORT : PORT], in_=gate[:, 0, :].rearrange("r (c t) -> c r t", t=P))
 
         nc.sync.dma_start(offs_sb[:], offs)
+        for r in range(PACK):
+            load_x_scales(r)
         load_x_words()
-        for q in range(P // QUADRANT):
-            load_x_scales(q)
         load_gate(nc.sync)
         for r in range(PACK):
             load_q_scales(r, nc.sync)
             load_k_scales(r, nc.sync)
         load_q(0)
-        load_v(0)
         load_bias(nc.sync)
+        load_v(0)
         load_q(1)
         for r, pos in enumerate((pos1, pos2, pos3)):
             nc.sync.dma_start(pos_sb[r][:], pos)
@@ -123,9 +124,8 @@ def tile_moe_qkv_kernel(tc, x_words, x_scales, wq_words, wq_scales, wk_words, wk
             load_k(i)
         for e in range(2, WHOLE):
             load_v(e)
-        for e in range(WHOLE, E):
-            for s in range(PASSES):
-                load_v_pass(e, s)
+        for s in range(PASSES):
+            load_v_pass(WHOLE, s)
 
         def bank(which):
             return psum.tile([P, PACK, P], F32, name="bank", tag=f"bank{which}")
@@ -140,7 +140,7 @@ def tile_moe_qkv_kernel(tc, x_words, x_scales, wq_words, wq_scales, wk_words, wk
             acc = bank(4)
             for r in range(TOP):
                 nc.tensor.transpose(acc[:, r, :], gate_rows[:, r, :], ident[:])
-            nc.scalar.copy(out=gate_col[:].rearrange("p (r c) -> p r c", c=TOKEN_PIECES), in_=acc[:, 0:TOP, 0:TOKEN_PIECES])
+            nc.scalar.copy(out=gate_col[:].rearrange("p (r c) -> p r c", c=TOKEN_PIECES), in_=acc[:, 0:TOP, 0 : TOKEN_PIECES * PORT : PORT])
             for r in range(TOP):
                 acc = bank(5 + r)
                 for c in range(TOKEN_PIECES):
@@ -279,10 +279,15 @@ def tile_moe_qkv_kernel(tc, x_words, x_scales, wq_words, wq_scales, wk_words, wk
             gather_words(c)
             gather_scales(c)
         spread_gate()
+        project(chunk(0, 0), q_weights, 5)
+        project(chunk(0, 1), q_weights, 6)
+        project(chunk(1, 0), q_weights, 7)
+        project(chunk(1, 1), q_weights, 4)
         round_piece(0, "stage0", on_vector=False)
-        for c in range(E // CHUNK):
-            for b in range(2):
-                project(chunk(c, b), q_weights, (5, 6, 7, 4, 0, 1, 2, 3)[2 * c + b])
+        project(chunk(2, 0), q_weights, 0)
+        project(chunk(3, 0), q_weights, 2)
+        project(chunk(2, 1), q_weights, 1)
+        project(chunk(3, 1), q_weights, 3)
         round_piece(1, "qw0", on_vector=False)
         quantise(0)
         combine_on_vector(0, 0, T, "total0", ("pair0", "third0"))
@@ -296,8 +301,9 @@ def tile_moe_qkv_kernel(tc, x_words, x_scales, wq_words, wq_scales, wk_words, wk
         y[5] = ring.tile([P, S], F32, name="y5", tag="raw1", align_bytes=ALIGN)
         project(pair(0, (4, 5)), v_weights, 4)
         for e in range(2, WHOLE):
-            round_piece(e, ("qw1", "stage0")[e % 2])
-            quantise(e)
+            if e >= 2:
+                round_piece(e, ("qw1", "stage0")[e % 2])
+                quantise(e)
             if e == E - 2:
                 project([(e, 4), (e, 5)], v_weights, 5)
             elif e % 2:

@@ -36,6 +36,7 @@ WALK = 4
 WHOLE = E - 1
 CODE_BUFS = 16
 PORT = 4
+BANK_BYTES = 2048
 
 
 def tile_moe_qkv_kernel(tc, x_words, x_scales, wq_words, wq_scales, wk_words, wk_scales, wv, bias, gate, offs, pos1, pos2, pos3, out):
@@ -61,8 +62,8 @@ def tile_moe_qkv_kernel(tc, x_words, x_scales, wq_words, wq_scales, wk_words, wk
         gs = [keep.tile([P, S], U8, name=f"gs{s}", align_bytes=ALIGN) for s in range(PASSES)]
         raw, staged, quantised, y = {}, {}, {}, {}
 
-        nc.vector.memset(xs[:].rearrange("p s t -> p (s t)").bitcast(I32), 0)
         nc.vector.memset(ws[:].rearrange("p s t -> p (s t)").bitcast(I32), 0)
+        nc.gpsimd.memset(xs[:].rearrange("p s t -> p (s t)").bitcast(I32), 0)
         nc.gpsimd.memset(gate_rows[:].rearrange("c r t -> c (r t)"), 0.0)
         make_identity(nc, ident[:])
 
@@ -106,12 +107,13 @@ def tile_moe_qkv_kernel(tc, x_words, x_scales, wq_words, wq_scales, wk_words, wk
             queue.dma_start(out=gate_rows[0 : TOKEN_PIECES * PORT : PORT], in_=gate[:, 0, :].rearrange("r (c t) -> c r t", t=P))
 
         nc.sync.dma_start(offs_sb[:], offs)
+        load_x_words()
         for r in range(PACK):
             load_x_scales(r)
-        load_x_words()
-        load_gate(nc.sync)
         for r in range(PACK):
             load_q_scales(r, nc.sync)
+            if r == 1:
+                load_gate(nc.sync)
             load_k_scales(r, nc.sync)
         load_q(0)
         load_bias(nc.sync)
@@ -128,7 +130,11 @@ def tile_moe_qkv_kernel(tc, x_words, x_scales, wq_words, wq_scales, wk_words, wk
             load_v_pass(WHOLE, s)
 
         def bank(which):
-            return psum.tile([P, PACK, P], F32, name="bank", tag=f"bank{which}")
+            return psum.tile([P, PACK, P], F32, name="bank", tag=f"bank{which}", offset=which * BANK_BYTES)
+
+        def two_banks(first):
+            both = psum.tile([P, 2 * PACK, P], F32, name="both", tag=f"both{first}", offset=first * BANK_BYTES)
+            return [(both[:, 0:PACK, :], 2), (both[:, PACK : 2 * PACK, :], 2)]
 
         def columns(first, count):
             return slice(first, first + count), slice(first // OFFSETS_A_COLUMN, (first + count) // OFFSETS_A_COLUMN)
@@ -259,8 +265,7 @@ def tile_moe_qkv_kernel(tc, x_words, x_scales, wq_words, wq_scales, wk_words, wk
                 for r in range(TOP):
                     nc.scalar.activation(out=scaled[:, c, r, :], in_=acc[:, r, :], func=COPY, scale=gate_column(r, first_piece + c))
             done = 0
-            for which, group in sum_banks:
-                acc = bank(which)
+            for acc, group in sum_banks():
                 for c in range(group):
                     for r in range(TOP):
                         nc.tensor.matmul(acc[:, c, :], scaled[:, done + c, r, :], ident[:], start=(r == 0), stop=(r == TOP - 1), is_transpose=True)
@@ -296,20 +301,20 @@ def tile_moe_qkv_kernel(tc, x_words, x_scales, wq_words, wq_scales, wk_words, wk
         for c in range(E // CHUNK):
             for b in range(2):
                 project(chunk(c, 2 + b), k_weights, (2, 3, 0, 1)[(2 * c + b) % 4])
-        combine_on_scalar(2, 0, TOKEN_PIECES, "kw0", (4, 5, 6, 2), [(7, TOKEN_PIECES)])
+        combine_on_scalar(2, 0, TOKEN_PIECES, "kw0", (4, 5, 6, 7), lambda: two_banks(2))
         y[4] = ring.tile([P, S], F32, name="y4", tag="raw0", align_bytes=ALIGN)
         y[5] = ring.tile([P, S], F32, name="y5", tag="raw1", align_bytes=ALIGN)
-        project(pair(0, (4, 5)), v_weights, 4)
+        project(pair(0, (4, 5)), v_weights, 2)
         for e in range(2, WHOLE):
             if e >= 2:
                 round_piece(e, ("qw1", "stage0")[e % 2])
                 quantise(e)
-            if e == E - 2:
-                project([(e, 4), (e, 5)], v_weights, 5)
+            if e >= 8:
+                project([(e, 4), (e, 5)], v_weights, (0, 1, 2)[e - 8])
             elif e % 2:
-                project(pair(e - 1, (4, 5)), v_weights, (4, 7, 5, 1, 3)[e // 2])
+                project(pair(e - 1, (4, 5)), v_weights, (2, 3, 2, 3)[e // 2])
             if e == 3:
-                combine_on_scalar(3, 0, TOKEN_PIECES, "kw1", (5, 6, 0, 1), [(3, TOKEN_PIECES)])
+                combine_on_scalar(3, 0, TOKEN_PIECES, "kw1", (4, 5, 6, 7), lambda: two_banks(0))
         last = E - 1
         rows = [raw[last, s][:].rearrange("p (j n) -> p j n", j=PACK) for s in range(PASSES)]
         round_rows((last, 0), new_stage(N, "raw8")[:], rows[0], False)
@@ -319,6 +324,6 @@ def tile_moe_qkv_kernel(tc, x_words, x_scales, wq_words, wq_scales, wk_words, wk
             quantise_rows(key)
         project([(last, 5)], v_weights, 6, on_vector=True)
         project([(last, 4)], v_weights, 7)
-        combine_on_scalar(4, 0, TOKEN_PIECES - 1, "kw2", (4, 5, 6), [(0, 2), (1, 1)], nc.scalar)
+        combine_on_scalar(4, 0, TOKEN_PIECES - 1, "kw2", (4, 5, 6), lambda: [(bank(0), 2), (bank(1), 1)], nc.scalar)
         combine_on_vector(5, 0, T, "kw3", ("raw4", "raw3"))
         combine_on_vector(4, T - P, P, "raw5", ("raw6", "raw7"))

@@ -26,15 +26,19 @@ QUADRANT = 32
 PASS_ROWS = P * PACK
 PASSES = K // PASS_ROWS
 BLOCKS = 3 * N // P
-TOKEN_PIECES = T // P
+PIECES = T // P
 OFFSETS_A_COLUMN = 16
 ALIGN = 64
 K_PLANE = 4
 CHUNK = 3
+CHUNKS = E // CHUNK
 Q_LOAD = 6
+K_LOAD = 4
 WALK = 4
-WHOLE = E - 1
-CODE_BUFS = 16
+BOTH = (0, 1)
+ROUND_ON_SCALAR = 1
+STAGE_BUFS = 3
+CODE_BUFS = 12
 PORT = 4
 BANK_BYTES = 2048
 
@@ -52,15 +56,16 @@ def tile_moe_qkv_kernel(tc, x_words, x_scales, wq_words, wq_scales, wk_words, wk
         xs = keep.tile([P, PASSES, T], U8, name="xs", align_bytes=ALIGN)
         ws = keep.tile([P, E * PASSES, N], U8, name="ws", align_bytes=ALIGN)
         qw = [ring.tile([P, Q_LOAD * PASSES, 2 * N], U8, name=f"qw{i}", align_bytes=ALIGN) for i in range(E // Q_LOAD)]
-        kw = [ring.tile([P, CHUNK * PASSES, N], I32, name=f"kw{i}", align_bytes=ALIGN) for i in range(E // CHUNK)]
+        kw = [[ring.tile([P, K_LOAD * PASSES, P], I32, name=f"kw{b}_{i}", align_bytes=ALIGN) for i in range(E // K_LOAD)] for b in range(2)]
         bias_sb = keep.tile([P, BLOCKS, E], F32, name="bias_sb")
         gate_rows = keep.tile([P, TOP, P], F32, name="gate_rows")
-        gate_col = keep.tile([P, TOP * TOKEN_PIECES], F32, name="gate_col")
+        gate_col = keep.tile([P, TOP * PIECES], F32, name="gate_col")
         gate_sb = [keep.tile([P, T], F32, name=f"gate_sb{r}") for r in range(TOP)]
         ident = keep.tile([P, P], F32, name="ident")
-        gw = [[keep.tile([P, CHUNK * C], U32, name=f"gw{s}_{c}", align_bytes=ALIGN) for c in range(E // CHUNK)] for s in range(PASSES)]
+        gw = [[keep.tile([P, CHUNK * C], U32, name=f"gw{s}_{c}", align_bytes=ALIGN) for c in range(CHUNKS)] for s in range(PASSES)]
         gs = [keep.tile([P, S], U8, name=f"gs{s}", align_bytes=ALIGN) for s in range(PASSES)]
         raw, staged, quantised, y = {}, {}, {}, {}
+        last = E - 1
 
         nc.vector.memset(ws[:].rearrange("p s t -> p (s t)").bitcast(I32), 0)
         nc.gpsimd.memset(xs[:].rearrange("p s t -> p (s t)").bitcast(I32), 0)
@@ -68,100 +73,78 @@ def tile_moe_qkv_kernel(tc, x_words, x_scales, wq_words, wq_scales, wk_words, wk
         make_identity(nc, ident[:])
 
         def load_v(e):
-            raw[e] = ring.tile([P, PASSES, PACK * N], F32, name="raw", tag=f"raw{e}", align_bytes=ALIGN)
-            nc.sync.dma_start(out=raw[e][:], in_=wv[e].rearrange("(s p j) n -> p s (j n)", s=PASSES, j=PACK))
+            both = ring.tile([P, PASSES, PACK * N], F32, name="raw", tag=f"raw{e}", align_bytes=ALIGN)
+            nc.sync.dma_start(out=both[:], in_=wv[e].rearrange("(s p j) n -> p s (j n)", s=PASSES, j=PACK))
+            for s in range(PASSES):
+                raw[e, s] = both[:, s, :]
 
         def load_v_pass(e, s):
-            raw[e, s] = ring.tile([P, PACK * N], F32, name="rawp", tag=f"raw{e}_{s}", align_bytes=ALIGN)
+            one = ring.tile([P, PACK * N], F32, name="rawp", tag=f"raw{e}_{s}", align_bytes=ALIGN)
             rows = wv[e, PASS_ROWS * s : PASS_ROWS * (s + 1), :]
-            nc.sync.dma_start(out=raw[e, s][:], in_=rows.rearrange("(p j) n -> p (j n)", j=PACK))
+            nc.sync.dma_start(out=one[:], in_=rows.rearrange("(p j) n -> p (j n)", j=PACK))
+            raw[e, s] = one[:]
 
         def load_q(i):
             words = wq_words[Q_LOAD * i : Q_LOAD * (i + 1)].rearrange("e s p w -> p (e s) w")
             nc.sync.dma_start(out=qw[i][:].bitcast(I32), in_=words.bitcast(I32))
 
-        def load_k(i):
-            words = wk_words[CHUNK * i : CHUNK * (i + 1)].rearrange("e s p n d -> p (e s) (n d)")
-            nc.sync.dma_start(out=kw[i][:], in_=words.bitcast(I32))
+        def load_k(b, i):
+            words = wk_words[K_LOAD * i : K_LOAD * (i + 1), :, :, b * P : (b + 1) * P, :].rearrange("e s p n d -> p (e s) (n d)")
+            nc.sync.dma_start(out=kw[b][i][:], in_=words.bitcast(I32))
 
         q_rows = wq_scales.rearrange("e s (q r) n -> r q (e s) n", r=PACK)
         k_rows = wk_scales.rearrange("e s (q r) n -> r q (e s) n", r=PACK)
-
-        def load_q_scales(r, queue):
-            queue.dma_start(out=ws[r:P:QUADRANT].bitcast(I32), in_=q_rows[r].bitcast(I32))
-
-        def load_k_scales(r, queue):
-            queue.dma_start(out=ws[K_PLANE + r : P : QUADRANT].bitcast(I32), in_=k_rows[r].bitcast(I32))
-
-        def load_x_scales(r):
-            rows = x_scales.rearrange("s (q r) t -> r q s t", r=PACK)[r]
-            nc.sync.dma_start(out=xs[r:P:QUADRANT].bitcast(I32), in_=rows.bitcast(I32))
-
-        def load_x_words():
-            nc.sync.dma_start(out=xw[:], in_=x_words.rearrange("s p t d -> p s (t d)").bitcast(I32))
-
-        def load_bias(queue):
-            queue.dma_start(out=bias_sb[:], in_=bias.rearrange("(b n) e -> n b e", n=P))
-
-        def load_gate(queue):
-            queue.dma_start(out=gate_rows[0 : TOKEN_PIECES * PORT : PORT], in_=gate[:, 0, :].rearrange("r (c t) -> c r t", t=P))
+        x_rows = x_scales.rearrange("s (q r) t -> r q s t", r=PACK)
 
         nc.sync.dma_start(offs_sb[:], offs)
-        load_x_words()
+        nc.sync.dma_start(out=xw[:], in_=x_words.rearrange("s p t d -> p s (t d)").bitcast(I32))
         for r in range(PACK):
-            load_x_scales(r)
+            nc.sync.dma_start(out=xs[r:P:QUADRANT].bitcast(I32), in_=x_rows[r].bitcast(I32))
         for r in range(PACK):
-            load_q_scales(r, nc.sync)
+            nc.sync.dma_start(out=ws[r:P:QUADRANT].bitcast(I32), in_=q_rows[r].bitcast(I32))
             if r == 1:
-                load_gate(nc.sync)
-            load_k_scales(r, nc.sync)
+                nc.sync.dma_start(out=gate_rows[0 : PIECES * PORT : PORT], in_=gate[:, 0, :].rearrange("r (c t) -> c r t", t=P))
+            nc.sync.dma_start(out=ws[K_PLANE + r : P : QUADRANT].bitcast(I32), in_=k_rows[r].bitcast(I32))
         load_q(0)
-        load_bias(nc.sync)
+        nc.sync.dma_start(out=bias_sb[:], in_=bias.rearrange("(b n) e -> n b e", n=P))
         load_v(0)
         load_q(1)
         for r, pos in enumerate((pos1, pos2, pos3)):
             nc.sync.dma_start(pos_sb[r][:], pos)
-        load_v(1)
-        for i in range(E // CHUNK):
-            load_k(i)
-        for e in range(2, WHOLE):
+        for e in range(1, last):
             load_v(e)
         for s in range(PASSES):
-            load_v_pass(WHOLE, s)
+            load_v_pass(last, s)
+        for b in range(2):
+            for i in range(E // K_LOAD):
+                load_k(b, i)
 
         def bank(which):
             return psum.tile([P, PACK, P], F32, name="bank", tag=f"bank{which}", offset=which * BANK_BYTES)
-
-        def two_banks(first):
-            both = psum.tile([P, 2 * PACK, P], F32, name="both", tag=f"both{first}", offset=first * BANK_BYTES)
-            return [(both[:, 0:PACK, :], 2), (both[:, PACK : 2 * PACK, :], 2)]
 
         def columns(first, count):
             return slice(first, first + count), slice(first // OFFSETS_A_COLUMN, (first + count) // OFFSETS_A_COLUMN)
 
         def gate_column(r, c):
-            return gate_col[:, TOKEN_PIECES * r + c : TOKEN_PIECES * r + c + 1]
+            return gate_col[:, PIECES * r + c : PIECES * r + c + 1]
 
         def spread_gate():
-            acc = bank(4)
+            acc = bank(0)
             for r in range(TOP):
                 nc.tensor.transpose(acc[:, r, :], gate_rows[:, r, :], ident[:])
-            nc.scalar.copy(out=gate_col[:].rearrange("p (r c) -> p r c", c=TOKEN_PIECES), in_=acc[:, 0:TOP, 0 : TOKEN_PIECES * PORT : PORT])
+            nc.scalar.copy(out=gate_col[:].rearrange("p (r c) -> p r c", c=PIECES), in_=acc[:, 0:TOP, 0 : PIECES * PORT : PORT])
             for r in range(TOP):
-                acc = bank(5 + r)
-                for c in range(TOKEN_PIECES):
+                acc = bank(1 + r)
+                for c in range(PIECES):
                     nc.tensor.transpose(acc[:, c, :], gate_column(r, c).to_broadcast([P, P]), ident[:])
                 nc.scalar.copy(out=gate_sb[r][:], in_=acc[:].rearrange("p c t -> p (c t)"))
 
-        def gather_scales(c):
-            cols, entries = columns(c * CHUNK * C, CHUNK * C)
-            for s in range(PASSES):
-                nc.vector.tensor_copy(gs[s][:, cols], xs[:, s, :].indirect(offs_sb[:, entries]))
-
-        def gather_words(c):
+        def gather_tokens(c):
             cols, entries = columns(c * CHUNK * C, CHUNK * C)
             for s in range(PASSES):
                 nc.vector.tensor_copy(gw[s][c][:], xw[:, s, :].bitcast(U32).indirect(offs_sb[:, entries]))
+            for s in range(PASSES):
+                nc.vector.tensor_copy(gs[s][:, cols], xs[:, s, :].indirect(offs_sb[:, entries]))
 
         def project(sums, weights, which, on_vector=False):
             acc = bank(which)
@@ -179,151 +162,122 @@ def tile_moe_qkv_kernel(tc, x_words, x_scales, wq_words, wq_scales, wk_words, wk
                         stop=(s == PASSES - 1),
                     )
             for i, (e, blk) in enumerate(sums):
-                slots = slice(e * C, (e + 1) * C)
                 if on_vector:
-                    nc.vector.tensor_scalar_add(out=y[blk][:, slots], in0=acc[:, i, :], scalar1=bias_sb[:, blk, e : e + 1])
+                    nc.vector.tensor_scalar_add(out=y[blk][:, e * C : (e + 1) * C], in0=acc[:, i, :], scalar1=bias_sb[:, blk, e : e + 1])
                 else:
-                    nc.scalar.activation(out=y[blk][:, slots], in_=acc[:, i, :], func=IDENT, bias=bias_sb[:, blk, e : e + 1])
+                    nc.scalar.activation(out=y[blk][:, e * C : (e + 1) * C], in_=acc[:, i, :], func=IDENT, bias=bias_sb[:, blk, e : e + 1])
 
         def q_weights(e, s, b):
             words = qw[e // Q_LOAD][:, (e % Q_LOAD) * PASSES + s, b * 2 * P : (b + 1) * 2 * P]
             return words.bitcast(FP4X4), ws[:, e * PASSES + s, b * P : (b + 1) * P]
 
         def k_weights(e, s, b):
-            words = kw[e // CHUNK][:, (e % CHUNK) * PASSES + s, b * P : (b + 1) * P]
+            words = kw[b][e // K_LOAD][:, (e % K_LOAD) * PASSES + s, :]
             return words.bitcast(FP8X4), ws[K_PLANE:P, e * PASSES + s, b * P : (b + 1) * P]
 
         def v_weights(e, s, b):
-            if (e, s, b) in quantised:
-                codes, scales = quantised[e, s, b]
-                return codes[:].bitcast(FP8X4), scales[:]
-            codes, scales = quantised[e, s]
-            return codes[:, b * P : (b + 1) * P].bitcast(FP8X4), scales[:, b * P : (b + 1) * P]
-
-        def pair(first, blks):
-            return [(e, blk) for blk in blks for e in (first, first + 1)]
+            return quantised[e, s, b]
 
         def chunk(c, blk):
             return [(e, blk) for e in range(c * CHUNK, (c + 1) * CHUNK)]
 
-        def round_rows(key, dst, src, on_vector):
-            staged[key] = dst
+        def round_rows(e, s, halves, dst, on_scalar):
+            staged[e, s, halves] = dst
+            rows = raw[e, s].rearrange("p (j n) -> p j n", j=PACK)[:, :, halves[0] * P : (halves[-1] + 1) * P]
             dst = dst.rearrange("p (c i j) -> p c j i", i=WALK, j=PACK)
-            src = src.rearrange("p j (c i) -> p c j i", i=WALK)
-            if on_vector:
-                nc.vector.tensor_copy(out=dst, in_=src)
-            else:
+            src = rows.rearrange("p j (c i) -> p c j i", i=WALK)
+            if on_scalar:
                 nc.scalar.copy(out=dst, in_=src)
+            else:
+                nc.vector.tensor_copy(out=dst, in_=src)
 
-        def new_stage(width, room):
-            return ring.tile([P, PACK * width], BF16, name="staged", tag=room, align_bytes=ALIGN)
-
-        def round_piece(e, room, on_vector=True):
-            both = new_stage(PASSES * N, room)
+        def round_v(e, on_scalar):
+            both = ring.tile([P, PASSES, PACK * N], BF16, name="staged", tag="staged", bufs=STAGE_BUFS, align_bytes=ALIGN)
             for s in range(PASSES):
-                round_rows((e, s), both[:, s * PACK * N : (s + 1) * PACK * N], raw[e][:, s, :].rearrange("p (j n) -> p j n", j=PACK), on_vector)
+                round_rows(e, s, BOTH, both[:, s, :], on_scalar)
 
-        def quantise_rows(key):
-            width = staged[key].shape[1] // PACK
+        def quantise_rows(e, s, halves):
+            width = len(halves) * P
             codes = ring.tile([P, width], U32, name="codes", tag="codes", bufs=CODE_BUFS, align_bytes=ALIGN)
             scales = ring.tile([P, width], U8, name="scales", tag="scales", bufs=CODE_BUFS, align_bytes=ALIGN)
-            nc.vector.quantize_mx(out=codes[:].bitcast(FP8X4), scales=scales[:], in_=staged[key])
-            quantised[key] = (codes, scales)
+            nc.vector.quantize_mx(out=codes[:].bitcast(FP8X4), scales=scales[:], in_=staged[e, s, halves])
+            for i, b in enumerate(halves):
+                quantised[e, s, b] = (codes[:, i * P : (i + 1) * P].bitcast(FP8X4), scales[:, i * P : (i + 1) * P])
 
-        def quantise(e):
-            for s in range(PASSES):
-                quantise_rows((e, s))
-
-        def combine_on_vector(blk, first, count, room, stages=("stage0", "stage1")):
+        def combine_on_vector(blk, first, count, rooms):
             cols, entries = columns(first, count)
-            two = ring.tile([P, 2, count], F32, name="two", tag=stages[0], align_bytes=ALIGN)
-            third = ring.tile([P, count], F32, name="third", tag=stages[1], align_bytes=ALIGN)
-            parts = (two[:, 0, :], two[:, 1, :], third[:])
-            total = ring.tile([P, count], F32, name="total", tag=room, align_bytes=ALIGN)
+            parts = ring.tile([P, TOP, count], F32, name="parts", tag=rooms[0], align_bytes=ALIGN)
+            total = ring.tile([P, count], F32, name="total", tag=rooms[1], align_bytes=ALIGN)
             for r in range(TOP):
-                nc.vector.tensor_tensor(parts[r], y[blk][:].indirect(pos_sb[r][:, entries]), gate_sb[r][:, cols], MULT)
-            nc.vector.tensor_tensor(parts[0], parts[0], parts[1], ADD)
-            nc.vector.tensor_tensor(total[:], parts[0], parts[2], ADD)
+                nc.vector.tensor_tensor(parts[:, r, :], y[blk][:].indirect(pos_sb[r][:, entries]), gate_sb[r][:, cols], MULT)
+            nc.vector.tensor_tensor(parts[:, 0, :], parts[:, 0, :], parts[:, 1, :], ADD)
+            nc.vector.tensor_tensor(total[:], parts[:, 0, :], parts[:, 2, :], ADD)
             nc.sync.dma_start(out=out[blk * P : (blk + 1) * P, cols], in_=total[:])
 
-        def fetch_on_scalar(blk, first_piece, pieces, room):
+        def combine_on_scalar(blks, first_piece, pieces, width, rooms, turn_banks, sum_banks):
             count = pieces * P
-            parts = ring.tile([P, TOP, count], F32, name="parts", tag=room, align_bytes=ALIGN)
-            for first in range(0, count, 2 * P):
-                width = min(2 * P, count - first)
-                cols, entries = columns(first_piece * P + first, width)
+            parts = [ring.tile([P, TOP, count], F32, name="parts", tag=room, align_bytes=ALIGN) for room in rooms]
+            for first in range(0, count, width):
+                cols, entries = columns(first_piece * P + first, min(width, count - first))
                 for r in range(TOP):
-                    nc.scalar.activation(out=parts[:, r, first : first + width], in_=y[blk][:].indirect(pos_sb[r][:, entries]), func=COPY)
-            return parts
-
-        def weigh_turned(blk, first_piece, pieces, parts, turn_banks, sum_banks, queue):
-            scaled = ring.tile([P, pieces, TOP, P], F32, name="scaled", tag="scaled", bufs=1)
-            for c in range(pieces):
-                acc = bank(turn_banks[c])
+                    for i, blk in enumerate(blks):
+                        nc.scalar.activation(out=parts[i][:, r, first : first + width], in_=y[blk][:].indirect(pos_sb[r][:, entries]), func=COPY)
+            scaled = ring.tile([P, pieces, TOP, len(blks), P], F32, name="scaled", tag="scaled")
+            for c0 in range(0, pieces, 2):
+                group = min(2, pieces - c0)
                 for r in range(TOP):
-                    nc.tensor.transpose(acc[:, r, :], parts[:, r, c * P : (c + 1) * P], ident[:])
-                for r in range(TOP):
-                    nc.scalar.activation(out=scaled[:, c, r, :], in_=acc[:, r, :], func=COPY, scale=gate_column(r, first_piece + c))
-            done = 0
-            for acc, group in sum_banks():
-                for c in range(group):
+                    acc = bank(turn_banks[r])
+                    for c in range(group):
+                        for i in range(len(blks)):
+                            nc.tensor.transpose(acc[:, c * len(blks) + i, :], parts[i][:, r, (c0 + c) * P : (c0 + c + 1) * P], ident[:])
+                    for c in range(group):
+                        nc.scalar.activation(out=scaled[:, c0 + c, r, :, :], in_=acc[:, c * len(blks) : (c + 1) * len(blks), :], func=COPY, scale=gate_column(r, first_piece + c0 + c))
+            for which, i, c0, run in sum_banks:
+                acc = bank(which)
+                for c in range(run):
                     for r in range(TOP):
-                        nc.tensor.matmul(acc[:, c, :], scaled[:, done + c, r, :], ident[:], start=(r == 0), stop=(r == TOP - 1), is_transpose=True)
-                cols = slice(done * P, (done + group) * P)
-                nc.scalar.copy(out=parts[:, 0, cols], in_=acc[:, 0:group, :].rearrange("p c t -> p (c t)"))
-                first = (first_piece + done) * P
-                queue.dma_start(out=out[blk * P : (blk + 1) * P, first : first + group * P], in_=parts[:, 0, cols])
-                done += group
+                        nc.tensor.matmul(acc[:, c, :], scaled[:, c0 + c, r, i, :], ident[:], start=(r == 0), stop=(r == TOP - 1), is_transpose=True)
+                cols = slice(c0 * P, (c0 + run) * P)
+                nc.scalar.copy(out=parts[i][:, 0, cols], in_=acc[:, 0:run, :].rearrange("p c t -> p (c t)"))
+                first = (first_piece + c0) * P
+                nc.sync.dma_start(out=out[blks[i] * P : (blks[i] + 1) * P, first : first + run * P], in_=parts[i][:, 0, cols])
 
-        def combine_on_scalar(blk, first_piece, pieces, room, turn_banks, sum_banks, queue=nc.sync):
-            weigh_turned(blk, first_piece, pieces, fetch_on_scalar(blk, first_piece, pieces, room), turn_banks, sum_banks, queue)
-
-        for blk in range(4):
+        for blk in range(2):
             y[blk] = ring.tile([P, S], F32, name=f"y{blk}", align_bytes=ALIGN)
-        for c in range(E // CHUNK):
-            gather_words(c)
-            gather_scales(c)
+        for c in range(CHUNKS):
+            gather_tokens(c)
         spread_gate()
-        project(chunk(0, 0), q_weights, 5)
-        project(chunk(0, 1), q_weights, 6)
-        project(chunk(1, 0), q_weights, 7)
-        project(chunk(1, 1), q_weights, 4)
-        round_piece(0, "stage0", on_vector=False)
-        project(chunk(2, 0), q_weights, 0)
-        project(chunk(3, 0), q_weights, 2)
-        project(chunk(2, 1), q_weights, 1)
-        project(chunk(3, 1), q_weights, 3)
-        round_piece(1, "qw0", on_vector=False)
-        quantise(0)
-        combine_on_vector(0, 0, T, "total0", ("pair0", "third0"))
-        quantise(1)
-        combine_on_vector(1, 0, T, "total1", ("qw1", "stage0"))
-        for c in range(E // CHUNK):
+        for e in range(ROUND_ON_SCALAR):
+            round_v(e, True)
+        for c in range(CHUNKS):
             for b in range(2):
-                project(chunk(c, 2 + b), k_weights, (2, 3, 0, 1)[(2 * c + b) % 4])
-        combine_on_scalar(2, 0, TOKEN_PIECES, "kw0", (4, 5, 6, 7), lambda: two_banks(2))
+                project(chunk(c, b), q_weights, (4 + 2 * c + b) % 8)
         y[4] = ring.tile([P, S], F32, name="y4", tag="raw0", align_bytes=ALIGN)
         y[5] = ring.tile([P, S], F32, name="y5", tag="raw1", align_bytes=ALIGN)
-        project(pair(0, (4, 5)), v_weights, 2)
-        for e in range(2, WHOLE):
-            if e >= 2:
-                round_piece(e, ("qw1", "stage0")[e % 2])
-                quantise(e)
-            if e >= 8:
-                project([(e, 4), (e, 5)], v_weights, (0, 1, 2)[e - 8])
-            elif e % 2:
-                project(pair(e - 1, (4, 5)), v_weights, (2, 3, 2, 3)[e // 2])
-            if e == 3:
-                combine_on_scalar(3, 0, TOKEN_PIECES, "kw1", (4, 5, 6, 7), lambda: two_banks(0))
-        last = E - 1
-        rows = [raw[last, s][:].rearrange("p (j n) -> p j n", j=PACK) for s in range(PASSES)]
-        round_rows((last, 0), new_stage(N, "raw8")[:], rows[0], False)
-        round_rows((last, 1, 1), new_stage(P, "stage0")[:], rows[1][:, :, P:N], True)
-        round_rows((last, 1, 0), new_stage(P, "raw9")[:], rows[1][:, :, 0:P], False)
-        for key in ((last, 0), (last, 1, 1), (last, 1, 0)):
-            quantise_rows(key)
-        project([(last, 5)], v_weights, 6, on_vector=True)
-        project([(last, 4)], v_weights, 7)
-        combine_on_scalar(4, 0, TOKEN_PIECES - 1, "kw2", (4, 5, 6), lambda: [(bank(0), 2), (bank(1), 1)], nc.scalar)
-        combine_on_vector(5, 0, T, "kw3", ("raw4", "raw3"))
-        combine_on_vector(4, T - P, P, "raw5", ("raw6", "raw7"))
+        for e in range(last):
+            if e >= ROUND_ON_SCALAR:
+                round_v(e, False)
+            for s in range(PASSES):
+                quantise_rows(e, s, BOTH)
+            project([(e, 4), (e, 5)], v_weights, (3, 2, 1)[e % 3])
+        combine_on_scalar((0, 1), 0, PIECES, T, ("qw0", "qw1"), (4, 5, 6), [(7, 0, 0, PIECES), (0, 1, 0, PIECES)])
+        ends = ring.tile([P, PASSES, PACK * N], BF16, name="staged", tag="staged", bufs=STAGE_BUFS, align_bytes=ALIGN)
+        round_rows(last, 0, BOTH, ends[:, 0, :], False)
+        round_rows(last, 1, (0,), ends[:, 1, 0 : PACK * P], False)
+        round_rows(last, 1, (1,), ends[:, 1, PACK * P : PACK * N], True)
+        quantise_rows(last, 0, BOTH)
+        quantise_rows(last, 1, (0,))
+        quantise_rows(last, 1, (1,))
+        project([(last, 4)], v_weights, 1, on_vector=True)
+        project([(last, 5)], v_weights, 7)
+        y[2] = ring.tile([P, S], F32, name="y2", tag="raw2", align_bytes=ALIGN)
+        y[3] = ring.tile([P, S], F32, name="y3", tag="raw3", align_bytes=ALIGN)
+        for i in range(E // K_LOAD):
+            project([(e, 2) for e in range(i * K_LOAD, (i + 1) * K_LOAD)], k_weights, (4, 5, 6)[i])
+        combine_on_vector(4, 0, T, ("raw4", "raw5"))
+        combine_on_vector(5, 0, T, ("raw6", "raw7"))
+        for i in range(E // K_LOAD):
+            project([(e, 3) for e in range(i * K_LOAD, (i + 1) * K_LOAD)], k_weights, (7, 4, 5)[i])
+        combine_on_scalar((2,), 0, 4, 2 * P, ("raw10",), (0, 1, 2), [(3, 0, 0, 2), (6, 0, 2, 2)])
+        combine_on_vector(3, 0, 2 * P, ("raw8", "raw9"))
+        combine_on_vector(3, 2 * P, 2 * P, ("raw11_1", "raw11_0"))

@@ -30,15 +30,17 @@ PIECES = T // P
 OFFSETS_A_COLUMN = 16
 ALIGN = 64
 K_PLANE = 4
+BYTE_WINDOW = 2048
+HALF = S // 2
+HALF_BYTES = 4 * HALF
 CHUNK = 3
 CHUNKS = E // CHUNK
 Q_LOAD = 6
-K_LOAD = 4
 WALK = 4
 BOTH = (0, 1)
 ROUND_ON_SCALAR = 1
-STAGE_BUFS = 3
-CODE_BUFS = 12
+STAGE_BUFS = 2
+CODE_BUFS = 10
 PORT = 4
 BANK_BYTES = 2048
 
@@ -48,29 +50,33 @@ def tile_moe_qkv_kernel(tc, x_words, x_scales, wq_words, wq_scales, wk_words, wk
     with ExitStack() as ctx:
         keep = ctx.enter_context(tc.tile_pool(name="keep", bufs=1))
         ring = ctx.enter_context(tc.tile_pool(name="ring", bufs=1))
+        tok = ctx.enter_context(tc.tile_pool(name="tok", bufs=1))
         psum = ctx.enter_context(tc.psum_pool(name="psum", bufs=1))
 
         offs_sb = keep.tile([P, S // OFFSETS_A_COLUMN], U16, name="offs_sb")
         pos_sb = [keep.tile([P, T // OFFSETS_A_COLUMN], U16, name=f"pos_sb{r}") for r in range(TOP)]
-        xw = keep.tile([P, PASSES, T], I32, name="xw", align_bytes=ALIGN)
-        xs = keep.tile([P, PASSES, T], U8, name="xs", align_bytes=ALIGN)
+        xw = keep.tile([P, (PASSES + 1) * T], I32, name="xw", align_bytes=ALIGN)
+        xs = tok.tile([P, BYTE_WINDOW], U8, name="xs", align_bytes=ALIGN, offset=2 * HALF_BYTES - ALIGN)
         ws = keep.tile([P, E * PASSES, N], U8, name="ws", align_bytes=ALIGN)
         qw = [ring.tile([P, Q_LOAD * PASSES, 2 * N], U8, name=f"qw{i}", align_bytes=ALIGN) for i in range(E // Q_LOAD)]
-        kw = [[ring.tile([P, K_LOAD * PASSES, P], I32, name=f"kw{b}_{i}", align_bytes=ALIGN) for i in range(E // K_LOAD)] for b in range(2)]
+        kw = [ring.tile([P, CHUNK * PASSES, N], I32, name=f"kw{i}", align_bytes=ALIGN) for i in range(CHUNKS)]
         bias_sb = keep.tile([P, BLOCKS, E], F32, name="bias_sb")
         gate_rows = keep.tile([P, TOP, P], F32, name="gate_rows")
         gate_col = keep.tile([P, TOP * PIECES], F32, name="gate_col")
         gate_sb = [keep.tile([P, T], F32, name=f"gate_sb{r}") for r in range(TOP)]
         ident = keep.tile([P, P], F32, name="ident")
-        gw = [[keep.tile([P, CHUNK * C], U32, name=f"gw{s}_{c}", align_bytes=ALIGN) for c in range(CHUNKS)] for s in range(PASSES)]
-        gs = [keep.tile([P, S], U8, name=f"gs{s}", align_bytes=ALIGN) for s in range(PASSES)]
+        gs = keep.tile([P, S], U8, name="gs", align_bytes=ALIGN)
+        gs_moved = keep.tile([P, S], U8, name="gs_moved", align_bytes=ALIGN)
+        gw = {}
         raw, staged, quantised, y = {}, {}, {}, {}
         last = E - 1
 
         nc.vector.memset(ws[:].rearrange("p s t -> p (s t)").bitcast(I32), 0)
-        nc.gpsimd.memset(xs[:].rearrange("p s t -> p (s t)").bitcast(I32), 0)
-        nc.gpsimd.memset(gate_rows[:].rearrange("c r t -> c (r t)"), 0.0)
+        nc.gpsimd.memset(xs[:].bitcast(I32), 0)
         make_identity(nc, ident[:])
+        nc.vector.memset(gate_rows[:].rearrange("c r t -> c (r t)"), 0.0)
+        nc.vector.memset(gs_moved[:].bitcast(I32), 0)
+        nc.vector.memset(xw[:, PASSES * T :], 0)
 
         def load_v(e):
             both = ring.tile([P, PASSES, PACK * N], F32, name="raw", tag=f"raw{e}", align_bytes=ALIGN)
@@ -88,18 +94,26 @@ def tile_moe_qkv_kernel(tc, x_words, x_scales, wq_words, wq_scales, wk_words, wk
             words = wq_words[Q_LOAD * i : Q_LOAD * (i + 1)].rearrange("e s p w -> p (e s) w")
             nc.sync.dma_start(out=qw[i][:].bitcast(I32), in_=words.bitcast(I32))
 
-        def load_k(b, i):
-            words = wk_words[K_LOAD * i : K_LOAD * (i + 1), :, :, b * P : (b + 1) * P, :].rearrange("e s p n d -> p (e s) (n d)")
-            nc.sync.dma_start(out=kw[b][i][:], in_=words.bitcast(I32))
+        def load_k(i):
+            words = wk_words[CHUNK * i : CHUNK * (i + 1)].rearrange("e s p n d -> p (e s) (n d)")
+            nc.sync.dma_start(out=kw[i][:], in_=words.bitcast(I32))
 
         q_rows = wq_scales.rearrange("e s (q r) n -> r q (e s) n", r=PACK)
         k_rows = wk_scales.rearrange("e s (q r) n -> r q (e s) n", r=PACK)
-        x_rows = x_scales.rearrange("s (q r) t -> r q s t", r=PACK)
+        x_rows = x_scales.rearrange("s (q r) t -> q s r t", r=PACK)
+
+        def columns(first, count):
+            return slice(first, first + count), slice(first // OFFSETS_A_COLUMN, (first + count) // OFFSETS_A_COLUMN)
+
+        def gather_words(s, h, dst):
+            gw[s, h] = dst
+            window = xw[:, s * T : (s + PASSES) * T].bitcast(U32)
+            nc.vector.tensor_copy(dst, window.indirect(offs_sb[:, columns(h * HALF, HALF)[1]]))
 
         nc.sync.dma_start(offs_sb[:], offs)
-        nc.sync.dma_start(out=xw[:], in_=x_words.rearrange("s p t d -> p s (t d)").bitcast(I32))
-        for r in range(PACK):
-            nc.sync.dma_start(out=xs[r:P:QUADRANT].bitcast(I32), in_=x_rows[r].bitcast(I32))
+        nc.sync.dma_start(out=xw[:, 0 : PASSES * T].rearrange("p (s t) -> p s t", s=PASSES), in_=x_words.rearrange("s p t d -> p s (t d)").bitcast(I32))
+        for q in range(P // QUADRANT):
+            nc.sync.dma_start(out=xs[q * QUADRANT : q * QUADRANT + PASSES * PACK, 0:T].bitcast(I32), in_=x_rows[q].bitcast(I32))
         for r in range(PACK):
             nc.sync.dma_start(out=ws[r:P:QUADRANT].bitcast(I32), in_=q_rows[r].bitcast(I32))
             if r == 1:
@@ -108,22 +122,29 @@ def tile_moe_qkv_kernel(tc, x_words, x_scales, wq_words, wq_scales, wk_words, wk
         load_q(0)
         nc.sync.dma_start(out=bias_sb[:], in_=bias.rearrange("(b n) e -> n b e", n=P))
         load_v(0)
+        nc.vector.tensor_copy(gs[:], xs[:].indirect(offs_sb[:]))
+        early = keep.tile([P, HALF], U32, name="gw_early", align_bytes=ALIGN)
+        below = tok.tile([P, S], U32, name="gw_below", align_bytes=ALIGN, offset=0)
+        above = tok.tile([P, HALF], U32, name="gw_above", align_bytes=ALIGN, offset=2 * HALF_BYTES + BYTE_WINDOW - 2 * ALIGN)
+        gather_words(0, 0, early[:])
+        gather_words(1, 0, below[:, 0:HALF])
+        gather_words(0, 1, above[:])
+        gather_words(1, 1, below[:, HALF:S])
+        for r in range(PACK):
+            nc.sync.dma_start(out=gs_moved[r:P:QUADRANT].bitcast(I32), in_=gs[PACK + r : P : QUADRANT].bitcast(I32))
         load_q(1)
+        load_v(1)
         for r, pos in enumerate((pos1, pos2, pos3)):
             nc.sync.dma_start(pos_sb[r][:], pos)
-        for e in range(1, last):
+        for i in range(CHUNKS):
+            load_k(i)
+        for e in range(2, last):
             load_v(e)
         for s in range(PASSES):
             load_v_pass(last, s)
-        for b in range(2):
-            for i in range(E // K_LOAD):
-                load_k(b, i)
 
         def bank(which):
             return psum.tile([P, PACK, P], F32, name="bank", tag=f"bank{which}", offset=which * BANK_BYTES)
-
-        def columns(first, count):
-            return slice(first, first + count), slice(first // OFFSETS_A_COLUMN, (first + count) // OFFSETS_A_COLUMN)
 
         def gate_column(r, c):
             return gate_col[:, PIECES * r + c : PIECES * r + c + 1]
@@ -139,25 +160,23 @@ def tile_moe_qkv_kernel(tc, x_words, x_scales, wq_words, wq_scales, wk_words, wk
                     nc.tensor.transpose(acc[:, c, :], gate_column(r, c).to_broadcast([P, P]), ident[:])
                 nc.scalar.copy(out=gate_sb[r][:], in_=acc[:].rearrange("p c t -> p (c t)"))
 
-        def gather_tokens(c):
-            cols, entries = columns(c * CHUNK * C, CHUNK * C)
-            for s in range(PASSES):
-                nc.vector.tensor_copy(gw[s][c][:], xw[:, s, :].bitcast(U32).indirect(offs_sb[:, entries]))
-            for s in range(PASSES):
-                nc.vector.tensor_copy(gs[s][:, cols], xs[:, s, :].indirect(offs_sb[:, entries]))
+        def token_scales(blk, s):
+            if s == 0:
+                return gs[:]
+            return gs_moved[:] if blk < 2 else gs[PACK:P]
 
         def project(sums, weights, which, on_vector=False):
             acc = bank(which)
             for i, (e, blk) in enumerate(sums):
-                c, u = divmod(e, CHUNK)
+                h, u = divmod(e, E // 2)
                 for s in range(PASSES):
                     words, scales = weights(e, s, blk % 2)
                     nc.tensor.matmul_mx(
                         out=acc[:, i, :],
                         lhsT=words,
                         lhsT_scale=scales,
-                        rhs=gw[s][c][:, u * C : (u + 1) * C].bitcast(FP8X4),
-                        rhs_scale=gs[s][:, e * C : (e + 1) * C],
+                        rhs=gw[s, h][:, u * C : (u + 1) * C].bitcast(FP8X4),
+                        rhs_scale=token_scales(blk, s)[:, e * C : (e + 1) * C],
                         start=(s == 0),
                         stop=(s == PASSES - 1),
                     )
@@ -172,7 +191,7 @@ def tile_moe_qkv_kernel(tc, x_words, x_scales, wq_words, wq_scales, wk_words, wk
             return words.bitcast(FP4X4), ws[:, e * PASSES + s, b * P : (b + 1) * P]
 
         def k_weights(e, s, b):
-            words = kw[b][e // K_LOAD][:, (e % K_LOAD) * PASSES + s, :]
+            words = kw[e // CHUNK][:, (e % CHUNK) * PASSES + s, b * P : (b + 1) * P]
             return words.bitcast(FP8X4), ws[K_PLANE:P, e * PASSES + s, b * P : (b + 1) * P]
 
         def v_weights(e, s, b):
@@ -218,10 +237,11 @@ def tile_moe_qkv_kernel(tc, x_words, x_scales, wq_words, wq_scales, wk_words, wk
             count = pieces * P
             parts = [ring.tile([P, TOP, count], F32, name="parts", tag=room, align_bytes=ALIGN) for room in rooms]
             for first in range(0, count, width):
-                cols, entries = columns(first_piece * P + first, min(width, count - first))
+                run = min(width, count - first)
+                entries = columns(first_piece * P + first, run)[1]
                 for r in range(TOP):
                     for i, blk in enumerate(blks):
-                        nc.scalar.activation(out=parts[i][:, r, first : first + width], in_=y[blk][:].indirect(pos_sb[r][:, entries]), func=COPY)
+                        nc.scalar.activation(out=parts[i][:, r, first : first + run], in_=y[blk][:].indirect(pos_sb[r][:, entries]), func=COPY)
             scaled = ring.tile([P, pieces, TOP, len(blks), P], F32, name="scaled", tag="scaled")
             for c0 in range(0, pieces, 2):
                 group = min(2, pieces - c0)
@@ -242,42 +262,42 @@ def tile_moe_qkv_kernel(tc, x_words, x_scales, wq_words, wq_scales, wk_words, wk
                 first = (first_piece + c0) * P
                 nc.sync.dma_start(out=out[blks[i] * P : (blks[i] + 1) * P, first : first + run * P], in_=parts[i][:, 0, cols])
 
-        for blk in range(2):
+        for blk in range(4):
             y[blk] = ring.tile([P, S], F32, name=f"y{blk}", align_bytes=ALIGN)
-        for c in range(CHUNKS):
-            gather_tokens(c)
         spread_gate()
-        for e in range(ROUND_ON_SCALAR):
-            round_v(e, True)
-        for c in range(CHUNKS):
-            for b in range(2):
-                project(chunk(c, b), q_weights, (4 + 2 * c + b) % 8)
+        for b in range(2):
+            for c in range(CHUNKS):
+                project(chunk(c, b), q_weights, (4 + CHUNKS * b + c) % 8)
         y[4] = ring.tile([P, S], F32, name="y4", tag="raw0", align_bytes=ALIGN)
         y[5] = ring.tile([P, S], F32, name="y5", tag="raw1", align_bytes=ALIGN)
-        for e in range(last):
-            if e >= ROUND_ON_SCALAR:
-                round_v(e, False)
+
+        def prepare_v(e):
+            round_v(e, e == ROUND_ON_SCALAR)
             for s in range(PASSES):
                 quantise_rows(e, s, BOTH)
-            project([(e, 4), (e, 5)], v_weights, (3, 2, 1)[e % 3])
-        combine_on_scalar((0, 1), 0, PIECES, T, ("qw0", "qw1"), (4, 5, 6), [(7, 0, 0, PIECES), (0, 1, 0, PIECES)])
+
+        prepare_v(0)
+        combine_on_vector(0, 0, T, ("parts0", "total0"))
+        prepare_v(1)
+        combine_on_vector(1, 0, T, ("qw0", "total1"))
+        for c in range(CHUNKS):
+            for b in range(2):
+                project(chunk(c, 2 + b), k_weights, (2 * c + b) % 4)
+        for e in range(last):
+            if e == 2:
+                combine_on_scalar((2, 3), 0, PIECES, T, ("kw0", "kw1"), (4, 5, 6), [(7, 0, 0, PIECES), (0, 1, 0, PIECES)])
+            if e >= 2:
+                prepare_v(e)
+            project([(e, 4), (e, 5)], v_weights, (3, 2)[e] if e < 2 else (2, 1, 3)[e % 3 - 3])
         ends = ring.tile([P, PASSES, PACK * N], BF16, name="staged", tag="staged", bufs=STAGE_BUFS, align_bytes=ALIGN)
-        round_rows(last, 0, BOTH, ends[:, 0, :], False)
-        round_rows(last, 1, (0,), ends[:, 1, 0 : PACK * P], False)
-        round_rows(last, 1, (1,), ends[:, 1, PACK * P : PACK * N], True)
+        round_rows(last, 0, BOTH, ends[:, 0, :], True)
+        round_rows(last, 1, (1,), ends[:, 1, PACK * P : PACK * N], False)
+        round_rows(last, 1, (0,), ends[:, 1, 0 : PACK * P], True)
         quantise_rows(last, 0, BOTH)
-        quantise_rows(last, 1, (0,))
         quantise_rows(last, 1, (1,))
-        project([(last, 4)], v_weights, 1, on_vector=True)
-        project([(last, 5)], v_weights, 7)
-        y[2] = ring.tile([P, S], F32, name="y2", tag="raw2", align_bytes=ALIGN)
-        y[3] = ring.tile([P, S], F32, name="y3", tag="raw3", align_bytes=ALIGN)
-        for i in range(E // K_LOAD):
-            project([(e, 2) for e in range(i * K_LOAD, (i + 1) * K_LOAD)], k_weights, (4, 5, 6)[i])
-        combine_on_vector(4, 0, T, ("raw4", "raw5"))
-        combine_on_vector(5, 0, T, ("raw6", "raw7"))
-        for i in range(E // K_LOAD):
-            project([(e, 3) for e in range(i * K_LOAD, (i + 1) * K_LOAD)], k_weights, (7, 4, 5)[i])
-        combine_on_scalar((2,), 0, 4, 2 * P, ("raw10",), (0, 1, 2), [(3, 0, 0, 2), (6, 0, 2, 2)])
-        combine_on_vector(3, 0, 2 * P, ("raw8", "raw9"))
-        combine_on_vector(3, 2 * P, 2 * P, ("raw11_1", "raw11_0"))
+        quantise_rows(last, 1, (0,))
+        project([(last, 5)], v_weights, 6, on_vector=True)
+        project([(last, 4)], v_weights, 7)
+        combine_on_scalar((4,), 0, PIECES - 1, 2 * P, ("kw2",), (4, 5, 1), [(0, 0, 0, 2), (2, 0, 2, 1)])
+        combine_on_vector(5, 0, T, ("raw4", "kw3"))
+        combine_on_vector(4, T - P, P, ("raw6", "raw5"))

@@ -38,7 +38,6 @@ CHUNKS = E // CHUNK
 Q_LOAD = 6
 WALK = 4
 BOTH = (0, 1)
-ROUND_ON_SCALAR = 1
 STAGE_BUFS = 2
 CODE_BUFS = 10
 PORT = 4
@@ -78,9 +77,9 @@ def tile_moe_qkv_kernel(tc, x_words, x_scales, wq_words, wq_scales, wk_words, wk
         nc.vector.memset(gs_moved[:].bitcast(I32), 0)
         nc.vector.memset(xw[:, PASSES * T :], 0)
 
-        def load_v(e):
+        def load_v(e, queue=nc.sync):
             both = ring.tile([P, PASSES, PACK * N], F32, name="raw", tag=f"raw{e}", align_bytes=ALIGN)
-            nc.sync.dma_start(out=both[:], in_=wv[e].rearrange("(s p j) n -> p s (j n)", s=PASSES, j=PACK))
+            queue.dma_start(out=both[:], in_=wv[e].rearrange("(s p j) n -> p s (j n)", s=PASSES, j=PACK))
             for s in range(PASSES):
                 raw[e, s] = both[:, s, :]
 
@@ -94,9 +93,9 @@ def tile_moe_qkv_kernel(tc, x_words, x_scales, wq_words, wq_scales, wk_words, wk
             words = wq_words[Q_LOAD * i : Q_LOAD * (i + 1)].rearrange("e s p w -> p (e s) w")
             nc.sync.dma_start(out=qw[i][:].bitcast(I32), in_=words.bitcast(I32))
 
-        def load_k(i):
+        def load_k(i, queue=nc.sync):
             words = wk_words[CHUNK * i : CHUNK * (i + 1)].rearrange("e s p n d -> p (e s) (n d)")
-            nc.sync.dma_start(out=kw[i][:], in_=words.bitcast(I32))
+            queue.dma_start(out=kw[i][:], in_=words.bitcast(I32))
 
         q_rows = wq_scales.rearrange("e s (q r) n -> r q (e s) n", r=PACK)
         k_rows = wk_scales.rearrange("e s (q r) n -> r q (e s) n", r=PACK)
@@ -121,7 +120,7 @@ def tile_moe_qkv_kernel(tc, x_words, x_scales, wq_words, wq_scales, wk_words, wk
             nc.sync.dma_start(out=ws[K_PLANE + r : P : QUADRANT].bitcast(I32), in_=k_rows[r].bitcast(I32))
         load_q(0)
         nc.sync.dma_start(out=bias_sb[:], in_=bias.rearrange("(b n) e -> n b e", n=P))
-        load_v(0)
+        load_q(1)
         nc.vector.tensor_copy(gs[:], xs[:].indirect(offs_sb[:]))
         early = keep.tile([P, HALF], U32, name="gw_early", align_bytes=ALIGN)
         below = tok.tile([P, S], U32, name="gw_below", align_bytes=ALIGN, offset=0)
@@ -132,13 +131,13 @@ def tile_moe_qkv_kernel(tc, x_words, x_scales, wq_words, wq_scales, wk_words, wk
         gather_words(1, 1, below[:, HALF:S])
         for r in range(PACK):
             nc.sync.dma_start(out=gs_moved[r:P:QUADRANT].bitcast(I32), in_=gs[PACK + r : P : QUADRANT].bitcast(I32))
-        load_q(1)
-        load_v(1)
+        load_v(0)
+        load_k(0)
         for r, pos in enumerate((pos1, pos2, pos3)):
             nc.sync.dma_start(pos_sb[r][:], pos)
-        for i in range(CHUNKS):
+        for i in range(1, CHUNKS):
             load_k(i)
-        for e in range(2, last):
+        for e in range(1, last):
             load_v(e)
         for s in range(PASSES):
             load_v_pass(last, s)
@@ -223,17 +222,24 @@ def tile_moe_qkv_kernel(tc, x_words, x_scales, wq_words, wq_scales, wk_words, wk
             for i, b in enumerate(halves):
                 quantised[e, s, b] = (codes[:, i * P : (i + 1) * P].bitcast(FP8X4), scales[:, i * P : (i + 1) * P])
 
-        def combine_on_vector(blk, first, count, rooms):
+        def weigh_on_vector(blk, first, count, room):
             cols, entries = columns(first, count)
-            parts = ring.tile([P, TOP, count], F32, name="parts", tag=rooms[0], align_bytes=ALIGN)
-            total = ring.tile([P, count], F32, name="total", tag=rooms[1], align_bytes=ALIGN)
+            parts = ring.tile([P, TOP, count], F32, name="parts", tag=room, align_bytes=ALIGN)
             for r in range(TOP):
                 nc.vector.tensor_tensor(parts[:, r, :], y[blk][:].indirect(pos_sb[r][:, entries]), gate_sb[r][:, cols], MULT)
             nc.vector.tensor_tensor(parts[:, 0, :], parts[:, 0, :], parts[:, 1, :], ADD)
-            nc.vector.tensor_tensor(total[:], parts[:, 0, :], parts[:, 2, :], ADD)
-            nc.sync.dma_start(out=out[blk * P : (blk + 1) * P, cols], in_=total[:])
+            return parts
 
-        def combine_on_scalar(blks, first_piece, pieces, width, rooms, turn_banks, sum_banks):
+        def finish_on_vector(blk, first, parts, room):
+            count = parts.shape[2]
+            total = ring.tile([P, count], F32, name="total", tag=room, align_bytes=ALIGN)
+            nc.vector.tensor_tensor(total[:], parts[:, 0, :], parts[:, 2, :], ADD)
+            nc.sync.dma_start(out=out[blk * P : (blk + 1) * P, first : first + count], in_=total[:])
+
+        def combine_on_vector(blk, first, count, rooms):
+            finish_on_vector(blk, first, weigh_on_vector(blk, first, count, rooms[0]), rooms[1])
+
+        def combine_on_scalar(blks, first_piece, pieces, width, rooms, turn_banks, sum_banks, queue=nc.sync):
             count = pieces * P
             parts = [ring.tile([P, TOP, count], F32, name="parts", tag=room, align_bytes=ALIGN) for room in rooms]
             for first in range(0, count, width):
@@ -243,15 +249,13 @@ def tile_moe_qkv_kernel(tc, x_words, x_scales, wq_words, wq_scales, wk_words, wk
                     for i, blk in enumerate(blks):
                         nc.scalar.activation(out=parts[i][:, r, first : first + run], in_=y[blk][:].indirect(pos_sb[r][:, entries]), func=COPY)
             scaled = ring.tile([P, pieces, TOP, len(blks), P], F32, name="scaled", tag="scaled")
-            for c0 in range(0, pieces, 2):
-                group = min(2, pieces - c0)
-                for r in range(TOP):
-                    acc = bank(turn_banks[r])
-                    for c in range(group):
-                        for i in range(len(blks)):
-                            nc.tensor.transpose(acc[:, c * len(blks) + i, :], parts[i][:, r, (c0 + c) * P : (c0 + c + 1) * P], ident[:])
-                    for c in range(group):
-                        nc.scalar.activation(out=scaled[:, c0 + c, r, :, :], in_=acc[:, c * len(blks) : (c + 1) * len(blks), :], func=COPY, scale=gate_column(r, first_piece + c0 + c))
+            for which, turns in turn_banks:
+                acc = bank(which)
+                for j, (c, r) in enumerate(turns):
+                    for i in range(len(blks)):
+                        nc.tensor.transpose(acc[:, j * len(blks) + i, :], parts[i][:, r, c * P : (c + 1) * P], ident[:])
+                for j, (c, r) in enumerate(turns):
+                    nc.scalar.activation(out=scaled[:, c, r, :, :], in_=acc[:, j * len(blks) : (j + 1) * len(blks), :], func=COPY, scale=gate_column(r, first_piece + c))
             for which, i, c0, run in sum_banks:
                 acc = bank(which)
                 for c in range(run):
@@ -260,35 +264,35 @@ def tile_moe_qkv_kernel(tc, x_words, x_scales, wq_words, wq_scales, wk_words, wk
                 cols = slice(c0 * P, (c0 + run) * P)
                 nc.scalar.copy(out=parts[i][:, 0, cols], in_=acc[:, 0:run, :].rearrange("p c t -> p (c t)"))
                 first = (first_piece + c0) * P
-                nc.sync.dma_start(out=out[blks[i] * P : (blks[i] + 1) * P, first : first + run * P], in_=parts[i][:, 0, cols])
+                queue.dma_start(out=out[blks[i] * P : (blks[i] + 1) * P, first : first + run * P], in_=parts[i][:, 0, cols])
 
         for blk in range(4):
             y[blk] = ring.tile([P, S], F32, name=f"y{blk}", align_bytes=ALIGN)
         spread_gate()
-        for b in range(2):
-            for c in range(CHUNKS):
-                project(chunk(c, b), q_weights, (4 + CHUNKS * b + c) % 8)
+        for h in range(2):
+            for b in range(2):
+                for c in range(2):
+                    project(chunk(2 * h + c, b), q_weights, 4 + 2 * b + c)
         y[4] = ring.tile([P, S], F32, name="y4", tag="raw0", align_bytes=ALIGN)
-        y[5] = ring.tile([P, S], F32, name="y5", tag="raw1", align_bytes=ALIGN)
+        y[5] = ring.tile([P, S], F32, name="y5", tag="qw1", align_bytes=ALIGN)
 
         def prepare_v(e):
-            round_v(e, e == ROUND_ON_SCALAR)
+            round_v(e, False)
             for s in range(PASSES):
                 quantise_rows(e, s, BOTH)
 
         prepare_v(0)
         combine_on_vector(0, 0, T, ("parts0", "total0"))
-        prepare_v(1)
         combine_on_vector(1, 0, T, ("qw0", "total1"))
         for c in range(CHUNKS):
             for b in range(2):
                 project(chunk(c, 2 + b), k_weights, (2 * c + b) % 4)
         for e in range(last):
-            if e == 2:
-                combine_on_scalar((2, 3), 0, PIECES, T, ("kw0", "kw1"), (4, 5, 6), [(7, 0, 0, PIECES), (0, 1, 0, PIECES)])
-            if e >= 2:
+            if e == 1:
+                combine_on_scalar((2, 3), 0, PIECES, T, ("kw0", "kw1"), [(4 + r, [(c, r), (c + 1, r)]) for c in (0, 2) for r in range(TOP)], [(7, 0, 0, PIECES), (0, 1, 0, PIECES)])
+            if e >= 1:
                 prepare_v(e)
-            project([(e, 4), (e, 5)], v_weights, (3, 2)[e] if e < 2 else (2, 1, 3)[e % 3 - 3])
+            project([(e, 4), (e, 5)], v_weights, 3 if e < 2 else (2, 1, 3)[e % 3 - 2])
         ends = ring.tile([P, PASSES, PACK * N], BF16, name="staged", tag="staged", bufs=STAGE_BUFS, align_bytes=ALIGN)
         round_rows(last, 0, BOTH, ends[:, 0, :], True)
         round_rows(last, 1, (1,), ends[:, 1, PACK * P : PACK * N], False)
@@ -298,6 +302,9 @@ def tile_moe_qkv_kernel(tc, x_words, x_scales, wq_words, wq_scales, wk_words, wk
         quantise_rows(last, 1, (0,))
         project([(last, 5)], v_weights, 6, on_vector=True)
         project([(last, 4)], v_weights, 7)
-        combine_on_scalar((4,), 0, PIECES - 1, 2 * P, ("kw2",), (4, 5, 1), [(0, 0, 0, 2), (2, 0, 2, 1)])
-        combine_on_vector(5, 0, T, ("raw4", "kw3"))
-        combine_on_vector(4, T - P, P, ("raw6", "raw5"))
+        combine_on_scalar((4,), 0, PIECES - 1, 2 * P, ("kw2",), [((4, 5, 3)[c], [(c, r) for r in range(TOP)]) for c in range(PIECES - 1)], [(0, 0, 0, 2), (2, 0, 2, 1)], nc.scalar)
+        whole = weigh_on_vector(5, 0, T, "raw4")
+        finish_on_vector(5, 0, whole[:, :, 0 : T - P], "kw3")
+        piece = weigh_on_vector(4, T - P, P, "raw6")
+        finish_on_vector(5, T - P, whole[:, :, T - P : T], "raw7")
+        finish_on_vector(4, T - P, piece, "raw5")

@@ -113,22 +113,19 @@ def tile_moe_qkv_kernel(tc, x_words, x_scales, wq_words, wq_scales, wk_words, wk
         nc.sync.dma_start(out=xw[:, 0 : PASSES * T].rearrange("p (s t) -> p s t", s=PASSES), in_=x_words.rearrange("s p t d -> p s (t d)").bitcast(I32))
         for q in range(P // QUADRANT):
             nc.sync.dma_start(out=xs[q * QUADRANT : q * QUADRANT + PASSES * PACK, 0:T].bitcast(I32), in_=x_rows[q].bitcast(I32))
+        load_q(0)
         for r in range(PACK):
             nc.sync.dma_start(out=ws[r:P:QUADRANT].bitcast(I32), in_=q_rows[r].bitcast(I32))
             if r == 1:
                 nc.sync.dma_start(out=gate_rows[0 : PIECES * PORT : PORT], in_=gate[:, 0, :].rearrange("r (c t) -> c r t", t=P))
             nc.sync.dma_start(out=ws[K_PLANE + r : P : QUADRANT].bitcast(I32), in_=k_rows[r].bitcast(I32))
-        load_q(0)
         nc.sync.dma_start(out=bias_sb[:], in_=bias.rearrange("(b n) e -> n b e", n=P))
         load_q(1)
         nc.vector.tensor_copy(gs[:], xs[:].indirect(offs_sb[:]))
-        early = keep.tile([P, HALF], U32, name="gw_early", align_bytes=ALIGN)
-        below = tok.tile([P, S], U32, name="gw_below", align_bytes=ALIGN, offset=0)
-        above = tok.tile([P, HALF], U32, name="gw_above", align_bytes=ALIGN, offset=2 * HALF_BYTES + BYTE_WINDOW - 2 * ALIGN)
-        gather_words(0, 0, early[:])
-        gather_words(1, 0, below[:, 0:HALF])
-        gather_words(0, 1, above[:])
-        gather_words(1, 1, below[:, HALF:S])
+        words = [tok.tile([P, S], U32, name=f"gw{s}", align_bytes=ALIGN, offset=s * (2 * HALF_BYTES + BYTE_WINDOW - 2 * ALIGN)) for s in range(PASSES)]
+        for h in range(2):
+            for s in range(PASSES):
+                gather_words(s, h, words[s][:, h * HALF : (h + 1) * HALF])
         for r in range(PACK):
             nc.sync.dma_start(out=gs_moved[r:P:QUADRANT].bitcast(I32), in_=gs[PACK + r : P : QUADRANT].bitcast(I32))
         load_v(0)
@@ -286,7 +283,7 @@ def tile_moe_qkv_kernel(tc, x_words, x_scales, wq_words, wq_scales, wk_words, wk
         combine_on_vector(1, 0, T, ("qw0", "total1"))
         for c in range(CHUNKS):
             for b in range(2):
-                project(chunk(c, 2 + b), k_weights, (2 * c + b) % 4)
+                project(chunk(c, 2 + b), k_weights, (6, 0, 6, 2)[c] + b)
         for e in range(last):
             if e == 1:
                 combine_on_scalar((2, 3), 0, PIECES, T, ("kw0", "kw1"), [(4 + r, [(c, r), (c + 1, r)]) for c in (0, 2) for r in range(TOP)], [(7, 0, 0, PIECES), (0, 1, 0, PIECES)])

from contextlib import ExitStack

import concourse.mybir as mybir
from concourse.masks import make_identity

K, T, E, C, N, TOP = 1024, 512, 12, 128, 256, 3
S = E * C
FLOPS = 2 * K * 3 * N * S

F32 = mybir.dt.float32
BF16 = mybir.dt.bfloat16
I32 = mybir.dt.int32
U32 = mybir.dt.uint32
U16 = mybir.dt.uint16
U8 = mybir.dt.uint8
FP8X4 = mybir.dt.float8_e4m3fn_x4
FP4X4 = mybir.dt.float4_e2m1fn_x4
MULT = mybir.AluOpType.mult
ADD = mybir.AluOpType.add
IDENT = mybir.ActivationFunctionType.Identity
COPY = mybir.ActivationFunctionType.Copy

P = 128
PACK = 4
QUADRANT = 32
PASS_ROWS = P * PACK
PASSES = K // PASS_ROWS
BLOCKS = 3 * N // P
PIECES = T // P
OFFSETS_A_COLUMN = 16
ALIGN = 64
K_PLANE = 4
BYTE_WINDOW = 2048
HALF = S // 2
HALF_BYTES = 4 * HALF
CHUNK = 3
CHUNKS = E // CHUNK
Q_LOAD = 6
WALK = 4
BOTH = (0, 1)
STAGE_BUFS = 2
CODE_BUFS = 10
PORT = 4
BANK_BYTES = 2048


def tile_moe_qkv_kernel(tc, x_words, x_scales, wq_words, wq_scales, wk_words, wk_scales, wv, bias, gate, offs, pos1, pos2, pos3, out):
    nc = tc.nc
    with ExitStack() as ctx:
        keep = ctx.enter_context(tc.tile_pool(name="keep", bufs=1))
        ring = ctx.enter_context(tc.tile_pool(name="ring", bufs=1))
        tok = ctx.enter_context(tc.tile_pool(name="tok", bufs=1))
        psum = ctx.enter_context(tc.psum_pool(name="psum", bufs=1))

        offs_sb = keep.tile([P, S // OFFSETS_A_COLUMN], U16, name="offs_sb")
        pos_sb = [keep.tile([P, T // OFFSETS_A_COLUMN], U16, name=f"pos_sb{r}") for r in range(TOP)]
        xw = keep.tile([P, (PASSES + 1) * T], I32, name="xw", align_bytes=ALIGN)
        xs = tok.tile([P, BYTE_WINDOW], U8, name="xs", align_bytes=ALIGN, offset=2 * HALF_BYTES - ALIGN)
        ws = keep.tile([P, E * PASSES, N], U8, name="ws", align_bytes=ALIGN)
        qw = [ring.tile([P, Q_LOAD * PASSES, 2 * N], U8, name=f"qw{i}", align_bytes=ALIGN) for i in range(E // Q_LOAD)]
        kw = [ring.tile([P, CHUNK * PASSES, N], I32, name=f"kw{i}", align_bytes=ALIGN) for i in range(CHUNKS)]
        bias_sb = keep.tile([P, BLOCKS, E], F32, name="bias_sb")
        gate_rows = keep.tile([P, TOP, P], F32, name="gate_rows")
        gate_col = keep.tile([P, TOP * PIECES], F32, name="gate_col")
        gate_sb = [keep.tile([P, T], F32, name=f"gate_sb{r}") for r in range(TOP)]
        ident = keep.tile([P, P], F32, name="ident")
        gs = keep.tile([P, S], U8, name="gs", align_bytes=ALIGN)
        gs_moved = keep.tile([P, S], U8, name="gs_moved", align_bytes=ALIGN)
        gw = {}
        raw, staged, quantised, y = {}, {}, {}, {}
        last = E - 1

        nc.vector.memset(ws[:].rearrange("p s t -> p (s t)").bitcast(I32), 0)
        nc.gpsimd.memset(xs[:].bitcast(I32), 0)
        make_identity(nc, ident[:])
        nc.vector.memset(gate_rows[:].rearrange("c r t -> c (r t)"), 0.0)
        nc.vector.memset(gs_moved[:].bitcast(I32), 0)
        nc.vector.memset(xw[:, PASSES * T :], 0)

        def load_v(e, queue=nc.sync):
            both = ring.tile([P, PASSES, PACK * N], F32, name="raw", tag=f"raw{e}", align_bytes=ALIGN)
            queue.dma_start(out=both[:], in_=wv[e].rearrange("(s p j) n -> p s (j n)", s=PASSES, j=PACK))
            for s in range(PASSES):
                raw[e, s] = both[:, s, :]

        def load_v_pass(e, s):
            one = ring.tile([P, PACK * N], F32, name="rawp", tag=f"raw{e}_{s}", align_bytes=ALIGN)
            rows = wv[e, PASS_ROWS * s : PASS_ROWS * (s + 1), :]
            nc.sync.dma_start(out=one[:], in_=rows.rearrange("(p j) n -> p (j n)", j=PACK))
            raw[e, s] = one[:]

        def load_q(i):
            words = wq_words[Q_LOAD * i : Q_LOAD * (i + 1)].rearrange("e s p w -> p (e s) w")
            nc.sync.dma_start(out=qw[i][:].bitcast(I32), in_=words.bitcast(I32))

        def load_k(i, queue=nc.sync):
            words = wk_words[CHUNK * i : CHUNK * (i + 1)].rearrange("e s p n d -> p (e s) (n d)")
            queue.dma_start(out=kw[i][:], in_=words.bitcast(I32))

        q_rows = wq_scales.rearrange("e s (q r) n -> r q (e s) n", r=PACK)
        k_rows = wk_scales.rearrange("e s (q r) n -> r q (e s) n", r=PACK)
        x_rows = x_scales.rearrange("s (q r) t -> q s r t", r=PACK)

        def columns(first, count):
            return slice(first, first + count), slice(first // OFFSETS_A_COLUMN, (first + count) // OFFSETS_A_COLUMN)

        def gather_words(s, h, dst):
            gw[s, h] = dst
            window = xw[:, s * T : (s + PASSES) * T].bitcast(U32)
            nc.vector.tensor_copy(dst, window.indirect(offs_sb[:, columns(h * HALF, HALF)[1]]))

        nc.sync.dma_start(offs_sb[:], offs)
        nc.sync.dma_start(out=xw[:, 0 : PASSES * T].rearrange("p (s t) -> p s t", s=PASSES), in_=x_words.rearrange("s p t d -> p s (t d)").bitcast(I32))
        for q in range(P // QUADRANT):
            nc.sync.dma_start(out=xs[q * QUADRANT : q * QUADRANT + PASSES * PACK, 0:T].bitcast(I32), in_=x_rows[q].bitcast(I32))
        load_q(0)
        for r in range(PACK):
            nc.sync.dma_start(out=ws[r:P:QUADRANT].bitcast(I32), in_=q_rows[r].bitcast(I32))
            if r == 1:
                nc.sync.dma_start(out=gate_rows[0 : PIECES * PORT : PORT], in_=gate[:, 0, :].rearrange("r (c t) -> c r t", t=P))
            nc.sync.dma_start(out=ws[K_PLANE + r : P : QUADRANT].bitcast(I32), in_=k_rows[r].bitcast(I32))
        nc.sync.dma_start(out=bias_sb[:], in_=bias.rearrange("(b n) e -> n b e", n=P))
        load_q(1)
        nc.vector.tensor_copy(gs[:], xs[:].indirect(offs_sb[:]))
        words = [tok.tile([P, S], U32, name=f"gw{s}", align_bytes=ALIGN, offset=s * (2 * HALF_BYTES + BYTE_WINDOW - 2 * ALIGN)) for s in range(PASSES)]
        for h in range(2):
            for s in range(PASSES):
                gather_words(s, h, words[s][:, h * HALF : (h + 1) * HALF])
        for r in range(PACK):
            nc.sync.dma_start(out=gs_moved[r:P:QUADRANT].bitcast(I32), in_=gs[PACK + r : P : QUADRANT].bitcast(I32))
        load_v(0)
        load_k(0)
        for r, pos in enumerate((pos1, pos2, pos3)):
            nc.sync.dma_start(pos_sb[r][:], pos)
        for i in range(1, CHUNKS):
            load_k(i)
        for e in range(1, last):
            load_v(e)
        for s in range(PASSES):
            load_v_pass(last, s)

        def bank(which):
            return psum.tile([P, PACK, P], F32, name="bank", tag=f"bank{which}", offset=which * BANK_BYTES)

        def gate_column(r, c):
            return gate_col[:, PIECES * r + c : PIECES * r + c + 1]

        def spread_gate():
            acc = bank(0)
            for r in range(TOP):
                nc.tensor.transpose(acc[:, r, :], gate_rows[:, r, :], ident[:])
            nc.scalar.copy(out=gate_col[:].rearrange("p (r c) -> p r c", c=PIECES), in_=acc[:, 0:TOP, 0 : PIECES * PORT : PORT])
            for r in range(TOP):
                acc = bank(1 + r)
                for c in range(PIECES):
                    nc.tensor.transpose(acc[:, c, :], gate_column(r, c).to_broadcast([P, P]), ident[:])
                nc.scalar.copy(out=gate_sb[r][:], in_=acc[:].rearrange("p c t -> p (c t)"))

        def token_scales(blk, s):
            if s == 0:
                return gs[:]
            return gs_moved[:] if blk < 2 else gs[PACK:P]

        def project(sums, weights, which, on_vector=False):
            acc = bank(which)
            for i, (e, blk) in enumerate(sums):
                h, u = divmod(e, E // 2)
                for s in range(PASSES):
                    words, scales = weights(e, s, blk % 2)
                    nc.tensor.matmul_mx(
                        out=acc[:, i, :],
                        lhsT=words,
                        lhsT_scale=scales,
                        rhs=gw[s, h][:, u * C : (u + 1) * C].bitcast(FP8X4),
                        rhs_scale=token_scales(blk, s)[:, e * C : (e + 1) * C],
                        start=(s == 0),
                        stop=(s == PASSES - 1),
                    )
            for i, (e, blk) in enumerate(sums):
                if on_vector:
                    nc.vector.tensor_scalar_add(out=y[blk][:, e * C : (e + 1) * C], in0=acc[:, i, :], scalar1=bias_sb[:, blk, e : e + 1])
                else:
                    nc.scalar.activation(out=y[blk][:, e * C : (e + 1) * C], in_=acc[:, i, :], func=IDENT, bias=bias_sb[:, blk, e : e + 1])

        def q_weights(e, s, b):
            words = qw[e // Q_LOAD][:, (e % Q_LOAD) * PASSES + s, b * 2 * P : (b + 1) * 2 * P]
            return words.bitcast(FP4X4), ws[:, e * PASSES + s, b * P : (b + 1) * P]

        def k_weights(e, s, b):
            words = kw[e // CHUNK][:, (e % CHUNK) * PASSES + s, b * P : (b + 1) * P]
            return words.bitcast(FP8X4), ws[K_PLANE:P, e * PASSES + s, b * P : (b + 1) * P]

        def v_weights(e, s, b):
            return quantised[e, s, b]

        def chunk(c, blk):
            return [(e, blk) for e in range(c * CHUNK, (c + 1) * CHUNK)]

        def round_rows(e, s, halves, dst, on_scalar):
            staged[e, s, halves] = dst
            rows = raw[e, s].rearrange("p (j n) -> p j n", j=PACK)[:, :, halves[0] * P : (halves[-1] + 1) * P]
            dst = dst.rearrange("p (c i j) -> p c j i", i=WALK, j=PACK)
            src = rows.rearrange("p j (c i) -> p c j i", i=WALK)
            if on_scalar:
                nc.scalar.copy(out=dst, in_=src)
            else:
                nc.vector.tensor_copy(out=dst, in_=src)

        def round_v(e, on_scalar):
            both = ring.tile([P, PASSES, PACK * N], BF16, name="staged", tag="staged", bufs=STAGE_BUFS, align_bytes=ALIGN)
            for s in range(PASSES):
                round_rows(e, s, BOTH, both[:, s, :], on_scalar)

        def quantise_rows(e, s, halves):
            width = len(halves) * P
            codes = ring.tile([P, width], U32, name="codes", tag="codes", bufs=CODE_BUFS, align_bytes=ALIGN)
            scales = ring.tile([P, width], U8, name="scales", tag="scales", bufs=CODE_BUFS, align_bytes=ALIGN)
            nc.vector.quantize_mx(out=codes[:].bitcast(FP8X4), scales=scales[:], in_=staged[e, s, halves])
            for i, b in enumerate(halves):
                quantised[e, s, b] = (codes[:, i * P : (i + 1) * P].bitcast(FP8X4), scales[:, i * P : (i + 1) * P])

        def weigh_on_vector(blk, first, count, room):
            cols, entries = columns(first, count)
            parts = ring.tile([P, TOP, count], F32, name="parts", tag=room, align_bytes=ALIGN)
            for r in range(TOP):
                nc.vector.tensor_tensor(parts[:, r, :], y[blk][:].indirect(pos_sb[r][:, entries]), gate_sb[r][:, cols], MULT)
            nc.vector.tensor_tensor(parts[:, 0, :], parts[:, 0, :], parts[:, 1, :], ADD)
            return parts

        def finish_on_vector(blk, first, parts, room):
            count = parts.shape[2]
            total = ring.tile([P, count], F32, name="total", tag=room, align_bytes=ALIGN)
            nc.vector.tensor_tensor(total[:], parts[:, 0, :], parts[:, 2, :], ADD)
            nc.sync.dma_start(out=out[blk * P : (blk + 1) * P, first : first + count], in_=total[:])

        def combine_on_vector(blk, first, count, rooms):
            finish_on_vector(blk, first, weigh_on_vector(blk, first, count, rooms[0]), rooms[1])

        def combine_on_scalar(blks, first_piece, pieces, width, rooms, turn_banks, sum_banks, queue=nc.sync):
            count = pieces * P
            parts = [ring.tile([P, TOP, count], F32, name="parts", tag=room, align_bytes=ALIGN) for room in rooms]
            for first in range(0, count, width):
                run = min(width, count - first)
                entries = columns(first_piece * P + first, run)[1]
                for r in range(TOP):
                    for i, blk in enumerate(blks):
                        nc.scalar.activation(out=parts[i][:, r, first : first + run], in_=y[blk][:].indirect(pos_sb[r][:, entries]), func=COPY)
            scaled = ring.tile([P, pieces, TOP, len(blks), P], F32, name="scaled", tag="scaled")
            for which, turns in turn_banks:
                acc = bank(which)
                for j, (c, r) in enumerate(turns):
                    for i in range(len(blks)):
                        nc.tensor.transpose(acc[:, j * len(blks) + i, :], parts[i][:, r, c * P : (c + 1) * P], ident[:])
                for j, (c, r) in enumerate(turns):
                    nc.scalar.activation(out=scaled[:, c, r, :, :], in_=acc[:, j * len(blks) : (j + 1) * len(blks), :], func=COPY, scale=gate_column(r, first_piece + c))
            for which, i, c0, run in sum_banks:
                acc = bank(which)
                for c in range(run):
                    for r in range(TOP):
                        nc.tensor.matmul(acc[:, c, :], scaled[:, c0 + c, r, i, :], ident[:], start=(r == 0), stop=(r == TOP - 1), is_transpose=True)
                cols = slice(c0 * P, (c0 + run) * P)
                nc.scalar.copy(out=parts[i][:, 0, cols], in_=acc[:, 0:run, :].rearrange("p c t -> p (c t)"))
                first = (first_piece + c0) * P
                queue.dma_start(out=out[blks[i] * P : (blks[i] + 1) * P, first : first + run * P], in_=parts[i][:, 0, cols])

        for blk in range(4):
            y[blk] = ring.tile([P, S], F32, name=f"y{blk}", align_bytes=ALIGN)
        spread_gate()
        for h in range(2):
            for b in range(2):
                for c in range(2):
                    project(chunk(2 * h + c, b), q_weights, 4 + 2 * b + c)
        y[4] = ring.tile([P, S], F32, name="y4", tag="raw0", align_bytes=ALIGN)
        y[5] = ring.tile([P, S], F32, name="y5", tag="qw1", align_bytes=ALIGN)

        def prepare_v(e):
            round_v(e, False)
            for s in range(PASSES):
                quantise_rows(e, s, BOTH)

        prepare_v(0)
        combine_on_vector(0, 0, T, ("parts0", "total0"))
        combine_on_vector(1, 0, T, ("qw0", "total1"))
        for c in range(CHUNKS):
            for b in range(2):
                project(chunk(c, 2 + b), k_weights, (6, 0, 6, 2)[c] + b)
        for e in range(last):
            if e == 1:
                combine_on_scalar((2, 3), 0, PIECES, T, ("kw0", "kw1"), [(4 + r, [(c, r), (c + 1, r)]) for c in (0, 2) for r in range(TOP)], [(7, 0, 0, PIECES), (0, 1, 0, PIECES)])
            if e >= 1:
                prepare_v(e)
            project([(e, 4), (e, 5)], v_weights, 3 if e < 2 else (2, 1, 3)[e % 3 - 2])
        ends = ring.tile([P, PASSES, PACK * N], BF16, name="staged", tag="staged", bufs=STAGE_BUFS, align_bytes=ALIGN)
        round_rows(last, 0, BOTH, ends[:, 0, :], True)
        round_rows(last, 1, (1,), ends[:, 1, PACK * P : PACK * N], False)
        round_rows(last, 1, (0,), ends[:, 1, 0 : PACK * P], True)
        quantise_rows(last, 0, BOTH)
        quantise_rows(last, 1, (1,))
        quantise_rows(last, 1, (0,))
        project([(last, 5)], v_weights, 6, on_vector=True)
        project([(last, 4)], v_weights, 7)
        combine_on_scalar((4,), 0, PIECES - 1, 2 * P, ("kw2",), [((4, 5, 3)[c], [(c, r) for r in range(TOP)]) for c in range(PIECES - 1)], [(0, 0, 0, 2), (2, 0, 2, 1)], nc.scalar)
        whole = weigh_on_vector(5, 0, T, "raw4")
        finish_on_vector(5, 0, whole[:, :, 0 : T - P], "kw3")
        piece = weigh_on_vector(4, T - P, P, "raw6")
        finish_on_vector(5, T - P, whole[:, :, T - P : T], "raw7")
        finish_on_vector(4, T - P, piece, "raw5")
